import numpy as np, ml_dtypes
CORES = [16,17,18,19,32,33,34,35]
N = 8
BF = ml_dtypes.bfloat16
def gentries(a):
    return np.ascontiguousarray(a.reshape(8, 16, -1).transpose(0, 2, 1)).reshape(8, -1)
def gtable(e):
    e = np.asarray(e); return np.ascontiguousarray(e.reshape(8, -1, 16).transpose(0, 2, 1)).reshape(128, -1).astype(np.int32)
W, C, S, L0, K, CAP, RO = 4096, 64, 64, 41, 64, 224, 3
U = C * L0
def orders(rng):
    return np.argsort(rng.random((N, 8, U)), axis=-1)
def aim(z, want):
    s = np.add.reduce(z, axis=2)[:, :, 0::2]
    ends = np.stack([s[..., 0], s[..., L0 - 1]], -1).reshape(N, 8, C)
    return (want - 61 * np.roll(ends, 1, axis=0)[..., None]) & (W - 1)
def pack(z, o, cn):
    a = np.take_along_axis(z.reshape(N, 8, 16, U), np.argsort(o, axis=-1)[:, :, None, :], 3)
    return {"x": a.reshape(N, 128, U).astype(np.float32).astype(BF), "oc": np.stack([gtable(v) for v in o]), "cd": np.stack([gtable(v.reshape(8, C * K)) for v in cn])}
def setup_inputs(rng):
    o = orders(rng); z = rng.integers(0, 16, (N, 8, 16, C, L0))
    share = rng.choice(np.array([0.0, 0.0, 0.25, 0.5]), (N, 8, 1, 1, 1))
    walk = np.clip(z[..., :1] + np.add.accumulate(rng.integers(-1, 2, z.shape), axis=-1), 0, 15)
    z = np.where(rng.random((N, 8, 1, C, 1)) < share, walk, z)
    return pack(z, o, rng.integers(0, W, (N, 8, C, K)))
def setup_inputs_room(rng):
    o = orders(rng); H = C // 2; mx = (L0 + 1) // 2; lo = CAP // H + 1
    z = rng.integers(0, 4, (N, 8, 16, C, L0)) + 12 * rng.integers(0, 2, (N, 8, 16, C, L0))
    z[:, :, :, 0::2] = rng.integers(0, 16, (N, 8, 16, H, L0))
    z[:, :, :, 0::2, 0] = rng.integers(7, 9, (N, 8, 16, H)); z[:, :, :, 0::2, L0 - 1] = rng.integers(7, 9, (N, 8, 16, H))
    want = np.zeros((N, 8, C, K), np.int64); many, huge = [int(v) for v in rng.permutation(8)[:2]]
    for q in range(N):
        for g in range(8):
            oo = o[q, g].reshape(C, L0)
            pool = np.concatenate([oo[0::2].reshape(-1), oo[1::2, 0], oo[1::2, L0 - 1], np.arange(U, W)])
            want[q, g] = rng.choice(pool, (C, K))
            total = CAP + int(rng.integers(-1, 2)); more = int(rng.integers(0, H + 1))
            if q == 0: total = CAP + (0, 1, -1)[g % 3]; more = (0, H)[int(g > 0)]
            sizes = []; rem = total
            while rem > mx:
                s = int(rng.integers(lo, min(mx, rem - 2) + 1)); sizes.append(s); rem -= s
            sizes.append(rem); sizes += [2] * min(more, H - len(sizes))
            if q > 0 and g == many:
                base = CAP // H; sz = base + (np.arange(H) < CAP - base * H).astype(np.int64)
                dd = rng.integers(0, base - 1, H // 2); sz[:H // 2] += dd; sz[H // 2:2 * (H // 2)] -= dd
                sizes = [int(v) for v in rng.permutation(sz)]
            if q > 0 and g == huge:
                sizes = [int(v) for v in rng.integers(mx - 1, mx + 1, H)]
            who = np.sort(rng.permutation(H)[:len(sizes)]); whom = rng.permutation(H)[:len(sizes)]
            for w, v, s in zip(who, whom, sizes):
                c = 2 * int(v) + 1; i = s - 1 if s < mx and rng.random() < 0.5 else L0 - s
                z[q, g, :, c, i] = rng.integers(7, 9, 16)
                spot = rng.random((2, K)) < 0.5; spot[int(rng.integers(0, 2)), int(rng.integers(0, K))] = True
                want[q, g, 2 * w:2 * w + 2][spot] = oo[c, i]
    return pack(z, o, aim(z, want))
def setup_inputs_ties(rng):
    o = orders(rng); pat = rng.integers(0, 16, (4, 16)); w = rng.integers(0, 4, (N, 8, C, L0)); w[:, int(rng.integers(0, 8))] = 0
    cn = rng.integers(0, W, (N, 8, C, K)); cn[:, ::3] = cn[:, ::3, :, :1]
    return pack(np.moveaxis(pat[w], -1, 2), o, cn)
def setup_inputs_edge(rng):
    o = orders(rng); z = rng.integers(0, 16, (N, 8, 16, C, L0)); h = (L0 - 1) // 2
    at = np.where(np.arange(8)[None, :, None, None] % 2 == 0, rng.choice(np.array([0, 1, L0 - 2, L0 - 1]), (N, 8, C, K)), rng.choice(np.array([h - 1, h, h, h + 1]), (N, 8, C, K)))
    ch = 2 * rng.integers(0, C // 2, (N, 8, C, K)) + 1
    want = np.take_along_axis(o, (ch * L0 + at).reshape(N, 8, C * K), 2).reshape(N, 8, C, K)
    want = np.where(rng.random(want.shape) < 0.125, rng.integers(U, W, want.shape), want)
    two = [int(v) for v in rng.permutation(8)[:2]]
    side = (np.arange(L0) + rng.integers(0, 2, (N, 2, C, 1))) % 2
    low = rng.integers(1, 4, (N, 2, 16, C, L0)); low[:, 1] = np.where(rng.random((N, 1, C, L0)) < 0.125, 0, low[:, 1])
    v0 = 2 * rng.integers(0, C // 2, N) + 1
    i0 = 1 + np.argmin(o[:, two[0]].reshape(N, C, L0)[np.arange(N), v0][:, 1:L0 - 1], axis=1)
    side[np.arange(N), 0, v0] = (np.arange(L0) - i0[:, None] + 1) % 2
    for q in range(N): low[q, 0, :, int(v0[q]), int(i0[q]) - 1:int(i0[q]) + 2] = 0
    side[:, 0, C - 2] = (np.arange(L0) + 1) % 2; low[:, 0, :, C - 2, 0] = 0; low[:, 0, :, C - 2, L0 - 1] = 0
    z[:, two] = np.where(side[:, :, None] == 1, 15 - low, low)
    es = np.roll(np.stack([side[:, :, 0::2, 0], side[:, :, 0::2, L0 - 1]], -1).reshape(N, 2, C), 1, axis=0)[..., None]
    vic = 2 * rng.integers(0, C // 2, (N, 2, C, K)) + 1; vic[:, 0] = v0[:, None, None]
    first = np.take_along_axis(side.reshape(N, 2, U), (vic * L0 + 1).reshape(N, 2, C * K), 2).reshape(N, 2, C, K)
    pc = 1 + (first != es).astype(np.int64) + 2 * rng.integers(0, h - 1, (N, 2, C, K))
    b0 = i0[:, None, None]; last = pc[:, 0, C - 2:]
    pc[:, 0, C - 2:] = np.where(last == b0, np.where(b0 + 2 <= L0 - 2, b0 + 2, b0 - 2), last); pc[:, 0, C - 1, K - 1] = i0
    want[:, two] = np.take_along_axis(o[:, two], (vic * L0 + pc).reshape(N, 2, C * K), 2).reshape(N, 2, C, K)
    return pack(z, o, aim(z, want))
def setup_inputs_still(rng):
    o = orders(rng); z = rng.integers(0, 16, (N, 8, 16, C, L0)); s = int(rng.integers(0, N)); g, h = [int(v) for v in rng.permutation(8)[:2]]
    z[s] = z[s][..., :1].copy(); z[:, g] = z[:, g][..., :1].copy(); z[:, h, :, 1::2] = z[:, h, :, 1::2, :1].copy()
    return pack(z, o, rng.integers(0, W, (N, 8, C, K)))
def setup_inputs_spread(rng):
    o = orders(rng); top = rng.integers(1, 17, (N, 8, 1, C, L0)) * (rng.random((N, 8, 1, C, L0)) > 0.0625)
    z = np.minimum((top * rng.random((N, 8, 16, C, L0)) ** rng.choice(np.array([1.0, 2.0, 4.0]), (N, 8, 16, 1, 1))).astype(np.int64), 15)
    near = rng.integers(0, W, (N, 8, 1, 1)) + rng.integers(0, 64, (N, 8, C, K))
    return pack(z, o, np.where(rng.random((N, 8, C, 1)) < 0.5, rng.integers(0, W, (N, 8, C, K)), near) & (W - 1))
def check_inputs(d):
    bad = []; v = np.asarray(d["x"]).astype(np.float32)
    if not np.all((v >= 0) & (v <= 15) & (v == np.floor(v))): bad.append("x: whole numbers from 0 to 15")
    if not all(np.array_equal(np.sort(gentries(a), axis=-1), np.tile(np.arange(U), (8, 1))) for a in d["oc"]): bad.append("oc: every column once")
    if np.min(d["cd"]) < 0 or np.max(d["cd"]) > W - 1: bad.append("range of cd")
    return bad
def reference(x, oc, cd):
    X = np.zeros((N, 8, 16, W), np.int16); X[..., :U] = x.astype(np.float32).reshape(N, 8, 16, U).astype(np.int16)
    O = np.full((N, 8, C, S), -1, np.int64); O[..., :L0] = np.stack([gentries(a) for a in oc]).reshape(N, 8, C, L0)
    ln = np.full((N, 8, C), L0, np.int64); cn = np.stack([gentries(a) for a in cd]).astype(np.int64).reshape(N, 8, C, K)
    j = np.arange(C // 2)
    for t in range(RO):
        att = np.arange(t % 2, C, 2)
        O1, ln1 = O.copy(), ln.copy()
        for p in range(N):
            q = (p + 1 + t % (N - 1)) % N
            for g in range(8):
                o, n, xq = O[q, g], ln[q, g], X[q, g]; a, na = O[p, g][att], ln[p, g][att]
                flat = o.reshape(-1); full = np.flatnonzero(flat >= 0); pl = np.full(W, -1, np.int64); pl[flat[full]] = full
                e = np.stack([a[:, 0], a[j, na - 1]], 1).reshape(-1); xe = X[p, g][:, e]
                m = (cn[q, g] + 61 * np.add.reduce(xe, axis=0, dtype=np.int64)[:, None]) & (W - 1)
                at = pl[m]; v = at // S; i = at % S; L = n[v]
                head = 2 * i + 1 < L; size = np.where(head, i + 1, L - i)
                ok = (at >= 0) & (v % 2 != t % 2) & (i >= 1) & (i <= L - 2) & (np.repeat(na, 2)[:, None] + size <= S)
                other = flat[np.clip(at + np.where(head, 1, -1), 0, C * S - 1)]
                xm = xq[:, m]
                gain = np.add.reduce(np.abs(xm - xq[:, other]), axis=0, dtype=np.int64) - np.add.reduce(np.abs(xe[:, :, None] - xm), axis=0, dtype=np.int64)
                gain = np.where(ok, gain, 0).reshape(C // 2, 2 * K); best = np.argmax(gain, axis=1)
                b = gain[j, best]; vb, ib, hb, sb = [w.reshape(C // 2, 2 * K)[j, best] for w in (v, i, head, size)]
                s = np.lexsort((j, -b)); s = s[b[s] > 0]
                win = np.sort(s[np.unique(vb[s], return_index=True)[1]])
                win = win[np.add.accumulate(sb[win]) <= CAP]
                k = U + CAP * t
                for w in win:
                    c, vc, ic, size_w = att[w], vb[w], ib[w], sb[w]
                    if hb[w]: part, rest = o[vc, ic::-1], o[vc, ic + 1:n[vc]]
                    else: part, rest = o[vc, ic:n[vc]], o[vc, :ic]
                    own = a[w, :na[w]]
                    if best[w] < K: own = own[::-1]
                    new = np.concatenate([own, np.arange(k, k + size_w)]); X[p, g][:, k:k + size_w] = xq[:, part]; k += size_w
                    O1[p, g, c, :len(new)] = new; ln1[p, g, c] = len(new)
                    O1[q, g, vc] = -1; O1[q, g, vc, :len(rest)] = rest; ln1[q, g, vc] = len(rest)
        O, ln = O1, ln1
    ix = O.reshape(N, 8, 1, C * S); y = np.where(ix >= 0, np.take_along_axis(X, np.maximum(ix, 0), 3), 0)
    return {"y": y.reshape(N, 128, C * S).astype(np.float32).astype(BF), "yo": O.reshape(N, 8, C * S).astype(np.float32)}

@@ -1,0 +1,749 @@
+from concourse.mybir import AluOpType, AxisListType, ActivationFunctionType
+
+ALU = AluOpType
+ACT = ActivationFunctionType
+U, CAP, W = 2624, 224, 4096
+PARTS, ZADDR, XSW = 8448, 8768, 8784
+MAGIC = 3221225472.0
+NS = (15, 15, 17)
+NS1 = (12, 11, 11)
+BF, F32, I32, U16 = "bfloat16", "float32", "int32", "uint16"
+
+
+def _sb(n, d):
+    return ("sbuf", [128, n], d)
+
+
+SCRATCH = {
+    "X": _sb(W, BF), "OCI": _sb(164, I32), "CDI": _sb(256, I32), "OCU": _sb(164, U16), "CDF": _sb(256, F32),
+    "XG": _sb(U + 8, BF), "AD": _sb(U + 8, BF), "DS": _sb(U, BF), "SRC": _sb(U, BF), "SC": _sb(U, BF),
+    "STC": _sb(W, F32), "MW": _sb(W, BF), "MG": _sb(W + 144, BF), "FD": _sb(W, BF),
+    "XS": _sb(XSW, BF), "CS": _sb(XSW, F32), "YO": _sb(W, F32), "OCR": _sb(U, F32),
+    "SLU": _sb(164, U16), "VLU": _sb(164, U16), "MI": _sb(256, I32), "MJ": _sb(256, I32), "MU": _sb(256, U16),
+    "IDW": _sb(160, BF), "NEGI": _sb(128, BF), "EIG": _sb(128, BF), "BLK": _sb(128, BF), "WZ": _sb(128, BF),
+    "FS": _sb(144, BF), "FV": _sb(144, BF), "MAS": _sb(144, BF), "MAV": _sb(144, BF), "MB": _sb(144, BF),
+    "MC": _sb(144, BF), "SLT": _sb(144, BF), "VLT": _sb(144, BF), "TGT": _sb(144, BF), "CW": _sb(160, BF),
+    "WDL": _sb(128, BF), "WDR": _sb(128, BF), "WDZ": _sb(128, BF), "TRI": _sb(128, BF), "UOH": _sb(128, BF),
+    "WQ": _sb(128, BF), "WG": _sb(128, BF), "WK": _sb(128, BF), "WR": _sb(256, BF), "WRG": _sb(256, BF),
+    "WC1": _sb(128, BF), "WC2": _sb(128, BF), "WC3": _sb(128, BF),
+    "PI": _sb(4, I32), "COL": _sb(32, F32), "E16": _sb(16, BF), "RW": _sb(48, F32), "IOT": _sb(256, BF),
+    "B82": _sb(256, BF), "NKK": _sb(256, BF), "ONE": _sb(128, BF), "KT": _sb(CAP, BF), "KW": _sb(16, BF),
+    "CWB": _sb(8, BF), "NJ": _sb(64, BF),
+    "AS": _sb(3 * 72, BF), "AL": _sb(3 * 72, BF), "ES": _sb(3 * 32, BF), "EL": _sb(3 * 32, BF),
+    "LS": _sb(3 * 240, BF), "LL": _sb(3 * 240, BF),
+    "XH": _sb(64, BF), "LIM": _sb(4, F32), "RR": _sb(256, F32), "PEN": _sb(256, F32), "T1": _sb(256, F32),
+    "KEY": _sb(256, F32), "SM": _sb(96, F32), "OFF": _sb(4, U16), "MBS": _sb(32, BF), "GD": _sb(64, BF),
+    "TQ": _sb(32, F32), "DF": _sb(64, F32), "WS": _sb(2, BF), "CMP": _sb(2 * CAP, BF), "CU": _sb(16, U16),
+    "CI": _sb(32, I32), "SPT": _sb(64, F32), "SPR": _sb(64, F32), "SPU": _sb(64, U16), "SP": _sb(1024 + CAP, BF),
+    "OH": _sb(256, BF), "DD": _sb(4, BF), "ST": _sb(24, BF), "SMK": _sb(8, BF), "EU": _sb(4, U16), "EW": _sb(4, F32),
+    "OWN": _sb(32, BF), "OWR": _sb(32, BF), "ER": _sb(32, BF), "CT": _sb(144, F32), "OWU": _sb(16, U16),
+    "ND": _sb(CAP, F32), "TG": _sb(CAP, F32), "TGB": _sb(CAP, BF), "TU": _sb(32, U16), "NUM": _sb(CAP, F32),
+    "I3": ("sbuf", [128, 4, 16], F32), "FA": ("sbuf", [128, 4, 32], F32), "FB": ("sbuf", [128, 4, 32], F32),
+    "FC": ("sbuf", [128, 4, 32], F32), "FP": ("sbuf", [128, 4, 32], F32), "FT": _sb(128, F32), "FU": _sb(256, U16),
+    "P0": ("psum", [128, 512], F32), "P1": ("psum", [128, 512], F32), "P2": ("psum", [128, 512], F32),
+    "P3": ("psum", [128, 512], F32), "P4": ("psum", [128, 512], F32), "P5": ("psum", [128, 512], F32),
+    "P6": ("psum", [128, 512], F32), "P7": ("psum", [128, 512], F32),
+}
+SEMAPHORES = ["qv", "qs", "qt", "qg", "ld0", "ld1", "ld2", "ld3", "ld4", "ld5", "ld6", "loc", "loc0", "a0", "a1", "a2",
+              "e0", "e1", "e2", "l0", "l1", "l2", "out0"]
+
+
+def rank_program(g, core, T, topo):
+    rank = T.rank_of(core)
+    if rank is None:
+        return
+    n_ranks = len(T.cores)
+    eng = {"v": g.vector, "s": g.scalar, "t": g.tensor, "g": g, "y": g.sync}
+    cnt = {"v": 0, "s": 0, "t": 0, "g": 0}
+    seen = {k: {} for k in eng}
+    acc = {}
+    sent = [0]
+
+    def A(name, c0=0, c1=None, st=1, p0=0, p1=128):
+        if c1 is None:
+            c1 = SCRATCH[name][1][1]
+        ap = T[name][p0:p1, c0:c1] if st == 1 else T[name][p0:p1, c0:c1:st]
+        return (ap, name, range(c0, c1, st))
+
+    def A3(name, c0, c1):
+        n = SCRATCH[name][1][2]
+        return (T[name][:, :, c0:c1], name, [n * b + c for b in range(4) for c in range(c0, c1)])
+
+    def A3b(name, b):
+        return (T[name][:, b, :], name, range(32 * b, 32 * b + 32))
+
+    def IND(win, off):
+        return (win[0].indirect(off[0]), win[1], win[2], off)
+
+    def wait(q, sem, val):
+        if seen[q].get(sem, 0) < val:
+            eng[q].wait_ge(T.sem[sem], val)
+            seen[q][sem] = val
+
+    def bits(cols, wide):
+        if wide:
+            cols = range(cols[0] // 8 * 8, cols[-1] // 8 * 8 + 8)
+        if isinstance(cols, range) and cols.step == 1:
+            return ((1 << len(cols)) - 1) << cols[0]
+        return sum(1 << c for c in cols)
+
+    def sync(q, reads, writes, sem, val):
+        dma = sem[0] != "q"
+        items = []
+        for lst, w in ((reads, False), (writes, True)):
+            for a in lst:
+                psum = SCRATCH[a[1]][0] == "psum"
+                items.append((a[1], 1 if psum else bits(a[2], dma), w, psum))
+                if len(a) > 3:
+                    items.append((a[3][1], bits(a[3][2], False), False, False))
+        need = {}
+        for name, m, w, psum in items:
+            for e in acc.get(name, []):
+                if e[0] & m and (w or e[1] or (psum and e[4] != q)) and not (q == "t" and e[4] == "t"):
+                    need[e[2]] = max(need.get(e[2], 0), e[3])
+        for s in need:
+            wait(q, s, need[s])
+        for name, m, w, psum in items:
+            lst = acc.setdefault(name, [])
+            lst[:] = [e for e in lst if not ((w or (e[4] == q and not e[1] and not dma)) and e[0] & ~m == 0)]
+            lst.append([m, w, sem, val, q])
+
+    def op(q, fn, reads, writes):
+        cnt[q] += 1
+        sync(q, [a for a in reads if isinstance(a, tuple)], writes, "q" + q, cnt[q])
+        fn().then_inc(T.sem["q" + q], 1)
+
+    def ap(x):
+        return x[0] if isinstance(x, tuple) else x
+
+    def ts(o, i, s1, o0, s2=None, o1=None):
+        if o1 is None:
+            op("v", lambda: g.vector.tensor_scalar(o[0], i[0], ap(s1), None, o0), [i, s1], [o])
+        else:
+            op("v", lambda: g.vector.tensor_scalar(o[0], i[0], ap(s1), ap(s2), o0, o1), [i, s1, s2], [o])
+
+    def tt(o, a, b, o0):
+        op("v", lambda: g.vector.tensor_tensor(o[0], a[0], b[0], o0), [a, b], [o])
+
+    def cp(o, i):
+        op("v", lambda: g.vector.tensor_copy(o[0], i[0]), [i], [o])
+
+    def ms(o, c):
+        op("v", lambda: g.vector.memset(o[0], c), [], [o])
+
+    def red(o, i, o0, ab=False):
+        op("v", lambda: g.vector.tensor_reduce(o[0], i[0], AxisListType.X, o0, apply_absolute_value=ab), [i], [o])
+
+    def tr(o, i):
+        op("v", lambda: g.vector.transpose(o[0], i[0]), [i], [o])
+
+    def act(o, i, f=ACT.Copy, bias=None, scale=1.0):
+        if bias is None:
+            op("s", lambda: g.scalar.activation(o[0], i[0], f, scale=ap(scale)), [i, scale], [o])
+        else:
+            op("s", lambda: g.scalar.activation(o[0], i[0], f, bias=ap(bias), scale=ap(scale)), [i, bias, scale], [o])
+
+    def mm(o, l, r, start, stop):
+        op("t", lambda: g.tensor.matmul(o[0], l[0], r[0], start, stop), [l, r], [o])
+
+    def iota(o, pat, base, cm, small=True):
+        if small:
+            op("g", lambda: g.iota(o[0], pat, base, cm, allow_small_or_imprecise_dtypes=True), [], [o])
+        else:
+            op("g", lambda: g.iota(o[0], pat, base, cm), [], [o])
+
+    def sel(o, i, pat, cmp, fill, base, cm):
+        op("g", lambda: g.affine_select(o[0], i[0], pat, cmp, float(fill), base, cm), [i], [o])
+
+    def ent(name, c0, phi, w):
+        v = A(name, c0, c0 + 113, 16)
+        sel(v, v, [[-16, 8]], ALU.not_equal, w, -phi, 1)
+
+    def ents(name, table):
+        for psi in table:
+            for phi, w in table[psi]:
+                ent(name, psi, phi, w)
+
+    def wrap(pb, n, name, src, width):
+        for r in range(16):
+            mm(A(pb, 0, n), A(name, 16 - r, 144 - r), A(src, r, width, 16), r == 0, r == 15)
+
+    def load(q, o, src, sem):
+        sync(q, [], [o], sem, 16)
+        eng[q].dma_start(o[0], src).then_inc(T.sem[sem], 16)
+
+    def send(src, dst_name, c0, c1, sem, to_rank, loc="loc"):
+        dst = T.cores[to_rank % n_ranks]
+        es = topo.engines(core, dst)[:8]
+        rid, pid, _ = topo.addr(dst)
+        sync("g", [src], [], loc, 10 ** 6)
+        g.remote_dma(T[dst_name][:, c0:c1], src[0], T.sem[sem], T.sem[loc], pid, rid, sum(1 << e for e in es))
+        if loc == "loc":
+            sent[0] += len(es)
+        return len(es)
+
+    def expect(name, c0, c1, sem, from_rank):
+        n = len(topo.engines(T.cores[from_rank % n_ranks], core)[:8])
+        acc.setdefault(name, []).append([bits(range(c0, c1), True), True, sem, n, "r"])
+
+    def col(i):
+        return A("COL", i, i + 1)
+
+    def sm(i):
+        return A("SM", 2 * i, 2 * i + 2)
+
+    def sm1(i, k):
+        return A("SM", 2 * i + k, 2 * i + k + 1)
+
+    def io_(a, b):
+        return A("IOT", a, b)
+
+    ident = A("IDW", 16, 144)
+    g8 = A("BLK", 0, 113, 16)
+    for t in range(3):
+        expect("AL", 72 * t, 72 * t + 72, "a%d" % t, rank - 1 - t)
+        expect("EL", 32 * t, 32 * t + 32, "e%d" % t, rank + 1 + t)
+        expect("LL", 240 * t, 240 * t + 240, "l%d" % t, rank + 1 + t)
+
+    load("y", A("OCI"), T.oc[:, :], "ld0")
+    load("y", A("X", 0, 1312), T.x[:, 0:1312], "ld1")
+    load("s", A("X", 1312, U), T.x[:, 1312:U], "ld2")
+    load("y", A("CDI"), T.cd[:, :], "ld3")
+    load("y", A("X", U, W), T.x[:, 0:W - U], "ld4")
+    iota(A("PI", 0, 1), [[0, 1]], 0, 1, False)
+    iota(A("IOT"), [[1, 256]], 0, 0)
+    iota(A("B82", 0, 82), [[0, 2], [1, 41]], 32, 0)
+    iota(A("B82", 88, 170), [[-1, 2], [0, 41]], 1, 0)
+    ms(A("RW"), 0.0)
+    for a, b, c in ((3, 4, 2.0), (4, 5, -2.0), (5, 6, -1.0), (6, 8, 1.0), (8, 9, 2.0), (9, 11, 256.0), (11, 13, -256.0)):
+        ms(A("RW", a, b), c)
+    ts(A("PI", 1, 2), A("PI", 0, 1), 15, ALU.bitwise_and)
+    ts(A("PI", 2, 3), A("PI", 0, 1), 31, ALU.bitwise_and)
+    cp(A("COL", 0, 2), A("PI", 1, 3))
+    ts(A("E16"), io_(0, 16), col(0), ALU.is_equal)
+    tt(A("RW", 0, 16), A("RW", 0, 16), A("E16"), ALU.mult)
+    ts(col(10), A("E16", 5, 6), 256.0, ALU.mult)
+    for i in range(5):
+        ts(col(5 + i), A("E16", 13, 14), float(1 << i), ALU.mult)
+    red(col(2), A("RW", 0, 16), ALU.add)
+    ts(A("B82", 88, 170), A("B82", 88, 170), col(10), ALU.mult)
+    ts(A("B82", 0, 82), A("B82", 0, 82), col(2), ALU.mult)
+    tt(A("SRC", 0, 82), A("B82", 0, 82), A("B82", 88, 170), ALU.add)
+    for i in range(4):
+        n = 82 << i
+        ts(A("SRC", n, 2 * n), A("SRC", 0, n), col(5 + i), ALU.add)
+    cp(A("OCU"), A("OCI"))
+    load("g", A("STC", U, W), T.x[:, 0:W - U], "ld5")
+    act(A("ONE"), io_(0, 128), ACT.Identity, 1.0, 0.0)
+    for name in ("IDW", "SLT", "MAS", "MB", "WDL", "WDR", "WDZ", "FS", "FV", "WK", "WQ", "WC3"):
+        act(A(name), io_(0, SCRATCH[name][1][1]), ACT.Copy, None, 0.0)
+    act(A("EIG"), io_(0, 128), ACT.Identity, 0.125, 0.0)
+    act(A("XG", U, U + 8), io_(0, 8), ACT.Copy, None, 0.0)
+    act(A("AD", 0, 1), io_(0, 1), ACT.Copy, None, 0.0)
+    act(A("AS"), io_(0, 216), ACT.Copy, None, 0.0)
+    sel(ident, A("ONE"), [[-1, 128]], ALU.is_equal, 0.0, 0, 1)
+    sel(A("BLK"), A("ONE"), [[-16, 8], [0, 16]], ALU.is_ge, 0.0, 0, 1)
+    sel(A("BLK"), A("BLK"), [[16, 8], [0, 16]], ALU.is_ge, 0.0, 15, -1)
+    act(A("SRC", 1312, U), A("SRC", 0, 1312), ACT.Identity, col(9))
+    act(A("NEGI"), ident, ACT.Copy, None, -1.0)
+    for name, cols in (("WDL", (0, 12)), ("WDR", (1, 10)), ("WDZ", (2,))):
+        for c in cols:
+            act(A(name, c, c + 113, 16), g8)
+    act(A("WZ"), A("BLK"), ACT.Copy, None, 61.0)
+    act(A("FS", 16, 129, 16), g8, ACT.Copy, None, -256.0)
+    act(A("FV", 16, 129, 16), g8, ACT.Copy, None, 512.0)
+    ents("SLT", {16: ((13, 82), (5, -41 / 256), (7, -41 / 256), (6, 1))})
+    ents("MAS", {16: ((1, 256), (9, 256), (10, -256), (3, -2 ** 17), (5, -2 ** 18), (6, -2 ** 18))})
+    sel(A("MAV"), A("MAS"), [[0, 144]], ALU.is_ge, 0.0, 0, 0)
+    ent("MAV", 16, 2, -256)
+    ents("MB", {16: ((0, 256), (11, 256), (12, -256), (1, -256), (9, -256), (10, 256), (3, 2 ** 17), (4, -2 ** 17))})
+    iota(A("NKK", 0, 256, 1, 0, 1), [[0, 2], [-1, 128]], 0, 0)
+
+    cp(IND(A("SC"), A("OCU", 0, 82)), A("SRC", 0, 1312))
+    cp(IND(A("SC"), A("OCU", 82, 164)), A("SRC", 1312, U))
+    cp(A("CDF"), A("CDI"))
+    for a, b, c in ((19, 20, -103.5), (20, 21, 103.5), (21, 22, 33.0), (22, 23, -71.0), (23, 24, -32.0),
+                    (24, 25, -104.0), (25, 29, -1e5), (30, 31, 32.0)):
+        ms(A("RW", a, b), c)
+    tt(A("RW", 16, 32), A("RW", 16, 32), A("E16"), ALU.mult)
+    red(col(3), A("RW", 16, 32), ALU.add)
+
+    def first_ends():
+        act(A("AS", 0, 32), A("XG", 0, U - 81, 82))
+        act(A("AS", 32, 64), A("XG", 40, U - 41, 82))
+        n0 = send(A("AS", 0, 72), "AL", 0, 72, "a0", rank + 1, "loc0")
+        g.sync.wait_ge(T.sem.loc0, n0)
+        fills = [("XS", c, min(U, XSW - c)) for c in range(0, XSW, U)] + [("MG", W, 144), ("SP", 1024, CAP)]
+        for name, c, n in fills:
+            sync("y", [], [A(name, c, c + n)], "ld6", 16 * len(fills))
+            g.sync.dma_start(T[name][:, c:c + n], T.x[:, 0:n]).then_inc(T.sem.ld6, 16)
+
+    def dist_a(src, c0, n, pb, d0):
+        mm(A(pb, 0, n), ident, A(src, c0, c0 + n), True, False)
+        mm(A(pb, 0, n), A("NEGI"), A(src, c0 + 1, c0 + n + 1), False, True)
+        act(A("AD", d0, d0 + n), A(pb, 0, n), ACT.Abs)
+
+    def dist_b(src, c0, n, pb, d0, last):
+        mm(A(pb, 0, n), A("WDL"), A("AD", d0, d0 + n), True, False)
+        mm(A(pb, 0, n), A("WDR"), A("AD", d0 + 1, d0 + n + 1), False, False)
+        mm(A(pb, 0, n), A("WDZ"), A(src, c0, c0 + n), False, last)
+
+    def lists(t):
+        b = 72 * t
+        for bit in range(2):
+            for qq in range(4):
+                mm(A("P4", 4 * bit + qq, 256, 8), A("WZ"), A("AL", b + 32 * bit, b + 32 * bit + 32), True, True)
+        for lo, hi in ((0, 128), (128, 256)):
+            tt(A("MI", lo, hi), A("CDF", lo, hi), A("P4", lo, hi), ALU.add)
+            ts(A("MJ", lo, hi), A("MI", lo, hi), 4095, ALU.bitwise_and)
+            cp(A("MU", lo, hi), A("MJ", lo, hi))
+        ts(A("XH"), A("AL", b, b + 64), 0.5, ALU.mult)
+
+    def setup():
+        chunks = [(c, min(512, U - c)) for c in range(0, U, 512)]
+        for i in range(len(chunks) + 1):
+            if i < 3:
+                lo, hi = (0, 66, 130)[i], (66, 130, 164)[i]
+                act(A("XG", 16 * lo, 16 * hi), IND(A("X", 0, U), A("OCU", lo, hi)))
+            if i == 2:
+                first_ends()
+            if i < len(chunks):
+                c, n = chunks[i]
+                dist_a("XG", c, n, "P%d" % (i % 2), c + 1)
+            if i > 0:
+                c, n = chunks[i - 1]
+                dist_b("XG", c, n, "P%d" % (2 + i % 2), c, True)
+                (act if i < 4 else cp)(A("DS", c, c + n), A("P%d" % (2 + i % 2), 0, n))
+            if i == 3:
+                for name in ("CW", "VLT", "WG", "WC1", "WC2", "MC", "TGT"):
+                    ms(A(name), 0.0)
+                for name, psi, phi, w in (
+                        ("WQ", 0, 3, 1), ("WQ", 3, 7, 1), ("WQ", 4, 15, 1), ("WQ", 7, 13, 16384), ("WQ", 8, 13, 1),
+                        ("WC1", 10, 9, -256), ("WC1", 12, 8, 256), ("WC1", 15, 3, 1), ("WC2", 9, 10, -131072),
+                        ("WC2", 10, 10, -131072), ("WC2", 12, 4, 256), ("WC2", 13, 11, 1), ("WC2", 15, 3, 2)):
+                    ts(A(name, psi, psi + 113, 16), A("IDW", 16 + phi, 129 + phi, 16), float(w), ALU.mult)
+            if i == 4:
+                wrap("P6", 164, "SLT", "SC", U)
+                ts(A("SLU"), A("P6", 0, 164), 9.0, ALU.add)
+            if i == 5:
+                lists(0)
+
+    def later_weights():
+        iota(A("NJ", 0, 64, 1, 0, 1), [[0, 2], [-1, 32]], 0, 0)
+        for gm in range(2):
+            sel(A("WR", 128 * gm, 128 * gm + 128), A("WC3"), [[-32, 4], [0, 32]], ALU.not_equal, 16384.0, -(16 * gm + 13), 1)
+            v = A("WRG", 128 * gm, 128 * gm + 128)
+            sel(v, A("EIG"), [[-32, 4], [0, 32]], ALU.is_ge, 0.0, -16 * gm, 1)
+            sel(v, v, [[32, 4], [0, 32]], ALU.is_ge, 0.0, 16 * gm + 15, -1)
+        ents("WQ", {1: ((7, 1), (8, -1)), 2: ((13, 256), (14, 1), (7, 1)), 5: ((1, 1), (9, 1), (10, -1)),
+                    6: ((0, 1), (11, 1), (12, -1), (1, -1), (9, -1), (10, 1))})
+        sel(A("TRI"), A("ONE"), [[1, 128]], ALU.is_ge, 0.0, 0, -1)
+        sel(A("TRI"), A("TRI"), [[-32, 4], [0, 32]], ALU.is_ge, 0.0, 0, 1)
+        v = A("CW", 32, 129, 32)
+        sel(v, A("ONE", 0, 4), [[-32, 4]], ALU.is_ge, 0.0, 0, 1)
+        sel(v, v, [[32, 4]], ALU.is_ge, 0.0, 31, -1)
+        ents("VLT", {16: ((13, 1), (5, -0.125), (7, -0.125))})
+        ents("WC1", {3: ((8, -1), (9, -1), (0, -1), (1, 2), (10, 0.5), (3, -1)), 5: ((8, 1), (10, 1), (3, -1), (12, -1)),
+                     6: ((9, -1), (10, 1), (2, -1), (3, 1)), 7: ((8, -1), (1, 1)), 8: ((8, -1), (9, -1), (0, -1), (1, 2)),
+                     9: ((5, 1), (9, -256)), 11: ((5, 1), (8, 256))})
+        ents("WC2", {3: ((9, 1), (8, -1), (0, -1), (10, 2.5), (4, -2)), 6: ((10, 2), (0, -1), (4, -1)),
+                     7: ((9, 1), (8, -1), (10, 1), (4, -1)), 8: ((9, 1), (8, -1), (0, -1), (10, 2), (4, -2)),
+                     11: ((5, 1), (4, 256)), 14: ((8, 1), (6, 1))})
+
+    def last_weights():
+        ents("MC", {16: ((7, 1), (8, -1))})
+        ents("WC3", {6: ((9, 1), (8, -1), (10, -255), (4, -1), (3, 256)), 13: ((11, 2), (10, 1), (12, -1 / 256))})
+        ents("TGT", {16: ((13, 128), (14, 1), (7, 1), (6, -2))})
+        iota(A3("I3", 0, 16), [[16, 4], [1, 16]], 0, 0)
+        iota(A("YO", 0, U), [[1, U]], 0, 0)
+
+    def feat(t, j, last=False):
+        for bit in range(2):
+            e = 2 * j + bit
+            o, i = A("FD", 64 * e, 64 * e + 64), IND(A("X"), A("MU", 4 * e, 4 * e + 4))
+            xe = A("AL", 72 * t + 32 * bit + j, 72 * t + 32 * bit + j + 1)
+            if j < NS[t]:
+                act(o, i, ACT.Abs, xe, -1.0)
+            else:
+                ts(o, i, xe, ALU.min, A("XH", 32 * bit + j, 32 * bit + j + 1), ALU.subtract)
+        r, h = j % 16, j // 16
+        mm(A("P0", 128 * h, 128 * h + 128), A("FS" if j < NS[t] else "FV", 16 - r, 144 - r),
+           A("FD", 128 * j, 128 * j + 128), False, last)
+
+    def meta(t, j0, j1):
+        o = A("MG", 128 * j0, 128 * j1)
+        if t == 0:
+            act(o, IND(A("STC"), A("MU", 8 * j0, 8 * j1)), ACT.Relu, col(3))
+        else:
+            act(o, IND(A("MW"), A("MU", 8 * j0, 8 * j1)), ACT.Relu)
+
+    def meta_mm(t, j0, j1):
+        for j in range(j0, j1):
+            r, h = j % 16, j // 16
+            rhs = A("MG", 128 * j, 128 * j + 128)
+            mm(A("P0", 128 * h, 128 * h + 128), A("MAS" if j < NS[t] else "MAV", 16 - r, 144 - r), rhs, False, False)
+            mm(A("P1", 128 * h, 128 * h + 128), A("MB", 16 - r, 144 - r), rhs, r == 0, r == 15)
+            if t > 0:
+                mm(A("P2", 128 * h, 128 * h + 128), A("MC", 16 - r, 144 - r), rhs, r == 0, r == 15)
+
+    def scalar_feats(t, extra):
+        mm(A("P0", 0, 256), A("ONE", 0, 128, 1, 0, 1), A("NKK", 0, 256, 1, 0, 1), True, False)
+        for j in range(NS1[t]):
+            feat(t, j)
+            if j in extra:
+                extra[j]()
+
+    def gathers(t, extra):
+        rest = list(range(NS[t], 32))
+        cuts = (0, 4, 8, 12, 16, 20, 24, 28, 30, 31, 32)
+        nv = 7 if t else 6
+        per = [len(rest) * (c + 1) // nv - len(rest) * c // nv for c in range(nv)] + [0] * (10 - nv)
+        for c in range(10):
+            meta(t, cuts[c], cuts[c + 1])
+            mine, rest = rest[:per[c]], rest[per[c]:]
+            for j in mine:
+                feat(t, j)
+            meta_mm(t, cuts[c], cuts[c + 1])
+        extra()
+        for j in range(NS1[t], NS[t]):
+            feat(t, j, j == NS[t] - 1)
+        ts(A("RR"), A("P1", 0, 256), 0.0, ALU.max)
+        if t > 0:
+            for h in range(2):
+                ts(A("PEN", 128 * h, 128 * h + 128), A("P2", 128 * h, 128 * h + 128), A("LIM", 2 + h, 3 + h), ALU.is_gt,
+                   -262144.0, ALU.mult)
+            tt(A("T1"), A("RR"), A("PEN"), ALU.add)
+
+    def q(i):
+        return A("TQ", i, i + 17, 16)
+
+    def q1(i, gm):
+        return A("TQ", i + 16 * gm, i + 16 * gm + 1)
+
+    def state(par, gen):
+        return 8 * gen + 4 * par
+
+    def choose(t, s_old, s_new, s_idle):
+        par = 1 - t % 2
+        tt(A("KEY"), A("P0", 0, 256), A("T1" if t else "RR"), ALU.add)
+        for h in range(2):
+            red(sm1(0, h), A("KEY", 128 * h, 128 * h + 128), ALU.max)
+        ts(sm(1), sm(0), MAGIC, ALU.add, MAGIC, ALU.subtract)
+        for h in range(2):
+            ts(A("OFF", h, h + 1), sm1(1, h), sm1(0, h), ALU.subtract, col(11 + h), ALU.add)
+        cp(A("MBS"), IND(A("MG"), A("OFF", 0, 2)))
+        tt(sm(2), sm(1), sm(0), ALU.subtract)
+        for h in range(2):
+            act(A("GD", 16 * h, 16 * h + 16), A("E16"), ACT.Relu, None, sm1(1, h))
+        for h in range(2):
+            ts(A("GD", 32 + 16 * h, 48 + 16 * h), A("E16"), sm1(2, h), ALU.mult)
+        mm(A("P3", 0, 32), A("WQ"), A("MBS"), True, False)
+        mm(A("P3", 0, 32), A("WG"), A("GD", 0, 32), False, False)
+        mm(A("P3", 0, 32), A("WK"), A("GD", 32, 64), False, True)
+        mm(A("P5", 0, 64), A("ONE", 0, 128, 1, 0, 1), A("NJ", 0, 64, 1, 0, 1), True, False)
+        for gm in range(2):
+            mm(A("P5", 32 * gm, 32 * gm + 32), A("WR", 128 * gm, 128 * gm + 128), A("MBS"), False, False)
+            mm(A("P5", 32 * gm, 32 * gm + 32), A("WRG", 128 * gm, 128 * gm + 128), A("GD", 0, 32), False, gm == 1)
+        tr(A("TQ"), A("P3", 0, 32))
+        ts(sm(3), q(0), 0.0, ALU.is_gt)
+        if t == 0:
+            ts(sm(4), sm(3), 2.0, ALU.mult, -1.0, ALU.add)
+            ts(sm(5), q(2), 128.0 * par, ALU.add)
+        else:
+            ts(sm(6), q(4), 2.0, ALU.is_ge, -2.0, ALU.mult)
+            ts(sm(7), sm(3), 2.0, ALU.mult, -1.0, ALU.add)
+            tt(sm(8), sm(6), q(3), ALU.mult)
+            ts(sm(9), sm(6), 1.0, ALU.add)
+            tt(sm(10), sm(8), q(2), ALU.add)
+            tt(sm(4), sm(7), sm(9), ALU.mult)
+            ts(sm(5), sm(10), 128.0 * par, ALU.add)
+        for gm in range(2):
+            ts(A("DF", 32 * gm, 32 * gm + 32), A("P5", 32 * gm, 32 * gm + 32), q1(7, gm), ALU.subtract, col(13), ALU.add)
+        for b in range(2):
+            for gm in range(2):
+                c = 32 * b + 16 * gm
+                act(A("SPT", c, c + 16), io_(16 * b, 16 * b + 16), ACT.Identity, sm1(5, gm), sm1(4, gm))
+        for gm in range(2):
+            red(sm1(11, gm), A("DF", 32 * gm, 32 * gm + 32), ALU.min, True)
+        tr(A("SPR"), A("SPT"))
+        ts(sm(12), q(1), 1.0, ALU.add, 0.0, ALU.max)
+        for b in range(2):
+            ts(A("SPU", b, 64, 2), A("SPR", 32 * b, 32 * b + 32), float(XSW - 1), ALU.min)
+        act(A("SP", 0, 1024), IND(A("XS"), A("SPU")))
+        tt(sm(13), sm(12), q(9), ALU.min)
+        for gm in range(2):
+            ts(A("WS", gm, gm + 1), sm1(11, gm), 4096.0, ALU.is_ge, sm1(13, gm), ALU.mult)
+        mm(A("P3", 0, 2), A("TRI"), A("WS"), True, True)
+        ts(sm(14), A("WS"), -1.0, ALU.mult, 32.0, ALU.add)
+        cp(sm(15), A("P3", 0, 2))
+        for gm in range(2):
+            ts(A("CMP", CAP * gm, CAP * gm + CAP), io_(0, CAP), sm1(15, gm), ALU.is_ge, sm1(14, gm), ALU.mult)
+        mm(A("P6", 0, 14), ident, A("KW", 0, 14), True, False)
+        for gm in range(2):
+            for r in range(16):
+                o = 32 - 16 * gm - r
+                mm(A("P6", 0, 14), A("CW", o, o + 128), A("CMP", CAP * gm + r, CAP * gm + CAP, 16), False,
+                   gm == 1 and r == 15)
+        eb = 32 * t
+
+        def ev(i):
+            return A("ES", eb + i, eb + i + 17, 16)
+
+        ts(sm(16), sm(15), float(CAP), ALU.is_le)
+        ts(sm(17), q(10), 64.0, ALU.is_lt)
+        tt(sm(18), sm(15), A("WS"), ALU.subtract)
+        tt(ev(0), sm(16), A("WS"), ALU.mult)
+        if t < 2:
+            tt(sm(19), sm(3), q(6), ALU.mult)
+        ts(ev(4), sm(18), 255.0, ALU.min)
+        tt(ev(1), ev(0), sm(17), ALU.mult)
+        ts(ev(2), ev(0), 0.0, ALU.is_gt)
+        if t < 2:
+            tt(ev(5), sm(19), q(5), ALU.add)
+        ts(ev(3), ev(1), 0.0, ALU.is_gt)
+        send(A("ES", eb, eb + 32), "EL", eb, eb + 32, "e%d" % t, rank - 1 - t)
+        tt(sm(20), sm(4), ev(0), ALU.mult)
+        if t > 0:
+            tt(sm(21), q(4), sm(6), ALU.add)
+            tt(sm(22), sm(3), sm(21), ALU.not_equal)
+        bit = sm(22) if t > 0 else sm(3)
+        for gm in range(2):
+            ts(A("OH", 128 * gm, 128 * gm + 128), A("UOH"), q1(8, gm), ALU.is_equal, -1.0, ALU.mult)
+        tt(A("DD", 1, 4, 2), sm(20), bit, ALU.mult)
+        cp(A("CU", 0, 14), A("P6", 0, 14))
+        tt(A("DD", 0, 3, 2), sm(20), A("DD", 1, 4, 2), ALU.subtract)
+        mm(A("P5", 0, 4), ident, A("ST", s_old, s_old + 4), True, False)
+        for gm in range(2):
+            mm(A("P5", 2 * gm, 2 * gm + 2), A("OH", 128 * gm, 128 * gm + 128), A("DD", 2 * gm, 2 * gm + 2), False, gm == 1)
+        lb = 240 * t
+        cp(A("LS", lb, lb + CAP), IND(A("SP"), A("CU", 0, 14)))
+        if t < 2:
+            cp(A("CI", 0, 14), A("P6", 0, 14))
+            for h in range(2):
+                act(A("SMK", 4 * h, 4 * h + 4), A("P5", 0, 4), ACT.Copy, None, col(14 + h))
+            ts(A("CI", 16, 30), A("CI", 0, 14), 5, ALU.arith_shift_right)
+            mm(A("P3", 0, 4), ident, A("CWB", 4 * par, 4 * par + 4), True, False)
+            for gm in range(2):
+                for h in range(2):
+                    o = 16 - 16 * gm + 16 * h
+                    mm(A("P3", h, 4, 2), A("IDW", o, o + 128), A("SMK", 4 * h + 2 * gm, 4 * h + 2 * gm + 2), False,
+                       gm == 1 and h == 1)
+            ab = 72 * (t + 1)
+            cp(A("EU"), A("P3", 0, 4))
+            cp(A("EW"), A("P3", 0, 4))
+            act(A("AS", ab, ab + 64), IND(A("XS"), A("EU")))
+            tt(A("AS", ab + 64, ab + 66), A("EW", 2, 4), A("EW", 0, 2), ALU.subtract)
+            cp(A("LS", lb + CAP, lb + CAP + 14), A("CI", 16, 30))
+            send(A("AS", ab, ab + 72), "AL", ab, ab + 72, "a%d" % (t + 1), rank + 2 + t)
+        send(A("LS", lb, lb + 240), "LL", lb, lb + 240, "l%d" % t, rank - 1 - t)
+        act(A("ST", s_new, s_new + 4), A("P5", 0, 4))
+        s_idle()
+
+    def own_vars(s, par):
+        cp(A("OWN", 8, 25, 16), A("ST", s, s + 3, 2))
+        cp(A("OWN", 9, 26, 16), A("ST", s + 1, s + 4, 2))
+        ms(A("OWN", 12, 29, 16), 256.0 * (1 - par))
+        tr(A("OWR"), A("OWN"))
+        tt(sm(24), A("ST", s + 1, s + 4, 2), A("ST", s, s + 3, 2), ALU.subtract)
+        ts(A("CT", 32 - 32 * par, 64 - 32 * par), io_(0, 32), 0.0, ALU.mult, col(4), ALU.add)
+
+    def arrive(t, s_old, s_new, more):
+        par = t % 2
+        eb, lb, c0 = 32 * t, 240 * t, U + CAP * t
+
+        def ev(i):
+            return A("EL", eb + i, eb + i + 17, 16)
+
+        tt(ev(6), ev(3), sm(24), ALU.mult)
+        tr(A("ER"), A("EL", eb, eb + 32))
+        mm(A("P7", 0, 32), A("WC1"), A("OWR"), True, False)
+        mm(A("P7", 0, 32), A("WC1"), A("ER"), False, True)
+        cp(A("CT", 32 * par, 32 * par + 32), A("P7", 0, 32))
+        tt(A("MW", 0, 640), IND(A("CT", 0, 64), A("VLU", 0, 40)), A("STC", 0, 640), ALU.add)
+        lists(t + 1)
+        act(A("X", c0, c0 + CAP), A("LL", lb, lb + CAP))
+        dist_a("X", c0 - 1, CAP + 1, "P6", 0)
+        dist_b("X", c0, CAP, "P3", 0, False)
+        mm(A("P3", 0, CAP), ident, A("KT"), False, True)
+
+        def nd():
+            act(A("ND"), A("P3", 0, CAP))
+            for k, name in ((1, "WC2"), (2, "WC3")):
+                mm(A("P7", 32 * k, 32 * k + 32), A(name), A("OWR"), True, False)
+                mm(A("P7", 32 * k, 32 * k + 32), A(name), A("ER"), False, True)
+            act(A("CT", 64, 96), A("P7", 32, 64))
+            act(A("CT", 104, 136), A("P7", 64, 96))
+
+        scalar_feats(t + 1, {1: nd})
+        tt(A("MW", 640, U), IND(A("CT", 0, 64), A("VLU", 40, 164)), A("STC", 640, U), ALU.add)
+        cp(A("OWU", 0, 14), A("LL", lb + CAP, lb + CAP + 14))
+        tt(A("MW", c0, c0 + CAP), IND(A("CT", 64, 104), A("OWU", 0, 14)), A("ND"), ALU.add)
+        tt(A("TG"), IND(A("CT", 104, 144), A("OWU", 0, 14)), A("ND"), ALU.add)
+        act(A("TGB"), A("TG"), ACT.Relu)
+        wrap("P6", 14, "TGT", "TGB", CAP)
+        ab = 72 * (t + 1)
+
+        def after():
+            cp(A("TU", 16 * t, 16 * t + 14), A("P6", 0, 14))
+            ts(sm(25), ev(1), -2.0, ALU.mult)
+            tt(A("ST", s_new, s_new + 3, 2), A("ST", s_old, s_old + 3, 2), ev(6), ALU.add)
+            tt(sm(26), ev(0), ev(6), ALU.subtract)
+            ts(sm(28), A("AL", ab + 64, ab + 66), -1.0, ALU.mult)
+            tt(sm(27), sm(25), sm(26), ALU.add)
+            tt(A("LIM", 0, 2), sm(28), A("AL", ab + 64, ab + 66), ALU.max)
+            cp(IND(A("XS"), A("TU", 16 * t, 16 * t + 14)), A("LL", lb, lb + CAP))
+            tt(A("ST", s_new + 1, s_new + 4, 2), A("ST", s_old + 1, s_old + 4, 2), sm(27), ALU.add)
+            ts(A("LIM", 2, 4), A("LIM", 0, 2), -1.0, ALU.mult, 62.0, ALU.add)
+            more()
+
+        gathers(t + 1, after)
+
+    def numbers(t):
+        ts(A("NUM"), io_(0, CAP), float(U + CAP * t), ALU.add)
+        cp(IND(A("CS"), A("TU", 16 * t, 16 * t + 14)), A("NUM"))
+
+    def final_lists(par):
+        for b in range(4):
+            tr(A("FT", 32 * b, 32 * b + 32), A3b("FA", b))
+        for b in range(4):
+            cp(A("FU", 4 * par + b, 256, 8), A("FT", 32 * b, 32 * b + 32))
+
+    def consts():
+        ts(col(11), col(0), 128.0, ALU.mult)
+        ts(col(12), col(0), 128.0, ALU.mult, 2048.0, ALU.add)
+        ts(col(13), col(1), -4096.0, ALU.add)
+        ts(col(14), col(1), 16.0, ALU.is_lt)
+        ts(col(15), col(1), 16.0, ALU.is_ge)
+        cp(col(20), A("PI", 0, 1))
+        ms(A("ES"), 0.0)
+        for t in range(3):
+            ms(A("LS", 240 * t + CAP, 240 * t + 240), 0.0)
+        tt(col(16), col(20), col(1), ALU.subtract)
+        ts(A("KW"), io_(0, 16), 16.0, ALU.mult, col(0), ALU.add)
+        ms(A("ST", 0, 8, 2), 32.0)
+        ms(A("ST", 1, 8, 2), 72.0)
+        ts(A("UOH"), io_(0, 128), col(16), ALU.subtract)
+        ts(A("WG", 5, 118, 16), g8, -1 / 256, ALU.mult)
+        ts(A("WG", 7, 120, 16), g8, 0.125, ALU.mult)
+        cp(A("WG", 9, 122, 16), g8)
+        cp(A("WK", 10, 123, 16), g8)
+        for par in range(2):
+            for h in range(2):
+                ts(A("CWB", 4 * par + h, 4 * par + 4, 2), A("ONE", 0, 2), col(11 + h), ALU.mult)
+        ts(A("CWB", 0, 4), A("CWB", 0, 4), 2.0, ALU.mult)
+        ts(A("CWB", 4, 8), A("CWB", 4, 8), 2.0, ALU.mult, 128.0, ALU.add)
+
+    def spread():
+        ms(A("XS", ZADDR, XSW), 0.0)
+        for i in range(41):
+            cp(A("XS", 32 + i, 8192, 128), A("XG", i, U, 41))
+
+    def idle0():
+        last_weights()
+        act(A("WC1", 4, 117, 16), A("WC1", 3, 116, 16), ACT.Copy, None, -1.0)
+        act(A("WC1", 14, 127, 16), A("WC1", 7, 120, 16), ACT.Copy, None, -1.0)
+        act(A("WC2", 4, 117, 16), A("WC2", 3, 116, 16), ACT.Copy, None, -1.0)
+        act(A("WC3", 7, 120, 16), A("WC2", 7, 120, 16))
+        act(A("WC3", 14, 127, 16), A("WC2", 14, 127, 16))
+        ms(A("RW", 37, 38), 600.0)
+        ms(A("RW", 41, 43), -1e5)
+        ms(A("OWN"), 0.0)
+        ts(A("VLU"), A("P4", 0, 164), 32.0, ALU.add)
+        tt(A("RW", 32, 48), A("RW", 32, 48), A("E16"), ALU.mult)
+        ms(A("OWN", 10, 27, 16), 1.0)
+        ts(A("OWN", 11, 28, 16), A("ONE", 0, 2), col(1), ALU.mult)
+        red(col(4), A("RW", 32, 48), ALU.add)
+        ts(col(21), A("E16", 13, 14), 64.0, ALU.mult)
+        ts(col(22), A("E16", 6, 7), -1000.0, ALU.mult)
+        ts(A("KT"), io_(0, CAP), col(2), ALU.mult)
+        tt(col(17), col(21), col(22), ALU.add)
+        own_vars(state(0, 0), 0)
+        ts(A("CT", 96, 104), io_(0, 8), 0.0, ALU.mult, col(4), ALU.add)
+        ts(A("CT", 136, 144), io_(0, 8), 0.0, ALU.mult, col(17), ALU.add)
+        act(A("MW", U + CAP, W), A("X", U + CAP, W), ACT.Identity, col(4))
+
+    def idle1():
+        own_vars(state(1, 1), 1)
+        ts(A("MW", U, U + CAP), A("X", W - CAP, W), col(4), ALU.add)
+        ms(A("CS", ZADDR, XSW), -1.0)
+        ts(A("CS", PARTS, PARTS + CAP), io_(0, CAP), float(U + 2 * CAP), ALU.add)
+        numbers(0)
+        act(A("OCR", 0, 2048), IND(A("YO", 0, U), A("OCU", 0, 128)))
+        cp(A("OCR", 2048, U), IND(A("YO", 0, U), A("OCU", 128, 164)))
+        for i in range(41):
+            sel(A("CS", 32 + i, 8192, 128), A("OCR", i, U, 41), [[0, 64]], ALU.is_ge, 0.0, 0, 0)
+
+    def shape(s, k, par):
+        tt(sm(k), A("ST", s + 1, s + 4, 2), A("ST", s, s + 3, 2), ALU.subtract)
+        ts(sm(k + 5), A("ST", s, s + 3, 2), col(18 + par), ALU.add)
+        ts(sm(k + 1), sm(k), 0.0, ALU.is_gt, 2.0, ALU.mult)
+        ts(sm(k + 2), sm(k + 1), -1.0, ALU.add)
+        tt(sm(k + 3), sm(k), sm(k + 2), ALU.mult)
+        ts(sm(k + 4), sm(k + 3), 1.0, ALU.add)
+
+    def even_own():
+        ts(col(18), col(1), 256.0, ALU.mult)
+        ts(col(19), col(1), 256.0, ALU.mult, 128.0, ALU.add)
+        shape(state(0, 2), 36, 0)
+        for gm in range(2):
+            ts(A3("FP", 16 * gm, 16 * gm + 16), A3("I3", 0, 16), sm1(40, gm), ALU.is_lt, -16384.0, ALU.mult)
+        for gm in range(2):
+            tt(A3("FP", 16 * gm, 16 * gm + 16), A3("FP", 16 * gm, 16 * gm + 16), A3("I3", 0, 16), ALU.add)
+        numbers(1)
+
+    def odd_final():
+        shape(state(1, 0), 30, 1)
+        for gm in range(2):
+            ts(A3("FB", 16 * gm, 16 * gm + 16), A3("I3", 0, 16), sm1(32, gm), ALU.mult, sm1(35, gm), ALU.add)
+            ts(A3("FC", 16 * gm, 16 * gm + 16), A3("I3", 0, 16), sm1(34, gm), ALU.is_ge, float(ZADDR), ALU.mult)
+        tt(A3("FA", 0, 32), A3("FB", 0, 32), A3("FC", 0, 32), ALU.max)
+        final_lists(1)
+
+    setup()
+    later_weights()
+    scalar_feats(0, {})
+    tt(A("STC", 0, U), IND(A("DS"), A("SLU")), A("SC"), ALU.add)
+    consts()
+    wrap("P4", 164, "VLT", "SC", U)
+    gathers(0, spread)
+    choose(0, state(1, 0), state(1, 1), idle0)
+    arrive(0, state(0, 0), state(0, 1), lambda: None)
+    choose(1, state(0, 1), state(0, 2), idle1)
+    arrive(1, state(1, 1), state(1, 2), even_own)
+    choose(2, state(1, 2), state(1, 0), odd_final)
+
+    def ev2(i):
+        return A("EL", 64 + i, 64 + i + 17, 16)
+
+    tt(sm(0), ev2(3), sm(36), ALU.mult)
+    ts(sm(1), ev2(3), -2.0, ALU.mult, 1.0, ALU.add)
+    tt(sm(2), ev2(4), sm(40), ALU.subtract)
+    tt(sm(3), ev2(0), sm(40), ALU.add)
+    tt(sm(4), sm(0), sm(41), ALU.add)
+    tt(sm(5), sm(1), sm(38), ALU.mult)
+    for gm in range(2):
+        ts(A3("FP", 16 * gm, 16 * gm + 16), A3("FP", 16 * gm, 16 * gm + 16), sm1(2, gm), ALU.add, float(PARTS), ALU.add)
+        ts(A3("FC", 16 * gm, 16 * gm + 16), A3("I3", 0, 16), sm1(3, gm), ALU.is_ge, float(ZADDR), ALU.mult)
+        ts(A3("FB", 16 * gm, 16 * gm + 16), A3("I3", 0, 16), sm1(5, gm), ALU.mult, sm1(4, gm), ALU.add)
+    tt(A3("FC", 0, 32), A3("FC", 0, 32), A3("FP", 0, 32), ALU.max)
+    tt(A3("FA", 0, 32), A3("FB", 0, 32), A3("FC", 0, 32), ALU.max)
+    final_lists(0)
+    cp(A("XS", PARTS, PARTS + CAP), A("LL", 480, 480 + CAP))
+    nout = [0]
+
+    def store(dst, src):
+        nout[0] += 16
+        sync("y", [src], [], "out0", 10 ** 6)
+        g.sync.dma_start(dst, src[0]).then_inc(T.sem.out0, 16)
+
+    for c in range(8):
+        o = A("FD", 512 * c, 512 * c + 512)
+        (cp if c % 2 else act)(o, IND(A("XS"), A("FU", 32 * c, 32 * c + 32)))
+        store(T.y[:, 512 * c:512 * c + 512], o)
+    for c in range(4):
+        (cp if c % 2 else act)(A("YO", 1024 * c, 1024 * c + 1024), IND(A("CS"), A("FU", 64 * c, 64 * c + 64)))
+    store(T.yo[:, :], (T.YO[0:128:16, :], "YO", range(W)))
+    g.sync.wait_ge(T.sem.out0, nout[0])
+    g.wait_ge(T.sem.loc, sent[0])
+    for k in ("v", "s", "t", "g"):
+        wait("g", "q" + k, cnt[k])

@@ -5,45 +5,27 @@ ACT = ActivationFunctionType
 U, CAP, W = 2624, 224, 4096
 PARTS, ZADDR, XSW = 8448, 8768, 8784
 MAGIC = 3221225472.0
-NS = (15, 15, 17)
-NS1 = (12, 11, 11)
+NS, NS1, NV = (18, 10, 12), (14, 8, 8), (5, 7, 7)
 BF, F32, I32, U16 = "bfloat16", "float32", "int32", "uint16"
-
-
-def _sb(n, d):
-    return ("sbuf", [128, n], d)
-
-
-SCRATCH = {
-    "X": _sb(W, BF), "OCI": _sb(164, I32), "CDI": _sb(256, I32), "OCU": _sb(164, U16), "CDF": _sb(256, F32),
-    "XG": _sb(U + 8, BF), "AD": _sb(U + 8, BF), "DS": _sb(U, BF), "SRC": _sb(U, BF), "SC": _sb(U, BF),
-    "STC": _sb(W, F32), "MW": _sb(W, BF), "MG": _sb(W + 144, BF), "FD": _sb(W, BF),
-    "XS": _sb(XSW, BF), "CS": _sb(XSW, F32), "YO": _sb(W, F32), "OCR": _sb(U, F32),
-    "SLU": _sb(164, U16), "VLU": _sb(164, U16), "MI": _sb(256, I32), "MJ": _sb(256, I32), "MU": _sb(256, U16),
-    "IDW": _sb(160, BF), "NEGI": _sb(128, BF), "EIG": _sb(128, BF), "BLK": _sb(128, BF), "WZ": _sb(128, BF),
-    "FS": _sb(144, BF), "FV": _sb(144, BF), "MAS": _sb(144, BF), "MAV": _sb(144, BF), "MB": _sb(144, BF),
-    "MC": _sb(144, BF), "SLT": _sb(144, BF), "VLT": _sb(144, BF), "TGT": _sb(144, BF), "CW": _sb(160, BF),
-    "WDL": _sb(128, BF), "WDR": _sb(128, BF), "WDZ": _sb(128, BF), "TRI": _sb(128, BF), "UOH": _sb(128, BF),
-    "WQ": _sb(128, BF), "WG": _sb(128, BF), "WK": _sb(128, BF), "WR": _sb(256, BF), "WRG": _sb(256, BF),
-    "WC1": _sb(128, BF), "WC2": _sb(128, BF), "WC3": _sb(128, BF),
-    "PI": _sb(4, I32), "COL": _sb(32, F32), "E16": _sb(16, BF), "RW": _sb(48, F32), "IOT": _sb(256, BF),
-    "B82": _sb(256, BF), "NKK": _sb(256, BF), "ONE": _sb(128, BF), "KT": _sb(CAP, BF), "KW": _sb(16, BF),
-    "CWB": _sb(8, BF), "NJ": _sb(64, BF),
-    "AS": _sb(3 * 72, BF), "AL": _sb(3 * 72, BF), "ES": _sb(3 * 32, BF), "EL": _sb(3 * 32, BF),
-    "LS": _sb(3 * 240, BF), "LL": _sb(3 * 240, BF),
-    "XH": _sb(64, BF), "LIM": _sb(4, F32), "RR": _sb(256, F32), "PEN": _sb(256, F32), "T1": _sb(256, F32),
-    "KEY": _sb(256, F32), "SM": _sb(96, F32), "OFF": _sb(4, U16), "MBS": _sb(32, BF), "GD": _sb(64, BF),
-    "TQ": _sb(32, F32), "DF": _sb(64, F32), "WS": _sb(2, BF), "CMP": _sb(2 * CAP, BF), "CU": _sb(16, U16),
-    "CI": _sb(32, I32), "SPT": _sb(64, F32), "SPR": _sb(64, F32), "SPU": _sb(64, U16), "SP": _sb(1024 + CAP, BF),
-    "OH": _sb(256, BF), "DD": _sb(4, BF), "ST": _sb(24, BF), "SMK": _sb(8, BF), "EU": _sb(4, U16), "EW": _sb(4, F32),
-    "OWN": _sb(32, BF), "OWR": _sb(32, BF), "ER": _sb(32, BF), "CT": _sb(144, F32), "OWU": _sb(16, U16),
-    "ND": _sb(CAP, F32), "TG": _sb(CAP, F32), "TGB": _sb(CAP, BF), "TU": _sb(32, U16), "NUM": _sb(CAP, F32),
-    "I3": ("sbuf", [128, 4, 16], F32), "FA": ("sbuf", [128, 4, 32], F32), "FB": ("sbuf", [128, 4, 32], F32),
-    "FC": ("sbuf", [128, 4, 32], F32), "FP": ("sbuf", [128, 4, 32], F32), "FT": _sb(128, F32), "FU": _sb(256, U16),
-    "P0": ("psum", [128, 512], F32), "P1": ("psum", [128, 512], F32), "P2": ("psum", [128, 512], F32),
-    "P3": ("psum", [128, 512], F32), "P4": ("psum", [128, 512], F32), "P5": ("psum", [128, 512], F32),
-    "P6": ("psum", [128, 512], F32), "P7": ("psum", [128, 512], F32),
-}
+SCRATCH = {}
+for _d, _l in (
+        (BF, dict(X=W, XG=U + 8, AD=U + 8, DS=U, SRC=U, SC=U, MW=W, MG=W + 144, FD=W, DI=U, XS=XSW, IDW=160, NEGI=128, EIG=128,
+                  BLK=128, WZ=128, FS=144, FV=144, MAS=144, MAV=144, MB=144, SLT=144, VLT=144, TGT=144, WB=128, WDN=128, LD=32,
+                  CB=256, CR=256, K16=16, WDL=128, WDR=128, WDZ=128, TRI=128, UOH=128, WQ=128, WG=128, WK=128, WR=256, WRG=256,
+                  WC1=128, WC2=128, WC3=128, E16=16, IOT=256, B82=256, NKK=256, ONE=128, KT=CAP, KW=16, CWB=8, NJ=64, AS=216,
+                  AL=216, ES=96, EL=96, LS=720, LL=720, XH=64, MBS=32, GD=64, WS=2, CMP=320, SP=1024 + CAP, OH=256, DD=4, ST=24,
+                  SMK=8, OWN=32, OWR=32, ER=32, TGB=CAP)),
+        (F32, dict(CDF=256, STC=W, CS=XSW, YO=W, OCR=U, BT=32, COL=32, RW=48, LIM=4, RR=256, KEY=256, SM=96, TQ=32, DF=64,
+                   SPT=64, SPR=64, EW=4, CT=144, ND=CAP, TG=CAP, NUM=CAP, FT=128)),
+        (I32, dict(OCI=164, CDI=256, MI=256, MJ=256, PI=4, CI=32)),
+        (U16, dict(OCU=164, SLU=164, VLU=164, MU=256, OFF=4, CU=16, SPU=64, EU=4, OWU=16, TU=32, FU=256))):
+    for _k in _l:
+        SCRATCH[_k] = ("sbuf", [128, _l[_k]], _d)
+SCRATCH["I3"] = ("sbuf", [128, 4, 16], F32)
+for _k in ("FA", "FB", "FC", "FP"):
+    SCRATCH[_k] = ("sbuf", [128, 4, 32], F32)
+for _k in range(8):
+    SCRATCH["P%d" % _k] = ("psum", [128, 512], F32)
 SEMAPHORES = ["qv", "qs", "qt", "qg", "ld0", "ld1", "ld2", "ld3", "ld4", "ld5", "ld6", "loc", "loc0", "a0", "a1", "a2",
               "e0", "e1", "e2", "l0", "l1", "l2", "out0"]
 
@@ -69,8 +51,14 @@ def rank_program(g, core, T, topo):
         n = SCRATCH[name][1][2]
         return (T[name][:, :, c0:c1], name, [n * b + c for b in range(4) for c in range(c0, c1)])
 
-    def A3b(name, b):
-        return (T[name][:, b, :], name, range(32 * b, 32 * b + 32))
+    def H(name, gm):
+        return A3(name, 16 * gm, 16 * gm + 16)
+
+    def B(name, k, n=128):
+        return A(name, n * k, n * k + n)
+
+    def S(name, c):
+        return A(name, c, c + 113, 16)
 
     def IND(win, off):
         return (win[0].indirect(off[0]), win[1], win[2], off)
@@ -155,14 +143,12 @@ def rank_program(g, core, T, topo):
     def sel(o, i, pat, cmp, fill, base, cm):
         op("g", lambda: g.affine_select(o[0], i[0], pat, cmp, float(fill), base, cm), [i], [o])
 
-    def ent(name, c0, phi, w):
-        v = A(name, c0, c0 + 113, 16)
-        sel(v, v, [[-16, 8]], ALU.not_equal, w, -phi, 1)
-
-    def ents(name, table):
-        for psi in table:
-            for phi, w in table[psi]:
-                ent(name, psi, phi, w)
+    def ents(table):
+        for k in range(max(len(v) for v in table.values())):
+            for key in table:
+                if k < len(table[key]):
+                    v = S(key[0], key[1])
+                    sel(v, v, [[-16, 8]], ALU.not_equal, table[key][k][1], -table[key][k][0], 1)
 
     def wrap(pb, n, name, src, width):
         for r in range(16):
@@ -198,8 +184,10 @@ def rank_program(g, core, T, topo):
     def io_(a, b):
         return A("IOT", a, b)
 
+    ADD, SUB, MUL, MAX, MIN = ALU.add, ALU.subtract, ALU.mult, ALU.max, ALU.min
     ident = A("IDW", 16, 144)
-    g8 = A("BLK", 0, 113, 16)
+    g8 = S("BLK", 0)
+    one_row = A("ONE", 0, 128, 1, 0, 1)
     for t in range(3):
         expect("AL", 72 * t, 72 * t + 72, "a%d" % t, rank - 1 - t)
         expect("EL", 32 * t, 32 * t + 32, "e%d" % t, rank + 1 + t)
@@ -215,25 +203,26 @@ def rank_program(g, core, T, topo):
     iota(A("B82", 0, 82), [[0, 2], [1, 41]], 32, 0)
     iota(A("B82", 88, 170), [[-1, 2], [0, 41]], 1, 0)
     ms(A("RW"), 0.0)
-    for a, b, c in ((3, 4, 2.0), (4, 5, -2.0), (5, 6, -1.0), (6, 8, 1.0), (8, 9, 2.0), (9, 11, 256.0), (11, 13, -256.0)):
+    for a, b, c in ((3, 4, 2.0), (4, 5, -2.0), (5, 6, -1.0), (6, 9, 1.0), (9, 11, 256.0), (11, 13, -256.0), (15, 16, -1.0)):
         ms(A("RW", a, b), c)
     ts(A("PI", 1, 2), A("PI", 0, 1), 15, ALU.bitwise_and)
     ts(A("PI", 2, 3), A("PI", 0, 1), 31, ALU.bitwise_and)
     cp(A("COL", 0, 2), A("PI", 1, 3))
     ts(A("E16"), io_(0, 16), col(0), ALU.is_equal)
-    tt(A("RW", 0, 16), A("RW", 0, 16), A("E16"), ALU.mult)
-    ts(col(10), A("E16", 5, 6), 256.0, ALU.mult)
-    for i in range(5):
-        ts(col(5 + i), A("E16", 13, 14), float(1 << i), ALU.mult)
-    red(col(2), A("RW", 0, 16), ALU.add)
-    ts(A("B82", 88, 170), A("B82", 88, 170), col(10), ALU.mult)
-    ts(A("B82", 0, 82), A("B82", 0, 82), col(2), ALU.mult)
-    tt(A("SRC", 0, 82), A("B82", 0, 82), A("B82", 88, 170), ALU.add)
+    tt(A("RW", 0, 16), A("RW", 0, 16), A("E16"), MUL)
+    ts(col(10), A("E16", 5, 6), 256.0, MUL)
+    for i in range(3):
+        ts(col(5 + i), A("E16", 13, 14), float(1 << i), MUL)
+    red(col(2), A("RW", 0, 16), ADD)
+    ts(A("B82", 88, 170), A("B82", 88, 170), col(10), MUL)
+    for i in range(3, 5):
+        ts(col(5 + i), A("E16", 13, 14), float(1 << i), MUL)
+    ts(A("B82", 0, 82), A("B82", 0, 82), col(2), MUL)
+    cp(A("OCU"), A("OCI"))
+    tt(A("SRC", 0, 82), A("B82", 0, 82), A("B82", 88, 170), ADD)
     for i in range(4):
         n = 82 << i
-        ts(A("SRC", n, 2 * n), A("SRC", 0, n), col(5 + i), ALU.add)
-    cp(A("OCU"), A("OCI"))
-    load("g", A("STC", U, W), T.x[:, 0:W - U], "ld5")
+        ts(A("SRC", n, 2 * n), A("SRC", 0, n), col(5 + i), ADD)
     act(A("ONE"), io_(0, 128), ACT.Identity, 1.0, 0.0)
     for name in ("IDW", "SLT", "MAS", "MB", "WDL", "WDR", "WDZ", "FS", "FV", "WK", "WQ", "WC3"):
         act(A(name), io_(0, SCRATCH[name][1][1]), ACT.Copy, None, 0.0)
@@ -241,32 +230,29 @@ def rank_program(g, core, T, topo):
     act(A("XG", U, U + 8), io_(0, 8), ACT.Copy, None, 0.0)
     act(A("AD", 0, 1), io_(0, 1), ACT.Copy, None, 0.0)
     act(A("AS"), io_(0, 216), ACT.Copy, None, 0.0)
-    sel(ident, A("ONE"), [[-1, 128]], ALU.is_equal, 0.0, 0, 1)
     sel(A("BLK"), A("ONE"), [[-16, 8], [0, 16]], ALU.is_ge, 0.0, 0, 1)
+    sel(ident, A("ONE"), [[-1, 128]], ALU.is_equal, 0.0, 0, 1)
     sel(A("BLK"), A("BLK"), [[16, 8], [0, 16]], ALU.is_ge, 0.0, 15, -1)
     act(A("SRC", 1312, U), A("SRC", 0, 1312), ACT.Identity, col(9))
     act(A("NEGI"), ident, ACT.Copy, None, -1.0)
     for name, cols in (("WDL", (0, 12)), ("WDR", (1, 10)), ("WDZ", (2,))):
         for c in cols:
-            act(A(name, c, c + 113, 16), g8)
+            act(S(name, c), g8)
     act(A("WZ"), A("BLK"), ACT.Copy, None, 61.0)
-    act(A("FS", 16, 129, 16), g8, ACT.Copy, None, -256.0)
-    act(A("FV", 16, 129, 16), g8, ACT.Copy, None, 512.0)
-    ents("SLT", {16: ((13, 82), (5, -41 / 256), (7, -41 / 256), (6, 1))})
-    ents("MAS", {16: ((1, 256), (9, 256), (10, -256), (3, -2 ** 17), (5, -2 ** 18), (6, -2 ** 18))})
+    act(S("FS", 16), g8, ACT.Copy, None, -256.0)
+    act(S("FV", 16), g8, ACT.Copy, None, 512.0)
+    load("g", A("STC", U, W), T.x[:, 0:W - U], "ld5")
+    ents({("MB", 16): ((0, 256), (11, 256), (12, -256), (1, -256), (9, -256), (10, 256), (3, 2 ** 17), (4, -2 ** 17),
+                       (8, 2 ** 16), (15, -2 ** 16)),
+          ("MAS", 16): ((1, 256), (9, 256), (10, -256), (3, -2 ** 17), (5, -2 ** 18), (6, -2 ** 18), (8, -2 ** 16)),
+          ("SLT", 16): ((13, 82), (5, -41 / 256), (7, -41 / 256), (6, 1)),
+          ("WQ", 6): ((0, 1), (11, 1), (12, -1), (1, -1), (9, -1), (10, 1)), ("WQ", 5): ((1, 1), (9, 1), (10, -1))})
     sel(A("MAV"), A("MAS"), [[0, 144]], ALU.is_ge, 0.0, 0, 0)
-    ent("MAV", 16, 2, -256)
-    ents("MB", {16: ((0, 256), (11, 256), (12, -256), (1, -256), (9, -256), (10, 256), (3, 2 ** 17), (4, -2 ** 17))})
     iota(A("NKK", 0, 256, 1, 0, 1), [[0, 2], [-1, 128]], 0, 0)
+    ents({("MAV", 16): ((2, -256),)})
 
     cp(IND(A("SC"), A("OCU", 0, 82)), A("SRC", 0, 1312))
     cp(IND(A("SC"), A("OCU", 82, 164)), A("SRC", 1312, U))
-    cp(A("CDF"), A("CDI"))
-    for a, b, c in ((19, 20, -103.5), (20, 21, 103.5), (21, 22, 33.0), (22, 23, -71.0), (23, 24, -32.0),
-                    (24, 25, -104.0), (25, 29, -1e5), (30, 31, 32.0)):
-        ms(A("RW", a, b), c)
-    tt(A("RW", 16, 32), A("RW", 16, 32), A("E16"), ALU.mult)
-    red(col(3), A("RW", 16, 32), ALU.add)
 
     def first_ends():
         act(A("AS", 0, 32), A("XG", 0, U - 81, 82))
@@ -279,13 +265,17 @@ def rank_program(g, core, T, topo):
             g.sync.dma_start(T[name][:, c:c + n], T.x[:, 0:n]).then_inc(T.sem.ld6, 16)
 
     def dist_a(src, c0, n, pb, d0):
+        if pb is None:
+            tt(A("DI", c0, c0 + n), A(src, c0, c0 + n), A(src, c0 + 1, c0 + n + 1), SUB)
+            act(A("AD", d0, d0 + n), A("DI", c0, c0 + n), ACT.Abs)
+            return
         mm(A(pb, 0, n), ident, A(src, c0, c0 + n), True, False)
         mm(A(pb, 0, n), A("NEGI"), A(src, c0 + 1, c0 + n + 1), False, True)
         act(A("AD", d0, d0 + n), A(pb, 0, n), ACT.Abs)
 
     def dist_b(src, c0, n, pb, d0, last):
         mm(A(pb, 0, n), A("WDL"), A("AD", d0, d0 + n), True, False)
-        mm(A(pb, 0, n), A("WDR"), A("AD", d0 + 1, d0 + n + 1), False, False)
+        mm(A(pb, 0, n), A("WDR" if last else "WDN"), A("AD", d0 + 1, d0 + n + 1), False, False)
         mm(A(pb, 0, n), A("WDZ"), A(src, c0, c0 + n), False, last)
 
     def lists(t):
@@ -293,11 +283,14 @@ def rank_program(g, core, T, topo):
         for bit in range(2):
             for qq in range(4):
                 mm(A("P4", 4 * bit + qq, 256, 8), A("WZ"), A("AL", b + 32 * bit, b + 32 * bit + 32), True, True)
-        for lo, hi in ((0, 128), (128, 256)):
-            tt(A("MI", lo, hi), A("CDF", lo, hi), A("P4", lo, hi), ALU.add)
+        halves = ((0, 96), (96, 256))
+        for lo, hi in halves:
+            tt(A("MI", lo, hi), A("CDF", lo, hi), A("P4", lo, hi), ADD)
+        for lo, hi in halves:
             ts(A("MJ", lo, hi), A("MI", lo, hi), 4095, ALU.bitwise_and)
+        for lo, hi in halves:
             cp(A("MU", lo, hi), A("MJ", lo, hi))
-        ts(A("XH"), A("AL", b, b + 64), 0.5, ALU.mult)
+        ts(A("XH"), A("AL", b, b + 64), 0.5, MUL)
 
     def setup():
         chunks = [(c, min(512, U - c)) for c in range(0, U, 512)]
@@ -307,87 +300,89 @@ def rank_program(g, core, T, topo):
                 act(A("XG", 16 * lo, 16 * hi), IND(A("X", 0, U), A("OCU", lo, hi)))
             if i == 2:
                 first_ends()
-            if i < len(chunks):
+            if i < 3:
                 c, n = chunks[i]
                 dist_a("XG", c, n, "P%d" % (i % 2), c + 1)
+            if i == 3:
+                dist_a("XG", 1536, 512, None, 1537)
+                dist_a("XG", 2048, 576, None, 2049)
             if i > 0:
                 c, n = chunks[i - 1]
                 dist_b("XG", c, n, "P%d" % (2 + i % 2), c, True)
-                (act if i < 4 else cp)(A("DS", c, c + n), A("P%d" % (2 + i % 2), 0, n))
+                (act if i != 4 else cp)(A("DS", c, c + n), A("P%d" % (2 + i % 2), 0, n))
             if i == 3:
-                for name in ("CW", "VLT", "WG", "WC1", "WC2", "MC", "TGT"):
+                for name in ("VLT", "WG", "WC1", "WC2", "WB", "WDN", "TGT"):
                     ms(A(name), 0.0)
                 for name, psi, phi, w in (
-                        ("WQ", 0, 3, 1), ("WQ", 3, 7, 1), ("WQ", 4, 15, 1), ("WQ", 7, 13, 16384), ("WQ", 8, 13, 1),
-                        ("WC1", 10, 9, -256), ("WC1", 12, 8, 256), ("WC1", 15, 3, 1), ("WC2", 9, 10, -131072),
-                        ("WC2", 10, 10, -131072), ("WC2", 12, 4, 256), ("WC2", 13, 11, 1), ("WC2", 15, 3, 2)):
-                    ts(A(name, psi, psi + 113, 16), A("IDW", 16 + phi, 129 + phi, 16), float(w), ALU.mult)
-            if i == 4:
+                        ("WQ", 0, 3, 1), ("WQ", 3, 7, 1), ("WQ", 4, 9, 1), ("WQ", 11, 14, 1), ("WQ", 7, 13, 16384),
+                        ("WQ", 8, 13, 1), ("WC1", 10, 9, -256), ("WC1", 12, 8, 256), ("WC2", 12, 4, 256), ("WC2", 13, 11, 1)):
+                    ts(S(name, psi), S("IDW", 16 + phi), float(w), MUL)
                 wrap("P6", 164, "SLT", "SC", U)
-                ts(A("SLU"), A("P6", 0, 164), 9.0, ALU.add)
-            if i == 5:
+                cp(A("CDF"), A("CDI"))
+                ts(A("SLU"), A("P6", 0, 164), 9.0, ADD)
+            if i == 4:
                 lists(0)
+            if i == 5:
+                for a, b, c in ((19, 20, -103.5), (20, 21, 103.5), (21, 22, 33.0), (22, 23, -71.0), (23, 24, -32.0),
+                                (24, 29, -1e5), (30, 31, 32.0), (31, 32, -1e5)):
+                    ms(A("RW", a, b), c)
+                tt(A("RW", 16, 32), A("RW", 16, 32), A("E16"), MUL)
+                red(col(3), A("RW", 16, 32), ADD)
 
     def later_weights():
         iota(A("NJ", 0, 64, 1, 0, 1), [[0, 2], [-1, 32]], 0, 0)
         for gm in range(2):
-            sel(A("WR", 128 * gm, 128 * gm + 128), A("WC3"), [[-32, 4], [0, 32]], ALU.not_equal, 16384.0, -(16 * gm + 13), 1)
-            v = A("WRG", 128 * gm, 128 * gm + 128)
-            sel(v, A("EIG"), [[-32, 4], [0, 32]], ALU.is_ge, 0.0, -16 * gm, 1)
-            sel(v, v, [[32, 4], [0, 32]], ALU.is_ge, 0.0, 16 * gm + 15, -1)
-        ents("WQ", {1: ((7, 1), (8, -1)), 2: ((13, 256), (14, 1), (7, 1)), 5: ((1, 1), (9, 1), (10, -1)),
-                    6: ((0, 1), (11, 1), (12, -1), (1, -1), (9, -1), (10, 1))})
+            sel(B("WRG", gm), A("EIG"), [[-32, 4], [0, 32]], ALU.is_ge, 0.0, -16 * gm, 1)
+            sel(B("WR", gm), A("WC3"), [[-32, 4], [0, 32]], ALU.not_equal, 16384.0, -(16 * gm + 13), 1)
         sel(A("TRI"), A("ONE"), [[1, 128]], ALU.is_ge, 0.0, 0, -1)
+        for gm in range(2):
+            sel(B("WRG", gm), B("WRG", gm), [[32, 4], [0, 32]], ALU.is_ge, 0.0, 16 * gm + 15, -1)
         sel(A("TRI"), A("TRI"), [[-32, 4], [0, 32]], ALU.is_ge, 0.0, 0, 1)
-        v = A("CW", 32, 129, 32)
-        sel(v, A("ONE", 0, 4), [[-32, 4]], ALU.is_ge, 0.0, 0, 1)
-        sel(v, v, [[32, 4]], ALU.is_ge, 0.0, 31, -1)
-        ents("VLT", {16: ((13, 1), (5, -0.125), (7, -0.125))})
-        ents("WC1", {3: ((8, -1), (9, -1), (0, -1), (1, 2), (10, 0.5), (3, -1)), 5: ((8, 1), (10, 1), (3, -1), (12, -1)),
-                     6: ((9, -1), (10, 1), (2, -1), (3, 1)), 7: ((8, -1), (1, 1)), 8: ((8, -1), (9, -1), (0, -1), (1, 2)),
-                     9: ((5, 1), (9, -256)), 11: ((5, 1), (8, 256))})
-        ents("WC2", {3: ((9, 1), (8, -1), (0, -1), (10, 2.5), (4, -2)), 6: ((10, 2), (0, -1), (4, -1)),
-                     7: ((9, 1), (8, -1), (10, 1), (4, -1)), 8: ((9, 1), (8, -1), (0, -1), (10, 2), (4, -2)),
-                     11: ((5, 1), (4, 256)), 14: ((8, 1), (6, 1))})
+        ents({("VLT", 16): ((13, 1), (5, -0.125), (7, -0.125)), ("WQ", 1): ((7, 1), (3, -1)),
+              ("WQ", 2): ((13, 256), (14, 1), (7, 1))})
+        ents({("WC1", 3): ((8, -1), (9, -1), (0, -1), (1, 2), (10, 0.5), (3, -1)),
+              ("WC1", 5): ((8, 1), (10, 1), (3, -1), (12, -1)), ("WC1", 6): ((9, -1), (10, 1), (2, -1), (3, 1)),
+              ("WC1", 7): ((8, -1), (1, 1)), ("WC1", 14): ((8, 1), (1, -1), (3, 128)), ("WC1", 9): ((5, 1), (9, -256)),
+              ("WC1", 11): ((5, 1), (8, 256)), ("WC1", 15): ((9, 1), (0, 1), (1, -1)),
+              ("WC2", 3): ((9, 1), (8, -1), (0, -1), (10, 2.5), (4, -2)), ("WC2", 6): ((10, 2), (0, -1), (4, -1)),
+              ("WC2", 7): ((9, 1), (8, -1), (10, 1), (4, -1)), ("WC2", 9): ((10, 252), (3, 2)),
+              ("WC2", 15): ((0, 1), (10, -1), (4, 1)), ("WC2", 11): ((5, 1), (4, 256)), ("WC2", 14): ((8, 1), (6, 1))})
 
-    def last_weights():
-        ents("MC", {16: ((7, 1), (8, -1))})
-        ents("WC3", {6: ((9, 1), (8, -1), (10, -255), (4, -1), (3, 256)), 13: ((11, 2), (10, 1), (12, -1 / 256))})
-        ents("TGT", {16: ((13, 128), (14, 1), (7, 1), (6, -2))})
+    def rest_weights():
+        ents({("WC3", 6): ((9, 1), (8, -1), (10, -255), (4, -1), (3, 256)), ("WC3", 13): ((11, 2), (10, 1), (12, -1 / 256)),
+              ("TGT", 16): ((13, 128), (14, 1), (7, 1), (6, -2))})
         iota(A3("I3", 0, 16), [[16, 4], [1, 16]], 0, 0)
         iota(A("YO", 0, U), [[1, U]], 0, 0)
 
-    def feat(t, j, last=False):
+    def feat_mm(t, j, last=False):
+        r, h = j % 16, j // 16
+        mm(B("P0", h), A("FS" if j < NS[t] else "FV", 16 - r, 144 - r), B("FD", j), False, last)
+
+    def feat(t, j, last=False, now=True):
         for bit in range(2):
             e = 2 * j + bit
-            o, i = A("FD", 64 * e, 64 * e + 64), IND(A("X"), A("MU", 4 * e, 4 * e + 4))
-            xe = A("AL", 72 * t + 32 * bit + j, 72 * t + 32 * bit + j + 1)
+            o, i = B("FD", e, 64), IND(A("X"), B("MU", e, 4))
+            xe = B("AL", 72 * t + 32 * bit + j, 1)
             if j < NS[t]:
                 act(o, i, ACT.Abs, xe, -1.0)
             else:
-                ts(o, i, xe, ALU.min, A("XH", 32 * bit + j, 32 * bit + j + 1), ALU.subtract)
-        r, h = j % 16, j // 16
-        mm(A("P0", 128 * h, 128 * h + 128), A("FS" if j < NS[t] else "FV", 16 - r, 144 - r),
-           A("FD", 128 * j, 128 * j + 128), False, last)
+                ts(o, i, xe, MIN, B("XH", 32 * bit + j, 1), SUB)
+        if now:
+            feat_mm(t, j, last)
 
     def meta(t, j0, j1):
-        o = A("MG", 128 * j0, 128 * j1)
         if t == 0:
-            act(o, IND(A("STC"), A("MU", 8 * j0, 8 * j1)), ACT.Relu, col(3))
+            act(A("MG", 128 * j0, 128 * j1), IND(A("STC"), A("MU", 8 * j0, 8 * j1)), ACT.Relu, col(3))
         else:
-            act(o, IND(A("MW"), A("MU", 8 * j0, 8 * j1)), ACT.Relu)
-
-    def meta_mm(t, j0, j1):
+            for j in range(j0, j1):
+                act(B("MG", j), IND(A("MW"), B("MU", j, 8)), ACT.Relu, B("BT", j, 1))
         for j in range(j0, j1):
             r, h = j % 16, j // 16
-            rhs = A("MG", 128 * j, 128 * j + 128)
-            mm(A("P0", 128 * h, 128 * h + 128), A("MAS" if j < NS[t] else "MAV", 16 - r, 144 - r), rhs, False, False)
-            mm(A("P1", 128 * h, 128 * h + 128), A("MB", 16 - r, 144 - r), rhs, r == 0, r == 15)
-            if t > 0:
-                mm(A("P2", 128 * h, 128 * h + 128), A("MC", 16 - r, 144 - r), rhs, r == 0, r == 15)
+            mm(B("P0", h), A("MAS" if j < NS[t] else "MAV", 16 - r, 144 - r), B("MG", j), False, False)
+            mm(B("P1", h), A("MB", 16 - r, 144 - r), B("MG", j), r == 0, r == 15)
 
     def scalar_feats(t, extra):
-        mm(A("P0", 0, 256), A("ONE", 0, 128, 1, 0, 1), A("NKK", 0, 256, 1, 0, 1), True, False)
+        mm(A("P0", 0, 256), one_row, A("NKK", 0, 256, 1, 0, 1), True, False)
         for j in range(NS1[t]):
             feat(t, j)
             if j in extra:
@@ -396,172 +391,191 @@ def rank_program(g, core, T, topo):
     def gathers(t, extra):
         rest = list(range(NS[t], 32))
         cuts = (0, 4, 8, 12, 16, 20, 24, 28, 30, 31, 32)
-        nv = 7 if t else 6
+        nv = NV[t]
         per = [len(rest) * (c + 1) // nv - len(rest) * c // nv for c in range(nv)] + [0] * (10 - nv)
+        mine = []
         for c in range(10):
             meta(t, cuts[c], cuts[c + 1])
+            for j in mine:
+                feat_mm(t, j)
             mine, rest = rest[:per[c]], rest[per[c]:]
             for j in mine:
-                feat(t, j)
-            meta_mm(t, cuts[c], cuts[c + 1])
+                feat(t, j, False, False)
         extra()
         for j in range(NS1[t], NS[t]):
             feat(t, j, j == NS[t] - 1)
-        ts(A("RR"), A("P1", 0, 256), 0.0, ALU.max)
-        if t > 0:
-            for h in range(2):
-                ts(A("PEN", 128 * h, 128 * h + 128), A("P2", 128 * h, 128 * h + 128), A("LIM", 2 + h, 3 + h), ALU.is_gt,
-                   -262144.0, ALU.mult)
-            tt(A("T1"), A("RR"), A("PEN"), ALU.add)
+        ts(A("RR"), A("P1", 0, 256), 0.0, MAX)
 
     def q(i):
         return A("TQ", i, i + 17, 16)
 
     def q1(i, gm):
-        return A("TQ", i + 16 * gm, i + 16 * gm + 1)
+        return B("TQ", i + 16 * gm, 1)
 
     def state(par, gen):
         return 8 * gen + 4 * par
 
-    def choose(t, s_old, s_new, s_idle):
+    def choose(t, s_old, s_new, s_idle, fill=lambda: None):
         par = 1 - t % 2
-        tt(A("KEY"), A("P0", 0, 256), A("T1" if t else "RR"), ALU.add)
         for h in range(2):
-            red(sm1(0, h), A("KEY", 128 * h, 128 * h + 128), ALU.max)
-        ts(sm(1), sm(0), MAGIC, ALU.add, MAGIC, ALU.subtract)
+            tt(B("KEY", h), B("P0", h), B("RR", h), ADD)
         for h in range(2):
-            ts(A("OFF", h, h + 1), sm1(1, h), sm1(0, h), ALU.subtract, col(11 + h), ALU.add)
+            red(sm1(0, h), B("KEY", h), MAX)
+        for h in range(2):
+            ts(sm1(1, h), sm1(0, h), MAGIC, ADD, MAGIC, SUB)
+        for h in range(2):
+            ts(B("OFF", h, 1), sm1(1, h), sm1(0, h), SUB, col(11 + h), ADD)
+        tt(sm(2), sm(1), sm(0), SUB)
         cp(A("MBS"), IND(A("MG"), A("OFF", 0, 2)))
-        tt(sm(2), sm(1), sm(0), ALU.subtract)
         for h in range(2):
-            act(A("GD", 16 * h, 16 * h + 16), A("E16"), ACT.Relu, None, sm1(1, h))
+            act(B("GD", h, 16), A("E16"), ACT.Relu, None, sm1(1, h))
         for h in range(2):
-            ts(A("GD", 32 + 16 * h, 48 + 16 * h), A("E16"), sm1(2, h), ALU.mult)
-        mm(A("P3", 0, 32), A("WQ"), A("MBS"), True, False)
-        mm(A("P3", 0, 32), A("WG"), A("GD", 0, 32), False, False)
+            ts(B("GD", 2 + h, 16), A("E16"), sm1(2, h), MUL)
+        mm(A("P3", 0, 32), A("WG"), A("GD", 0, 32), True, False)
+        mm(A("P3", 0, 32), A("WQ"), A("MBS"), False, False)
         mm(A("P3", 0, 32), A("WK"), A("GD", 32, 64), False, True)
-        mm(A("P5", 0, 64), A("ONE", 0, 128, 1, 0, 1), A("NJ", 0, 64, 1, 0, 1), True, False)
+        mm(A("P5", 0, 64), one_row, A("NJ", 0, 64, 1, 0, 1), True, False)
         for gm in range(2):
-            mm(A("P5", 32 * gm, 32 * gm + 32), A("WR", 128 * gm, 128 * gm + 128), A("MBS"), False, False)
-            mm(A("P5", 32 * gm, 32 * gm + 32), A("WRG", 128 * gm, 128 * gm + 128), A("GD", 0, 32), False, gm == 1)
+            mm(B("P5", gm, 32), B("WR", gm), A("MBS"), False, False)
+            mm(B("P5", gm, 32), B("WRG", gm), A("GD", 0, 32), False, gm == 1)
+        fill()
         tr(A("TQ"), A("P3", 0, 32))
         ts(sm(3), q(0), 0.0, ALU.is_gt)
-        if t == 0:
-            ts(sm(4), sm(3), 2.0, ALU.mult, -1.0, ALU.add)
-            ts(sm(5), q(2), 128.0 * par, ALU.add)
-        else:
-            ts(sm(6), q(4), 2.0, ALU.is_ge, -2.0, ALU.mult)
-            ts(sm(7), sm(3), 2.0, ALU.mult, -1.0, ALU.add)
-            tt(sm(8), sm(6), q(3), ALU.mult)
-            ts(sm(9), sm(6), 1.0, ALU.add)
-            tt(sm(10), sm(8), q(2), ALU.add)
-            tt(sm(4), sm(7), sm(9), ALU.mult)
-            ts(sm(5), sm(10), 128.0 * par, ALU.add)
+        if t > 0:
+            ts(sm(6), q(4), 253.0, ALU.is_ge, -2.0, MUL)
+            ts(sm(42), q(11), 128.0, ALU.is_ge, 128.0, MUL)
         for gm in range(2):
-            ts(A("DF", 32 * gm, 32 * gm + 32), A("P5", 32 * gm, 32 * gm + 32), q1(7, gm), ALU.subtract, col(13), ALU.add)
+            ts(B("DF", gm, 32), B("P5", gm, 32), q1(7, gm), SUB, col(13), ADD)
+        if t == 0:
+            ts(sm(4), sm(3), 2.0, MUL, -1.0, ADD)
+            ts(sm(43), sm(3), 0.5, MUL)
+        else:
+            ts(sm(7), sm(3), 2.0, MUL, -1.0, ADD)
+            tt(sm(8), sm(6), q(3), MUL)
+            ts(sm(9), sm(6), 1.0, ADD)
+            tt(sm(10), q(2), sm(42), SUB)
+            ts(sm(21), sm(42), -1 / 128, MUL, 0.5, ADD)
+            tt(sm(4), sm(7), sm(9), MUL)
+            tt(sm(5), sm(10), sm(8), ADD)
+            tt(sm(43), sm(21), sm(3), MUL)
         for b in range(2):
             for gm in range(2):
-                c = 32 * b + 16 * gm
-                act(A("SPT", c, c + 16), io_(16 * b, 16 * b + 16), ACT.Identity, sm1(5, gm), sm1(4, gm))
+                act(B("SPT", 2 * b + gm, 16), B("IOT", b, 16), ACT.Identity, sm1(5, gm) if t else q1(2, gm), sm1(4, gm))
         for gm in range(2):
-            red(sm1(11, gm), A("DF", 32 * gm, 32 * gm + 32), ALU.min, True)
+            red(sm1(11, gm), B("DF", gm, 32), MIN, True)
+        tt(sm(44), sm(43), q(1), ADD)
+        ts(sm(17), q(10), 64.0, ALU.is_lt)
+        if t < 2:
+            tt(sm(19), sm(3), q(6), MUL)
+        ts(sm(12), sm(44), 1.0, ADD, 0.0, MAX)
         tr(A("SPR"), A("SPT"))
-        ts(sm(12), q(1), 1.0, ALU.add, 0.0, ALU.max)
+        if t > 0:
+            ts(sm(23), sm(21), 0.0, ALU.is_lt)
+        tt(sm(13), sm(12), q(9), MIN)
         for b in range(2):
-            ts(A("SPU", b, 64, 2), A("SPR", 32 * b, 32 * b + 32), float(XSW - 1), ALU.min)
+            ts(A("SPU", b, 64, 2), B("SPR", b, 32), 128.0 * par, ADD, float(XSW - 1), MIN)
         act(A("SP", 0, 1024), IND(A("XS"), A("SPU")))
-        tt(sm(13), sm(12), q(9), ALU.min)
         for gm in range(2):
-            ts(A("WS", gm, gm + 1), sm1(11, gm), 4096.0, ALU.is_ge, sm1(13, gm), ALU.mult)
-        mm(A("P3", 0, 2), A("TRI"), A("WS"), True, True)
-        ts(sm(14), A("WS"), -1.0, ALU.mult, 32.0, ALU.add)
-        cp(sm(15), A("P3", 0, 2))
-        for gm in range(2):
-            ts(A("CMP", CAP * gm, CAP * gm + CAP), io_(0, CAP), sm1(15, gm), ALU.is_ge, sm1(14, gm), ALU.mult)
-        mm(A("P6", 0, 14), ident, A("KW", 0, 14), True, False)
-        for gm in range(2):
-            for r in range(16):
-                o = 32 - 16 * gm - r
-                mm(A("P6", 0, 14), A("CW", o, o + 128), A("CMP", CAP * gm + r, CAP * gm + CAP, 16), False,
-                   gm == 1 and r == 15)
+            ts(B("WS", gm, 1), sm1(11, gm), 4096.0, ALU.is_ge, sm1(13, gm), MUL)
         eb = 32 * t
 
         def ev(i):
             return A("ES", eb + i, eb + i + 17, 16)
 
-        ts(sm(16), sm(15), float(CAP), ALU.is_le)
-        ts(sm(17), q(10), 64.0, ALU.is_lt)
-        tt(sm(18), sm(15), A("WS"), ALU.subtract)
-        tt(ev(0), sm(16), A("WS"), ALU.mult)
         if t < 2:
-            tt(sm(19), sm(3), q(6), ALU.mult)
-        ts(ev(4), sm(18), 255.0, ALU.min)
-        tt(ev(1), ev(0), sm(17), ALU.mult)
-        ts(ev(2), ev(0), 0.0, ALU.is_gt)
-        if t < 2:
-            tt(ev(5), sm(19), q(5), ALU.add)
-        ts(ev(3), ev(1), 0.0, ALU.is_gt)
-        send(A("ES", eb, eb + 32), "EL", eb, eb + 32, "e%d" % t, rank - 1 - t)
-        tt(sm(20), sm(4), ev(0), ALU.mult)
+            tt(ev(5), sm(19), q(5), ADD)
         if t > 0:
-            tt(sm(21), q(4), sm(6), ALU.add)
-            tt(sm(22), sm(3), sm(21), ALU.not_equal)
-        bit = sm(22) if t > 0 else sm(3)
+            tt(sm(22), sm(3), sm(23), ALU.not_equal)
+        mm(A("P3", 0, 2), A("TRI"), A("WS"), True, True)
+        tt(sm(29), A("WS"), sm(17), MUL)
+        ts(sm(14), A("WS"), -1.0, MUL, 32.0, ADD)
+        ts(sm(16), A("P3", 0, 2), float(CAP), ALU.is_le)
+        tt(sm(18), A("P3", 0, 2), A("WS"), SUB)
+        ts(sm(45), A("P3", 0, 2), -7.5, ADD)
+        cp(sm(15), A("P3", 0, 2))
+        tt(ev(0), sm(16), A("WS"), MUL)
+        tt(ev(1), sm(16), sm(29), MUL)
+        tt(ev(2), sm(16), A("WS"), MIN)
+        tt(ev(3), sm(16), sm(29), MIN)
+        ts(ev(4), sm(18), 255.0, MIN)
+        send(B("ES", t, 32), "EL", eb, eb + 32, "e%d" % t, rank - 1 - t)
+        ts(sm(46), sm(45), MAGIC / 16, ADD, MAGIC / 16, SUB)
+        mm(A("P6", 0, 14), ident, A("KW", 0, 14), True, False)
+        tt(sm(1), sm(4), sm(22) if t > 0 else sm(3), MUL)
         for gm in range(2):
-            ts(A("OH", 128 * gm, 128 * gm + 128), A("UOH"), q1(8, gm), ALU.is_equal, -1.0, ALU.mult)
-        tt(A("DD", 1, 4, 2), sm(20), bit, ALU.mult)
+            ts(B("OH", gm), A("UOH"), q1(8, gm), ALU.is_equal, -1.0, MUL)
+        tt(sm(47), sm(15), sm(46), SUB)
+        tt(sm(2), sm(4), sm(1), SUB)
+        for gm in range(2):
+            ts(A("CMP", 32 * gm, 32 * gm + 14), A("K16", 0, 14), sm1(46, gm), ALU.is_gt, sm1(14, gm), MUL)
+            ts(A("CMP", 32 * gm + 16, 32 * gm + 30), A("K16", 0, 14), sm1(46, gm), ALU.is_equal, sm1(14, gm), MUL)
+        for gm in range(2):
+            ts(A("CMP", 64 + 128 * gm, 192 + 128 * gm), B("CR", gm), sm1(47, gm), ALU.is_gt)
+        for gm in range(2):
+            mm(A("P6", 0, 14), B("CB", gm), A("CMP", 32 * gm, 32 * gm + 14), False, False)
+            mm(A("P6", 0, 14), A("CMP", 64 + 128 * gm, 192 + 128 * gm), A("CMP", 32 * gm + 16, 32 * gm + 30), False, gm == 1)
+        tt(A("DD", 1, 4, 2), sm(1), ev(0), MUL)
+        tt(A("DD", 0, 3, 2), sm(2), ev(0), MUL)
         cp(A("CU", 0, 14), A("P6", 0, 14))
-        tt(A("DD", 0, 3, 2), sm(20), A("DD", 1, 4, 2), ALU.subtract)
         mm(A("P5", 0, 4), ident, A("ST", s_old, s_old + 4), True, False)
         for gm in range(2):
-            mm(A("P5", 2 * gm, 2 * gm + 2), A("OH", 128 * gm, 128 * gm + 128), A("DD", 2 * gm, 2 * gm + 2), False, gm == 1)
+            mm(B("P5", gm, 2), B("OH", gm), B("DD", gm, 2), False, gm == 1)
         lb = 240 * t
-        cp(A("LS", lb, lb + CAP), IND(A("SP"), A("CU", 0, 14)))
         if t < 2:
             cp(A("CI", 0, 14), A("P6", 0, 14))
+        cp(A("LS", lb, lb + CAP), IND(A("SP"), A("CU", 0, 14)))
+        if t < 2:
             for h in range(2):
-                act(A("SMK", 4 * h, 4 * h + 4), A("P5", 0, 4), ACT.Copy, None, col(14 + h))
+                act(B("SMK", h, 4), A("P5", 0, 4), ACT.Copy, None, col(14 + h))
             ts(A("CI", 16, 30), A("CI", 0, 14), 5, ALU.arith_shift_right)
-            mm(A("P3", 0, 4), ident, A("CWB", 4 * par, 4 * par + 4), True, False)
+            mm(A("P3", 0, 4), ident, B("CWB", par, 4), True, False)
             for gm in range(2):
                 for h in range(2):
                     o = 16 - 16 * gm + 16 * h
-                    mm(A("P3", h, 4, 2), A("IDW", o, o + 128), A("SMK", 4 * h + 2 * gm, 4 * h + 2 * gm + 2), False,
-                       gm == 1 and h == 1)
+                    mm(A("P3", h, 4, 2), A("IDW", o, o + 128), B("SMK", 2 * h + gm, 2), False, gm == 1 and h == 1)
             ab = 72 * (t + 1)
             cp(A("EU"), A("P3", 0, 4))
             cp(A("EW"), A("P3", 0, 4))
             act(A("AS", ab, ab + 64), IND(A("XS"), A("EU")))
-            tt(A("AS", ab + 64, ab + 66), A("EW", 2, 4), A("EW", 0, 2), ALU.subtract)
             cp(A("LS", lb + CAP, lb + CAP + 14), A("CI", 16, 30))
+            tt(A("AS", ab + 64, ab + 66), A("EW", 2, 4), A("EW", 0, 2), SUB)
             send(A("AS", ab, ab + 72), "AL", ab, ab + 72, "a%d" % (t + 1), rank + 2 + t)
         send(A("LS", lb, lb + 240), "LL", lb, lb + 240, "l%d" % t, rank - 1 - t)
         act(A("ST", s_new, s_new + 4), A("P5", 0, 4))
         s_idle()
 
+    def hd(s):
+        return A("ST", s, s + 3, 2)
+
     def own_vars(s, par):
-        cp(A("OWN", 8, 25, 16), A("ST", s, s + 3, 2))
-        cp(A("OWN", 9, 26, 16), A("ST", s + 1, s + 4, 2))
+        cp(A("OWN", 8, 25, 16), hd(s))
+        cp(A("OWN", 9, 26, 16), hd(s + 1))
         ms(A("OWN", 12, 29, 16), 256.0 * (1 - par))
+        tt(sm(24), hd(s + 1), hd(s), SUB)
         tr(A("OWR"), A("OWN"))
-        tt(sm(24), A("ST", s + 1, s + 4, 2), A("ST", s, s + 3, 2), ALU.subtract)
-        ts(A("CT", 32 - 32 * par, 64 - 32 * par), io_(0, 32), 0.0, ALU.mult, col(4), ALU.add)
+        act(B("CT", 1 - par, 32), io_(0, 32), ACT.Identity, col(4), 0.0)
 
     def arrive(t, s_old, s_new, more):
         par = t % 2
-        eb, lb, c0 = 32 * t, 240 * t, U + CAP * t
+        eb, lb, c0, ab = 32 * t, 240 * t, U + CAP * t, 72 * (t + 1)
 
         def ev(i):
             return A("EL", eb + i, eb + i + 17, 16)
 
-        tt(ev(6), ev(3), sm(24), ALU.mult)
-        tr(A("ER"), A("EL", eb, eb + 32))
+        tr(A("ER"), B("EL", t, 32))
         mm(A("P7", 0, 32), A("WC1"), A("OWR"), True, False)
         mm(A("P7", 0, 32), A("WC1"), A("ER"), False, True)
-        cp(A("CT", 32 * par, 32 * par + 32), A("P7", 0, 32))
-        tt(A("MW", 0, 640), IND(A("CT", 0, 64), A("VLU", 0, 40)), A("STC", 0, 640), ALU.add)
+        tt(ev(6), ev(3), sm(24), MUL)
+        cp(B("CT", par, 32), A("P7", 0, 32))
+        tr(A("ER"), B("EL", t, 32))
+        tt(A("MW", 0, 640), IND(A("CT", 0, 64), A("VLU", 0, 40)), A("STC", 0, 640), ADD)
         lists(t + 1)
+        act(A("LIM", 0, 2), A("AL", ab + 64, ab + 66), ACT.Abs)
+        act(A("LIM", 2, 4), A("LIM", 0, 2), ACT.Identity, col(24))
         act(A("X", c0, c0 + CAP), A("LL", lb, lb + CAP))
+        for h in range(2):
+            act(B("LD", h, 16), A("E16"), ACT.Copy, None, B("LIM", 2 + h, 1))
+        mm(A("P2", 0, 32), A("WB"), A("LD"), True, True)
         dist_a("X", c0 - 1, CAP + 1, "P6", 0)
         dist_b("X", c0, CAP, "P3", 0, False)
         mm(A("P3", 0, CAP), ident, A("KT"), False, True)
@@ -569,166 +583,179 @@ def rank_program(g, core, T, topo):
         def nd():
             act(A("ND"), A("P3", 0, CAP))
             for k, name in ((1, "WC2"), (2, "WC3")):
-                mm(A("P7", 32 * k, 32 * k + 32), A(name), A("OWR"), True, False)
-                mm(A("P7", 32 * k, 32 * k + 32), A(name), A("ER"), False, True)
+                mm(B("P7", k, 32), A(name), A("OWR"), True, False)
+                mm(B("P7", k, 32), A(name), A("ER"), False, True)
+            act(A("BT"), A("P2", 0, 32))
             act(A("CT", 64, 96), A("P7", 32, 64))
             act(A("CT", 104, 136), A("P7", 64, 96))
 
         scalar_feats(t + 1, {1: nd})
-        tt(A("MW", 640, U), IND(A("CT", 0, 64), A("VLU", 40, 164)), A("STC", 640, U), ALU.add)
+        tt(A("MW", 640, U), IND(A("CT", 0, 64), A("VLU", 40, 164)), A("STC", 640, U), ADD)
         cp(A("OWU", 0, 14), A("LL", lb + CAP, lb + CAP + 14))
-        tt(A("MW", c0, c0 + CAP), IND(A("CT", 64, 104), A("OWU", 0, 14)), A("ND"), ALU.add)
-        tt(A("TG"), IND(A("CT", 104, 144), A("OWU", 0, 14)), A("ND"), ALU.add)
-        act(A("TGB"), A("TG"), ACT.Relu)
+        ts(sm(25), ev(1), -2.0, MUL)
+        tt(sm(26), ev(0), ev(6), SUB)
+        tt(A("MW", c0, c0 + CAP), IND(A("CT", 64, 104), A("OWU", 0, 14)), A("ND"), ADD)
+        tt(A("TG"), IND(A("CT", 104, 144), A("OWU", 0, 14)), A("ND"), ADD)
+        tt(sm(27), sm(25), sm(26), ADD)
+        tt(hd(s_new), hd(s_old), ev(6), ADD)
+        ts(A("TGB"), A("TG"), 0.0, MAX)
         wrap("P6", 14, "TGT", "TGB", CAP)
-        ab = 72 * (t + 1)
 
         def after():
             cp(A("TU", 16 * t, 16 * t + 14), A("P6", 0, 14))
-            ts(sm(25), ev(1), -2.0, ALU.mult)
-            tt(A("ST", s_new, s_new + 3, 2), A("ST", s_old, s_old + 3, 2), ev(6), ALU.add)
-            tt(sm(26), ev(0), ev(6), ALU.subtract)
-            ts(sm(28), A("AL", ab + 64, ab + 66), -1.0, ALU.mult)
-            tt(sm(27), sm(25), sm(26), ALU.add)
-            tt(A("LIM", 0, 2), sm(28), A("AL", ab + 64, ab + 66), ALU.max)
+            tt(hd(s_new + 1), hd(s_old + 1), sm(27), ADD)
             cp(IND(A("XS"), A("TU", 16 * t, 16 * t + 14)), A("LL", lb, lb + CAP))
-            tt(A("ST", s_new + 1, s_new + 4, 2), A("ST", s_old + 1, s_old + 4, 2), sm(27), ALU.add)
-            ts(A("LIM", 2, 4), A("LIM", 0, 2), -1.0, ALU.mult, 62.0, ALU.add)
             more()
 
         gathers(t + 1, after)
 
     def numbers(t):
-        ts(A("NUM"), io_(0, CAP), float(U + CAP * t), ALU.add)
+        ts(A("NUM"), io_(0, CAP), float(U + CAP * t), ADD)
         cp(IND(A("CS"), A("TU", 16 * t, 16 * t + 14)), A("NUM"))
 
     def final_lists(par):
         for b in range(4):
-            tr(A("FT", 32 * b, 32 * b + 32), A3b("FA", b))
+            tr(B("FT", b, 32), (T.FA[:, b, :], "FA", range(32 * b, 32 * b + 32)))
         for b in range(4):
-            cp(A("FU", 4 * par + b, 256, 8), A("FT", 32 * b, 32 * b + 32))
+            cp(A("FU", 4 * par + b, 256, 8), B("FT", b, 32))
 
-    def consts():
-        ts(col(11), col(0), 128.0, ALU.mult)
-        ts(col(12), col(0), 128.0, ALU.mult, 2048.0, ALU.add)
-        ts(col(13), col(1), -4096.0, ALU.add)
+    def spread():
+        ts(col(11), col(0), 128.0, MUL)
+        ts(col(12), col(0), 128.0, MUL, 2048.0, ADD)
+        ts(col(13), col(1), -4096.0, ADD)
         ts(col(14), col(1), 16.0, ALU.is_lt)
         ts(col(15), col(1), 16.0, ALU.is_ge)
         cp(col(20), A("PI", 0, 1))
         ms(A("ES"), 0.0)
         for t in range(3):
             ms(A("LS", 240 * t + CAP, 240 * t + 240), 0.0)
-        tt(col(16), col(20), col(1), ALU.subtract)
-        ts(A("KW"), io_(0, 16), 16.0, ALU.mult, col(0), ALU.add)
+        tt(col(16), col(20), col(1), SUB)
+        ts(A("KW"), io_(0, 16), 16.0, MUL, col(0), ADD)
         ms(A("ST", 0, 8, 2), 32.0)
         ms(A("ST", 1, 8, 2), 72.0)
-        ts(A("UOH"), io_(0, 128), col(16), ALU.subtract)
-        ts(A("WG", 5, 118, 16), g8, -1 / 256, ALU.mult)
-        ts(A("WG", 7, 120, 16), g8, 0.125, ALU.mult)
-        cp(A("WG", 9, 122, 16), g8)
-        cp(A("WK", 10, 123, 16), g8)
+        ts(A("UOH"), io_(0, 128), col(16), SUB)
+        ts(S("WG", 5), g8, -1 / 256, MUL)
+        ts(S("WG", 7), g8, 0.125, MUL)
+        cp(S("WG", 9), g8)
+        ts(A("K16"), io_(0, 16), 16.0, MUL)
+        for gm in range(2):
+            ts(B("OH", gm), A("UOH"), 1.0 - 16 * gm, ADD, 0.0, MAX)
+            ts(B("CB", gm), A("UOH"), 16.0 * gm + 16, ALU.is_lt)
+        cp(S("WK", 10), g8)
         for par in range(2):
             for h in range(2):
-                ts(A("CWB", 4 * par + h, 4 * par + 4, 2), A("ONE", 0, 2), col(11 + h), ALU.mult)
-        ts(A("CWB", 0, 4), A("CWB", 0, 4), 2.0, ALU.mult)
-        ts(A("CWB", 4, 8), A("CWB", 4, 8), 2.0, ALU.mult, 128.0, ALU.add)
-
-    def spread():
+                ts(A("CWB", 4 * par + h, 4 * par + 4, 2), A("ONE", 0, 2), col(11 + h), MUL)
+        tt(A("CR"), A("OH"), A("CB"), MUL)
+        ts(A("CWB", 0, 4), A("CWB", 0, 4), 2.0, MUL)
+        ts(A("CWB", 4, 8), A("CWB", 4, 8), 2.0, MUL, 128.0, ADD)
         ms(A("XS", ZADDR, XSW), 0.0)
         for i in range(41):
             cp(A("XS", 32 + i, 8192, 128), A("XG", i, U, 41))
+        ts(A("CB"), A("CR"), 0.0, ALU.is_gt)
 
-    def idle0():
-        last_weights()
-        act(A("WC1", 4, 117, 16), A("WC1", 3, 116, 16), ACT.Copy, None, -1.0)
-        act(A("WC1", 14, 127, 16), A("WC1", 7, 120, 16), ACT.Copy, None, -1.0)
-        act(A("WC2", 4, 117, 16), A("WC2", 3, 116, 16), ACT.Copy, None, -1.0)
-        act(A("WC3", 7, 120, 16), A("WC2", 7, 120, 16))
-        act(A("WC3", 14, 127, 16), A("WC2", 14, 127, 16))
+    def fill0():
+        ms(col(24), -62.0)
+        tt(col(25), A("E16", 9, 10), A("E16", 10, 11), ADD)
         ms(A("RW", 37, 38), 600.0)
         ms(A("RW", 41, 43), -1e5)
         ms(A("OWN"), 0.0)
-        ts(A("VLU"), A("P4", 0, 164), 32.0, ALU.add)
-        tt(A("RW", 32, 48), A("RW", 32, 48), A("E16"), ALU.mult)
+        ts(col(21), A("E16", 13, 14), 64.0, MUL)
+        ts(col(22), A("E16", 6, 7), -1000.0, MUL)
+
+    def idle0():
+        rest_weights()
+        act(S("WC1", 4), S("WC1", 3), ACT.Copy, None, -1.0)
+        act(S("WC1", 8), S("WC1", 7))
+        act(S("WC2", 8), S("WC2", 7))
+        act(S("WC2", 10), S("WC2", 9))
+        act(S("WB", 8), g8)
+        act(S("WB", 15), g8)
+        act(S("WDN", 1), g8)
+        act(S("WC2", 4), S("WC2", 3), ACT.Copy, None, -1.0)
+        act(S("WC3", 7), S("WC2", 7))
+        act(S("WC3", 14), S("WC2", 14))
+        tt(A("RW", 32, 48), A("RW", 32, 48), A("E16"), MUL)
+        ts(A("VLU"), A("P4", 0, 164), 32.0, ADD)
         ms(A("OWN", 10, 27, 16), 1.0)
-        ts(A("OWN", 11, 28, 16), A("ONE", 0, 2), col(1), ALU.mult)
-        red(col(4), A("RW", 32, 48), ALU.add)
-        ts(col(21), A("E16", 13, 14), 64.0, ALU.mult)
-        ts(col(22), A("E16", 6, 7), -1000.0, ALU.mult)
-        ts(A("KT"), io_(0, CAP), col(2), ALU.mult)
-        tt(col(17), col(21), col(22), ALU.add)
+        ts(A("OWN", 11, 28, 16), A("ONE", 0, 2), col(1), MUL)
+        red(col(4), A("RW", 32, 48), ADD)
+        ts(col(23), col(25), -256.0, MUL, col(2), ADD)
+        tt(col(17), col(21), col(22), ADD)
         own_vars(state(0, 0), 0)
-        ts(A("CT", 96, 104), io_(0, 8), 0.0, ALU.mult, col(4), ALU.add)
-        ts(A("CT", 136, 144), io_(0, 8), 0.0, ALU.mult, col(17), ALU.add)
+        act(A("KT"), io_(0, CAP), ACT.Copy, None, col(23))
+        act(A("CT", 96, 104), io_(0, 8), ACT.Identity, col(4), 0.0)
+        act(A("CT", 136, 144), io_(0, 8), ACT.Identity, col(17), 0.0)
         act(A("MW", U + CAP, W), A("X", U + CAP, W), ACT.Identity, col(4))
+
+    def shape(s, k, par):
+        tt(sm(k), hd(s + 1), hd(s), SUB)
+        ts(sm(k + 5), hd(s), col(18 + par), ADD)
+        ts(sm(k + 1), sm(k), 0.0, ALU.is_gt, 2.0, MUL)
+        ts(sm(k + 2), sm(k + 1), -1.0, ADD)
+        tt(sm(k + 3), sm(k), sm(k + 2), MUL)
+        ts(sm(k + 4), sm(k + 3), 1.0, ADD)
+
+    def fill1():
+        ms(A("CS", ZADDR, XSW), -1.0)
+        ts(A("CS", PARTS, PARTS + CAP), io_(0, CAP), float(U + 2 * CAP), ADD)
 
     def idle1():
         own_vars(state(1, 1), 1)
-        ts(A("MW", U, U + CAP), A("X", W - CAP, W), col(4), ALU.add)
-        ms(A("CS", ZADDR, XSW), -1.0)
-        ts(A("CS", PARTS, PARTS + CAP), io_(0, CAP), float(U + 2 * CAP), ALU.add)
-        numbers(0)
+        ts(A("MW", U, U + CAP), A("X", W - CAP, W), col(4), ADD)
         act(A("OCR", 0, 2048), IND(A("YO", 0, U), A("OCU", 0, 128)))
+        numbers(0)
         cp(A("OCR", 2048, U), IND(A("YO", 0, U), A("OCU", 128, 164)))
         for i in range(41):
             sel(A("CS", 32 + i, 8192, 128), A("OCR", i, U, 41), [[0, 64]], ALU.is_ge, 0.0, 0, 0)
 
-    def shape(s, k, par):
-        tt(sm(k), A("ST", s + 1, s + 4, 2), A("ST", s, s + 3, 2), ALU.subtract)
-        ts(sm(k + 5), A("ST", s, s + 3, 2), col(18 + par), ALU.add)
-        ts(sm(k + 1), sm(k), 0.0, ALU.is_gt, 2.0, ALU.mult)
-        ts(sm(k + 2), sm(k + 1), -1.0, ALU.add)
-        tt(sm(k + 3), sm(k), sm(k + 2), ALU.mult)
-        ts(sm(k + 4), sm(k + 3), 1.0, ALU.add)
-
     def even_own():
-        ts(col(18), col(1), 256.0, ALU.mult)
-        ts(col(19), col(1), 256.0, ALU.mult, 128.0, ALU.add)
+        ts(col(18), col(1), 256.0, MUL)
+        ts(col(19), col(1), 256.0, MUL, 128.0, ADD)
         shape(state(0, 2), 36, 0)
+        ts(sm(28), sm(40), -float(PARTS), ADD)
         for gm in range(2):
-            ts(A3("FP", 16 * gm, 16 * gm + 16), A3("I3", 0, 16), sm1(40, gm), ALU.is_lt, -16384.0, ALU.mult)
+            ts(H("FP", gm), H("I3", 0), sm1(40, gm), ALU.is_lt, -16384.0, MUL)
         for gm in range(2):
-            tt(A3("FP", 16 * gm, 16 * gm + 16), A3("FP", 16 * gm, 16 * gm + 16), A3("I3", 0, 16), ALU.add)
+            tt(H("FP", gm), H("FP", gm), H("I3", 0), ADD)
         numbers(1)
 
     def odd_final():
         shape(state(1, 0), 30, 1)
         for gm in range(2):
-            ts(A3("FB", 16 * gm, 16 * gm + 16), A3("I3", 0, 16), sm1(32, gm), ALU.mult, sm1(35, gm), ALU.add)
-            ts(A3("FC", 16 * gm, 16 * gm + 16), A3("I3", 0, 16), sm1(34, gm), ALU.is_ge, float(ZADDR), ALU.mult)
-        tt(A3("FA", 0, 32), A3("FB", 0, 32), A3("FC", 0, 32), ALU.max)
+            ts(H("FB", gm), H("I3", 0), sm1(32, gm), MUL, sm1(35, gm), ADD)
+            ts(H("FC", gm), H("I3", 0), sm1(34, gm), ALU.is_ge, float(ZADDR), MUL)
+        tt(A3("FA", 0, 32), A3("FB", 0, 32), A3("FC", 0, 32), MAX)
         final_lists(1)
 
     setup()
     later_weights()
-    scalar_feats(0, {})
-    tt(A("STC", 0, U), IND(A("DS"), A("SLU")), A("SC"), ALU.add)
-    consts()
-    wrap("P4", 164, "VLT", "SC", U)
+    scalar_feats(0, {9: lambda: wrap("P4", 164, "VLT", "SC", U)})
+    tt(A("STC", 0, U), IND(A("DS"), A("SLU")), A("SC"), ADD)
     gathers(0, spread)
-    choose(0, state(1, 0), state(1, 1), idle0)
+    choose(0, state(1, 0), state(1, 1), idle0, fill0)
     arrive(0, state(0, 0), state(0, 1), lambda: None)
-    choose(1, state(0, 1), state(0, 2), idle1)
+    choose(1, state(0, 1), state(0, 2), idle1, fill1)
     arrive(1, state(1, 1), state(1, 2), even_own)
     choose(2, state(1, 2), state(1, 0), odd_final)
 
     def ev2(i):
         return A("EL", 64 + i, 64 + i + 17, 16)
 
-    tt(sm(0), ev2(3), sm(36), ALU.mult)
-    ts(sm(1), ev2(3), -2.0, ALU.mult, 1.0, ALU.add)
-    tt(sm(2), ev2(4), sm(40), ALU.subtract)
-    tt(sm(3), ev2(0), sm(40), ALU.add)
-    tt(sm(4), sm(0), sm(41), ALU.add)
-    tt(sm(5), sm(1), sm(38), ALU.mult)
+    tt(sm(2), ev2(4), sm(28), SUB)
+    tt(sm(0), ev2(3), sm(36), MUL)
+    ts(sm(1), ev2(3), -2.0, MUL, 1.0, ADD)
+    tt(sm(3), ev2(0), sm(40), ADD)
+    tt(sm(4), sm(0), sm(41), ADD)
+    tt(sm(5), sm(1), sm(38), MUL)
     for gm in range(2):
-        ts(A3("FP", 16 * gm, 16 * gm + 16), A3("FP", 16 * gm, 16 * gm + 16), sm1(2, gm), ALU.add, float(PARTS), ALU.add)
-        ts(A3("FC", 16 * gm, 16 * gm + 16), A3("I3", 0, 16), sm1(3, gm), ALU.is_ge, float(ZADDR), ALU.mult)
-        ts(A3("FB", 16 * gm, 16 * gm + 16), A3("I3", 0, 16), sm1(5, gm), ALU.mult, sm1(4, gm), ALU.add)
-    tt(A3("FC", 0, 32), A3("FC", 0, 32), A3("FP", 0, 32), ALU.max)
-    tt(A3("FA", 0, 32), A3("FB", 0, 32), A3("FC", 0, 32), ALU.max)
+        act(H("FP", gm), H("FP", gm), ACT.Identity, sm1(2, gm))
+        ts(H("FC", gm), H("I3", 0), sm1(3, gm), ALU.is_ge, float(ZADDR), MUL)
+    for gm in range(2):
+        ts(H("FB", gm), H("I3", 0), sm1(5, gm), MUL, sm1(4, gm), ADD)
+    tt(A3("FC", 0, 32), A3("FC", 0, 32), A3("FP", 0, 32), MAX)
+    tt(A3("FA", 0, 32), A3("FB", 0, 32), A3("FC", 0, 32), MAX)
     final_lists(0)
-    cp(A("XS", PARTS, PARTS + CAP), A("LL", 480, 480 + CAP))
+    act(A("XS", PARTS, PARTS + CAP), A("LL", 480, 480 + CAP))
     nout = [0]
 
     def store(dst, src):
@@ -737,12 +764,12 @@ def rank_program(g, core, T, topo):
         g.sync.dma_start(dst, src[0]).then_inc(T.sem.out0, 16)
 
     for c in range(8):
-        o = A("FD", 512 * c, 512 * c + 512)
-        (cp if c % 2 else act)(o, IND(A("XS"), A("FU", 32 * c, 32 * c + 32)))
-        store(T.y[:, 512 * c:512 * c + 512], o)
+        (cp if c % 2 else act)(B("FD", c, 512), IND(A("XS"), B("FU", c, 32)))
+        store(T.y[:, 512 * c:512 * c + 512], B("FD", c, 512))
     for c in range(4):
-        (cp if c % 2 else act)(A("YO", 1024 * c, 1024 * c + 1024), IND(A("CS"), A("FU", 64 * c, 64 * c + 64)))
-    store(T.yo[:, :], (T.YO[0:128:16, :], "YO", range(W)))
+        lo, hi = 1024 * c, 1024 * c + 1024
+        (cp if c % 2 else act)(A("YO", lo, hi), IND(A("CS"), B("FU", c, 64)))
+        store(T.yo[:, lo:hi], (T.YO[0:128:16, lo:hi], "YO", range(lo, hi)))
     g.sync.wait_ge(T.sem.out0, nout[0])
     g.wait_ge(T.sem.loc, sent[0])
     for k in ("v", "s", "t", "g"):

@@ -3,31 +3,144 @@ from concourse.mybir import AluOpType, AxisListType, ActivationFunctionType
 ALU = AluOpType
 ACT = ActivationFunctionType
 U, CAP, W = 2624, 224, 4096
-PARTS, ZADDR, XSW = 8448, 8768, 8784
+PARTS, ZADDR, XSW = 8576, 8896, 8912
 MAGIC = 3221225472.0
-NS, NS1, NV = (18, 10, 12), (14, 8, 8), (5, 7, 7)
+CYC, GAT, SCA, HOP, FAR = 0.00083, 1.4, 3.0, 0.12, 1.9
+TRIES, SHAKE, SPARE, TEMP = 1200, 2.0, 0.1, 0.2
 BF, F32, I32, U16 = "bfloat16", "float32", "int32", "uint16"
 SCRATCH = {}
 for _d, _l in (
-        (BF, dict(X=W, XG=U + 8, AD=U + 8, DS=U, SRC=U, SC=U, MW=W, MG=W + 144, FD=W, DI=U, XS=XSW, IDW=160, NEGI=128, EIG=128,
-                  BLK=128, WZ=128, FS=144, FV=144, MAS=144, MAV=144, MB=144, SLT=144, VLT=144, TGT=144, WB=128, WDN=128, LD=32,
-                  CB=256, CR=256, K16=16, WDL=128, WDR=128, WDZ=128, TRI=128, UOH=128, WQ=128, WG=128, WK=128, WR=256, WRG=256,
-                  WC1=128, WC2=128, WC3=128, E16=16, IOT=256, B82=256, NKK=256, ONE=128, KT=CAP, KW=16, CWB=8, NJ=64, AS=216,
-                  AL=216, ES=96, EL=96, LS=720, LL=720, XH=64, MBS=32, GD=64, WS=2, CMP=320, SP=1024 + CAP, OH=256, DD=4, ST=24,
-                  SMK=8, OWN=32, OWR=32, ER=32, TGB=CAP)),
-        (F32, dict(CDF=256, STC=W, CS=XSW, YO=W, OCR=U, BT=32, COL=32, RW=48, LIM=4, RR=256, KEY=256, SM=96, TQ=32, DF=64,
-                   SPT=64, SPR=64, EW=4, CT=144, ND=CAP, TG=CAP, NUM=CAP, FT=128)),
-        (I32, dict(OCI=164, CDI=256, MI=256, MJ=256, PI=4, CI=32)),
-        (U16, dict(OCU=164, SLU=164, VLU=164, MU=256, OFF=4, CU=16, SPU=64, EU=4, OWU=16, TU=32, FU=256))):
+        (BF, dict(X=W, XG=U + 8, AD=U + 8, MW=W, MG=W + 144, FD=W, XS=XSW, IDW=160, NEGI=128, I256=128, INEG=128,
+                  BLK=128, WZ=128, WA=512, WB=512, WC=464, HALF=128, N256=128, N1K=128, SELW=64, B32=128, TGT=144, G=768,
+                  RH=256, ZR=896, CQ=128, CB=256, CR=256, K16=16, TRI=128, TRN=128, TRS=128, UOH=128, WR=256, WRG=256,
+                  E16=16, IOT=256, NKK=128, ONE=128, KT=CAP, KW=16, CWB=4, NJ=72, AS=216, AL=216, ES=96, EL=96, LS=720,
+                  LL=720, XH=64, MBS=32, GD=64, WS=2, CMP=320, SP=1024 + CAP, OH=256, OW=512, ST=24, SMK=8, OWN=32,
+                  OWR=32, ER=64, TGB=CAP, B1=32, B2=32, SCL=32, CC=32, PRE=32)),
+        (F32, dict(STC=W, CS=XSW, YO=W, NO=U, OCR=U, SRC=U // 2, DS=U, B82=176, COL=40, RW=32, SM=120, TQ=64, DF=80,
+                   SPT=64, SPR=64, EW=4, EB=4, CT=104, ND=CAP, NUM=2 * CAP, FT=256, IDF=128, VLT=144)),
+        (I32, dict(OCI=164, CDI=256, MI=256, MJ=256, PI=4)),
+        (U16, dict(OCU=164, VLU=164, MU=256, OFF=4, CU=16, SPU=64, EU=4, OWU=16, TU=32, FU=256))):
     for _k in _l:
         SCRATCH[_k] = ("sbuf", [128, _l[_k]], _d)
 SCRATCH["I3"] = ("sbuf", [128, 4, 16], F32)
-for _k in ("FA", "FB", "FC", "FP"):
-    SCRATCH[_k] = ("sbuf", [128, 4, 32], F32)
+SCRATCH["FA"] = ("sbuf", [128, 28, 32], F32)
 for _k in range(8):
     SCRATCH["P%d" % _k] = ("psum", [128, 512], F32)
-SEMAPHORES = ["qv", "qs", "qt", "qg", "ld0", "ld1", "ld2", "ld3", "ld4", "ld5", "ld6", "loc", "loc0", "a0", "a1", "a2",
-              "e0", "e1", "e2", "l0", "l1", "l2", "out0"]
+PART = dict(WDL=("WA", 0, 128, 4), WDR=("WA", 128, 128, 4), WDZ=("WA", 256, 128, 4), WDN=("WA", 384, 128, 4),
+            WQ1=("WB", 0, 128, 6), WQ2=("WB", 128, 128, 6), WC1=("WB", 256, 128, 6), WC2=("WB", 384, 128, 6),
+            WG1=("WC", 0, 128, 5), WG2=("WC", 128, 128, 5), WK=("WC", 256, 128, 5), WM=("WC", 384, 48, 5),
+            WF=("WC", 432, 32, 5))
+SEMAPHORES = ["qv", "qs", "qt", "qg", "ld0", "ld1", "ld2", "ld3", "ld4", "ld6", "loc", "loc0", "a0", "a1", "a2",
+              "e0", "e1", "e2", "l0", "l1", "l2", "out0", "fill"]
+ORDER = []
+
+
+def bits(cols, wide):
+    if wide:
+        cols = range(cols[0] // 8 * 8, cols[-1] // 8 * 8 + 8)
+    if isinstance(cols, range) and cols.step == 1:
+        return ((1 << len(cols)) - 1) << cols[0]
+    return sum(1 << c for c in cols)
+
+
+def touched(c):
+    items = []
+    for lst, w in ((c["r"], False), (c["w"], True)):
+        for a in lst:
+            psum = SCRATCH[a[1]][0] == "psum"
+            items.append((a[1], 1 if psum else bits(a[2], c["dma"]), w, psum))
+            if len(a) > 3:
+                items.append((a[3][1], bits(a[3][2], False), False, False))
+    return items
+
+
+def schedule(calls, lanes):
+    n = len(calls)
+    pred, acc = [set() for _ in calls], {}
+    for i, c in enumerate(calls):
+        items = touched(c) + [(a[1], bits(a[2], True), True, False) for a in c["far"]]
+        for name, m, w, psum in items:
+            for e in acc.get(name, []):
+                o = calls[e[2]]
+                if e[0] & m and (w or e[1] or (psum and (o["q"] != c["q"] or c["alt"] or o["alt"]))) \
+                        and not (c["any"] and o["any"] == c["any"]):
+                    pred[i].add(e[2])
+        for name, m, w, psum in items:
+            lst = acc.setdefault(name, [])
+            if w and not c["any"]:
+                lst[:] = [e for e in lst if e[0] & ~m]
+            lst.append((m, w, i))
+        pred[i] |= set(c["after"])
+        pred[i].discard(i)
+
+    def gap(a, b):
+        return calls[a]["late"] + (0.0 if calls[a]["q"] == "t" == calls[b]["q"] else HOP)
+
+    cost, queue = [c["cost"] for c in calls], [c["q"] for c in calls]
+    before = [[(p, gap(p, i)) for p in pred[i]] for i in range(n)]
+    after = [[] for _ in calls]
+    for i in range(n):
+        for p, d in before[i]:
+            after[p].append((i, d))
+
+    def place(turn, deps, lead, choose=False):
+        start, busy = [0.0] * n, {q: ([], []) for q in "vstgy"}
+        for i in turn:
+            t0, found = max([start[p] + cost[p] + d for p, d in deps[i]] + [lead[i]]), None
+            for q, c in (calls[i]["alt"] if choose and calls[i]["alt"] else ((queue[i], cost[i]),)):
+                t, (begins, ends) = t0, busy[q]
+                lo, hi = 0, len(ends)
+                while lo < hi:
+                    mid = (lo + hi) // 2
+                    lo, hi = (mid + 1, hi) if ends[mid] <= t else (lo, mid)
+                while lo < len(ends) and begins[lo] < t + c - 1e-9:
+                    t = max(t, ends[lo])
+                    lo += 1
+                end = t + c + (SPARE if q == "v" else 0)
+                if found is None or end < found[0]:
+                    found = (end, t, q, c, lo)
+            _, t, queue[i], cost[i], lo = found
+            busy[queue[i]][0].insert(lo, t)
+            busy[queue[i]][1].insert(lo, t + cost[i])
+            start[i] = t
+        return start
+
+    late, zero, prio = [c["late"] for c in calls], [0.0] * n, [0.0] * n
+    nxt = {a: b for lane in lanes for a, b in zip(lane, lane[1:])}
+    for _ in range(3):
+        for i in range(n - 1, -1, -1):
+            prio[i] = cost[i] + max([d + prio[s] for s, d in after[i]] + [late[i], prio[nxt[i]] if i in nxt else 0])
+
+    def in_turn(key):
+        key = list(key)
+        for i in range(n):
+            for p, _ in before[i]:
+                if key[p] >= key[i]:
+                    key[i] = key[p] + 1e-6
+        return sorted(range(n), key=lambda i: key[i])
+
+    seed = [12345]
+
+    def rand():
+        seed[0] = (seed[0] * 1103515245 + 12345) % 2147483648
+        return seed[0] / 2147483648
+
+    def polish(start):
+        back = place(sorted(range(n), key=lambda i: -start[i] - cost[i]), after, late)
+        start = place(sorted(range(n), key=lambda i: -back[i] - cost[i]), before, zero, True)
+        return max(start[i] + cost[i] + late[i] for i in range(n)), start, list(queue), list(cost)
+
+    best = now = polish(place(in_turn([-x for x in prio]), before, zero))
+    for k in range(TRIES):
+        queue[:], cost[:] = now[2], now[3]
+        t0, width, size = rand() * now[0], 2 + 6 * rand(), SHAKE * rand()
+        key = [s + (size * (rand() - 0.5) if t0 - width < s < t0 else 0) for s in now[1]]
+        new = polish(place(in_turn(key), before, zero, True))
+        if new[0] < now[0] + TEMP * rand() * (1 - k / TRIES):
+            now = new
+        if new[0] < best[0]:
+            best = new
+    return [(i, best[2][i]) for i in sorted(range(n), key=lambda i: best[1][i])]
 
 
 def rank_program(g, core, T, topo):
@@ -36,23 +149,24 @@ def rank_program(g, core, T, topo):
         return
     n_ranks = len(T.cores)
     eng = {"v": g.vector, "s": g.scalar, "t": g.tensor, "g": g, "y": g.sync}
-    cnt = {"v": 0, "s": 0, "t": 0, "g": 0}
-    seen = {k: {} for k in eng}
-    acc = {}
+    calls, lanes = [], []
     sent = [0]
 
     def A(name, c0=0, c1=None, st=1, p0=0, p1=128):
+        if name in PART:
+            name, base, n = PART[name][:3]
+            c0, c1 = base + c0, base + (n if c1 is None else c1)
         if c1 is None:
             c1 = SCRATCH[name][1][1]
         ap = T[name][p0:p1, c0:c1] if st == 1 else T[name][p0:p1, c0:c1:st]
         return (ap, name, range(c0, c1, st))
 
-    def A3(name, c0, c1):
+    def A3(name, c0, c1, b0, b1):
         n = SCRATCH[name][1][2]
-        return (T[name][:, :, c0:c1], name, [n * b + c for b in range(4) for c in range(c0, c1)])
+        return (T[name][:, b0:b1, c0:c1], name, [n * b + c for b in range(b0, b1) for c in range(c0, c1)])
 
-    def H(name, gm):
-        return A3(name, 16 * gm, 16 * gm + 16)
+    def F(k, gm=None):
+        return A3("FA", 0, 32, 4 * k, 4 * k + 4) if gm is None else A3("FA", 16 * gm, 16 * gm + 16, 4 * k, 4 * k + 4)
 
     def B(name, k, n=128):
         return A(name, n * k, n * k + n)
@@ -60,120 +174,126 @@ def rank_program(g, core, T, topo):
     def S(name, c):
         return A(name, c, c + 113, 16)
 
+    def R(name, c0=0, c1=None, st=1):
+        return A(name, c0, c1, st, 0, 1)
+
     def IND(win, off):
         return (win[0].indirect(off[0]), win[1], win[2], off)
 
-    def wait(q, sem, val):
-        if seen[q].get(sem, 0) < val:
-            eng[q].wait_ge(T.sem[sem], val)
-            seen[q][sem] = val
+    def note(q, fn, reads, writes, cost, sem=None, val=0, late=0.0, any_order=None, far=(), after=(), alt=None):
+        calls.append(dict(q=q, fn=fn, r=[a for a in reads if isinstance(a, tuple)], w=writes, cost=cost, sem=sem, val=val,
+                          dma=sem is not None, late=late, any=any_order, far=far, after=after, alt=alt, n=1))
+        return len(calls) - 1
 
-    def bits(cols, wide):
-        if wide:
-            cols = range(cols[0] // 8 * 8, cols[-1] // 8 * 8 + 8)
-        if isinstance(cols, range) and cols.step == 1:
-            return ((1 << len(cols)) - 1) << cols[0]
-        return sum(1 << c for c in cols)
+    def price(reads, o, rate=None):
+        aps = [a for a in reads if isinstance(a, tuple)] + [o]
+        ind = [a for a in aps if len(a) > 3]
+        if ind:
+            return (0.065 if rate else 0.05) + 16 * len(ind[0][3][2]) * (SCA if ind[0] is o else GAT) * CYC
+        if rate is None:
+            rate = 0.5 if all(SCRATCH[a[1]][2] in (BF, U16) or len(a[2]) == 1 for a in aps) else 1
+        return 0.03 + max(64, len(reads[0][2] if reads else o[2]) * rate) * CYC
 
-    def sync(q, reads, writes, sem, val):
-        dma = sem[0] != "q"
-        items = []
-        for lst, w in ((reads, False), (writes, True)):
-            for a in lst:
-                psum = SCRATCH[a[1]][0] == "psum"
-                items.append((a[1], 1 if psum else bits(a[2], dma), w, psum))
-                if len(a) > 3:
-                    items.append((a[3][1], bits(a[3][2], False), False, False))
-        need = {}
-        for name, m, w, psum in items:
-            for e in acc.get(name, []):
-                if e[0] & m and (w or e[1] or (psum and e[4] != q)) and not (q == "t" and e[4] == "t"):
-                    need[e[2]] = max(need.get(e[2], 0), e[3])
-        for s in need:
-            wait(q, s, need[s])
-        for name, m, w, psum in items:
-            lst = acc.setdefault(name, [])
-            lst[:] = [e for e in lst if not ((w or (e[4] == q and not e[1] and not dma)) and e[0] & ~m == 0)]
-            lst.append([m, w, sem, val, q])
+    def op(q, fn, reads, o, rate=None):
+        note(q, fn, reads, [o], price(reads, o, rate))
 
-    def op(q, fn, reads, writes):
-        cnt[q] += 1
-        sync(q, [a for a in reads if isinstance(a, tuple)], writes, "q" + q, cnt[q])
-        fn().then_inc(T.sem["q" + q], 1)
+    def either(fs, fv, reads, o):
+        k = len(calls)
+        cs, cv = price(reads, o, 1), price(reads, o)
+        note("s", lambda: fs() if calls[k]["q"] == "s" else fv(), reads, [o], cs, alt=(("s", cs), ("v", cv)))
+        return calls[k]
 
     def ap(x):
         return x[0] if isinstance(x, tuple) else x
 
     def ts(o, i, s1, o0, s2=None, o1=None):
         if o1 is None:
-            op("v", lambda: g.vector.tensor_scalar(o[0], i[0], ap(s1), None, o0), [i, s1], [o])
+            op("v", lambda: g.vector.tensor_scalar(o[0], i[0], ap(s1), None, o0), [i, s1], o)
         else:
-            op("v", lambda: g.vector.tensor_scalar(o[0], i[0], ap(s1), ap(s2), o0, o1), [i, s1, s2], [o])
+            op("v", lambda: g.vector.tensor_scalar(o[0], i[0], ap(s1), ap(s2), o0, o1), [i, s1, s2], o)
 
     def tt(o, a, b, o0):
-        op("v", lambda: g.vector.tensor_tensor(o[0], a[0], b[0], o0), [a, b], [o])
+        op("v", lambda: g.vector.tensor_tensor(o[0], a[0], b[0], o0), [a, b], o,
+           2 if SCRATCH[a[1]][0] == SCRATCH[b[1]][0] else 1)
 
     def cp(o, i):
-        op("v", lambda: g.vector.tensor_copy(o[0], i[0]), [i], [o])
+        op("v", lambda: g.vector.tensor_copy(o[0], i[0]), [i], o)
 
     def ms(o, c):
-        op("v", lambda: g.vector.memset(o[0], c), [], [o])
+        op("v", lambda: g.vector.memset(o[0], c), [], o)
 
     def red(o, i, o0, ab=False):
-        op("v", lambda: g.vector.tensor_reduce(o[0], i[0], AxisListType.X, o0, apply_absolute_value=ab), [i], [o])
+        op("v", lambda: g.vector.tensor_reduce(o[0], i[0], AxisListType.X, o0, apply_absolute_value=ab), [i], o, 1)
 
     def tr(o, i):
-        op("v", lambda: g.vector.transpose(o[0], i[0]), [i], [o])
+        op("v", lambda: g.vector.transpose(o[0], i[0]), [i], o)
 
-    def act(o, i, f=ACT.Copy, bias=None, scale=1.0):
+    def act(o, i, f, bias=None, scale=1.0):
         if bias is None:
-            op("s", lambda: g.scalar.activation(o[0], i[0], f, scale=ap(scale)), [i, scale], [o])
+            op("s", lambda: g.scalar.activation(o[0], i[0], f, scale=ap(scale)), [i, scale], o, 1)
         else:
-            op("s", lambda: g.scalar.activation(o[0], i[0], f, bias=ap(bias), scale=ap(scale)), [i, bias, scale], [o])
+            op("s", lambda: g.scalar.activation(o[0], i[0], f, bias=ap(bias), scale=ap(scale)), [i, bias, scale], o, 1)
 
-    def mm(o, l, r, start, stop):
-        op("t", lambda: g.tensor.matmul(o[0], l[0], r[0], start, stop), [l, r], [o])
+    def lin(o, i, bias, scale=1.0):
+        either(lambda: g.scalar.activation(o[0], i[0], ACT.Identity, bias=ap(bias), scale=ap(scale)),
+               lambda: g.vector.tensor_scalar(o[0], i[0], ap(scale), ap(bias), ALU.mult, ALU.add), [i, bias, scale], o)
+
+    def mul(o, i, scale):
+        either(lambda: g.scalar.activation(o[0], i[0], ACT.Copy, scale=ap(scale)),
+               lambda: g.vector.tensor_scalar(o[0], i[0], ap(scale), None, ALU.mult), [i, scale], o)
+
+    def mov(o, i):
+        either(lambda: g.scalar.activation(o[0], i[0], ACT.Copy), lambda: g.vector.tensor_copy(o[0], i[0]), [i], o)
+
+    def relu(o, i, bias=0.0):
+        either(lambda: g.scalar.activation(o[0], i[0], ACT.Relu, bias=ap(bias)),
+               lambda: g.vector.tensor_scalar(o[0], i[0], ap(bias), 0.0, ALU.add, ALU.max), [i, bias], o)
+
+    def mm(o, l, r, start, stop, group=None, part=None):
+        def fn():
+            if group:
+                group[0] -= 1
+            return g.tensor.matmul(o[0], l[0], (part() if part else r)[0], start, group[0] == 0 if group else stop)
+        cost = max(min(64, len(l[2])), len(r[2])) * (4 if SCRATCH[l[1]][2] == F32 else 1) * CYC / 2
+        note("t", fn, [l, r], [o], cost, any_order=group and group[1])
 
     def iota(o, pat, base, cm, small=True):
-        if small:
-            op("g", lambda: g.iota(o[0], pat, base, cm, allow_small_or_imprecise_dtypes=True), [], [o])
-        else:
-            op("g", lambda: g.iota(o[0], pat, base, cm), [], [o])
+        note("g", lambda: g.iota(o[0], pat, base, cm, allow_small_or_imprecise_dtypes=True) if small else
+             g.iota(o[0], pat, base, cm), [], [o], 0.13 + 2 * len(o[2]) * CYC)
 
     def sel(o, i, pat, cmp, fill, base, cm):
-        op("g", lambda: g.affine_select(o[0], i[0], pat, cmp, float(fill), base, cm), [i], [o])
+        note("g", lambda: g.affine_select(o[0], i[0], pat, cmp, float(fill), base, cm), [i], [o], 0.17 + 2 * len(o[2]) * CYC)
 
-    def ents(table):
-        for k in range(max(len(v) for v in table.values())):
-            for key in table:
-                if k < len(table[key]):
-                    v = S(key[0], key[1])
-                    sel(v, v, [[-16, 8]], ALU.not_equal, table[key][k][1], -table[key][k][0], 1)
+    def gfill(o, v=0):
+        iota(o, [[0, len(o[2])]], v, 0)
 
     def wrap(pb, n, name, src, width):
         for r in range(16):
             mm(A(pb, 0, n), A(name, 16 - r, 144 - r), A(src, r, width, 16), r == 0, r == 15)
 
-    def load(q, o, src, sem):
-        sync(q, [], [o], sem, 16)
-        eng[q].dma_start(o[0], src).then_inc(T.sem[sem], 16)
+    def load(q, o, src, sem, late):
+        note(q, lambda: eng[q].dma_start(o[0], src).then_inc(T.sem[sem], 16), [], [o], 0.05, sem, 16, late)
 
-    def send(src, dst_name, c0, c1, sem, to_rank, loc="loc"):
-        dst = T.cores[to_rank % n_ranks]
-        es = topo.engines(core, dst)[:8]
-        rid, pid, _ = topo.addr(dst)
-        sync("g", [src], [], loc, 10 ** 6)
-        g.remote_dma(T[dst_name][:, c0:c1], src[0], T.sem[sem], T.sem[loc], pid, rid, sum(1 << e for e in es))
+    def engines(src, dst):
+        return topo.engines(src, dst)[:8]
+
+    def send(src, dst, sem, to_rank, loc="loc", first=0.0):
+        to = T.cores[to_rank % n_ranks]
+        es = engines(core, to)
+        rid, pid, _ = topo.addr(to)
         if loc == "loc":
             sent[0] += len(es)
-        return len(es)
+        return note("g", lambda: g.remote_dma(dst[0], src[0], T.sem[sem], T.sem[loc], pid, rid, sum(1 << e for e in es)),
+                    [src], [], 0.5 + first, loc, 10 ** 6, FAR - 0.5, far=[dst])
 
-    def expect(name, c0, c1, sem, from_rank):
-        n = len(topo.engines(T.cores[from_rank % n_ranks], core)[:8])
-        acc.setdefault(name, []).append([bits(range(c0, c1), True), True, sem, n, "r"])
+    def chain(first, qn):
+        lanes.append([k for k in range(first, len(calls)) if calls[k]["q"] == qn])
 
     def col(i):
         return A("COL", i, i + 1)
+
+    def e16(i):
+        return A("E16", i, i + 1)
 
     def sm(i):
         return A("SM", 2 * i, 2 * i + 2)
@@ -187,589 +307,592 @@ def rank_program(g, core, T, topo):
     ADD, SUB, MUL, MAX, MIN = ALU.add, ALU.subtract, ALU.mult, ALU.max, ALU.min
     ident = A("IDW", 16, 144)
     g8 = S("BLK", 0)
-    one_row = A("ONE", 0, 128, 1, 0, 1)
-    for t in range(3):
-        expect("AL", 72 * t, 72 * t + 72, "a%d" % t, rank - 1 - t)
-        expect("EL", 32 * t, 32 * t + 32, "e%d" % t, rank + 1 + t)
-        expect("LL", 240 * t, 240 * t + 240, "l%d" % t, rank + 1 + t)
+    one_row = R("ONE")
+    i3 = A3("I3", 0, 16, 0, 4)
 
-    load("y", A("OCI"), T.oc[:, :], "ld0")
-    load("y", A("X", 0, 1312), T.x[:, 0:1312], "ld1")
-    load("s", A("X", 1312, U), T.x[:, 1312:U], "ld2")
-    load("y", A("CDI"), T.cd[:, :], "ld3")
-    load("y", A("X", U, W), T.x[:, 0:W - U], "ld4")
+    load("y", A("OCI"), T.oc[:, :], "ld0", 2.7)
+    load("y", A("X", 0, 1312), T.x[:, 0:1312], "ld1", 3.7)
+    load("s", A("X", 1312, U), T.x[:, 1312:U], "ld2", 3.7)
+    load("y", A("CDI"), T.cd[:, :], "ld3", 4.2)
+    load("y", A("X", U, W), T.x[:, 0:W - U], "ld4", 5.0)
+    lanes.append([0, 1, 3, 4])
+    ms(A("ONE"), 1.0)
+    ms(A("IDW"), 0.0)
+    ms(R("ZR", 0, 768), 0.0)
     iota(A("PI", 0, 1), [[0, 1]], 0, 1, False)
-    iota(A("IOT"), [[1, 256]], 0, 0)
+    iota(io_(0, 16), [[1, 16]], 0, 0)
     iota(A("B82", 0, 82), [[0, 2], [1, 41]], 32, 0)
     iota(A("B82", 88, 170), [[-1, 2], [0, 41]], 1, 0)
+    sel(ident, A("ONE"), [[-1, 128]], ALU.is_equal, 0.0, 0, 1)
+    sel(A("BLK"), A("ONE"), [[-16, 8], [0, 16]], ALU.is_ge, 0.0, 0, 1)
+    iota(col(20), [[0, 1]], 1, -1)
+    sel(A("BLK"), A("BLK"), [[16, 8], [0, 16]], ALU.is_ge, 0.0, 15, -1)
     ms(A("RW"), 0.0)
-    for a, b, c in ((3, 4, 2.0), (4, 5, -2.0), (5, 6, -1.0), (6, 9, 1.0), (9, 11, 256.0), (11, 13, -256.0), (15, 16, -1.0)):
-        ms(A("RW", a, b), c)
     ts(A("PI", 1, 2), A("PI", 0, 1), 15, ALU.bitwise_and)
     ts(A("PI", 2, 3), A("PI", 0, 1), 31, ALU.bitwise_and)
     cp(A("COL", 0, 2), A("PI", 1, 3))
+    for a, b, c in ((3, 4, 2.0), (4, 5, -2.0), (5, 6, -1.0), (6, 8, 1.0), (9, 11, 256.0), (11, 13, -256.0),
+                    (19, 20, -103.5), (20, 21, 103.5), (21, 22, 33.0), (22, 23, -71.0), (23, 24, -32.0), (25, 29, -1e5)):
+        ms(A("RW", a, b), c)
     ts(A("E16"), io_(0, 16), col(0), ALU.is_equal)
-    tt(A("RW", 0, 16), A("RW", 0, 16), A("E16"), MUL)
-    ts(col(10), A("E16", 5, 6), 256.0, MUL)
-    for i in range(3):
-        ts(col(5 + i), A("E16", 13, 14), float(1 << i), MUL)
-    red(col(2), A("RW", 0, 16), ADD)
-    ts(A("B82", 88, 170), A("B82", 88, 170), col(10), MUL)
-    for i in range(3, 5):
-        ts(col(5 + i), A("E16", 13, 14), float(1 << i), MUL)
-    ts(A("B82", 0, 82), A("B82", 0, 82), col(2), MUL)
-    cp(A("OCU"), A("OCI"))
+    for k in range(2):
+        tt(B("RW", k, 16), B("RW", k, 16), A("E16"), MUL)
+        red(col(2 + k), B("RW", k, 16), ADD)
+    mul(col(10), e16(5), 256.0)
+    for i in range(5):
+        mul(col(5 + i), e16(13), float(1 << i))
+    mul(A("B82", 88, 170), A("B82", 88, 170), col(10))
+    mul(A("B82", 0, 82), A("B82", 0, 82), col(2))
     tt(A("SRC", 0, 82), A("B82", 0, 82), A("B82", 88, 170), ADD)
     for i in range(4):
         n = 82 << i
-        ts(A("SRC", n, 2 * n), A("SRC", 0, n), col(5 + i), ADD)
-    act(A("ONE"), io_(0, 128), ACT.Identity, 1.0, 0.0)
-    for name in ("IDW", "SLT", "MAS", "MB", "WDL", "WDR", "WDZ", "FS", "FV", "WK", "WQ", "WC3"):
-        act(A(name), io_(0, SCRATCH[name][1][1]), ACT.Copy, None, 0.0)
-    act(A("EIG"), io_(0, 128), ACT.Identity, 0.125, 0.0)
-    act(A("XG", U, U + 8), io_(0, 8), ACT.Copy, None, 0.0)
-    act(A("AD", 0, 1), io_(0, 1), ACT.Copy, None, 0.0)
-    act(A("AS"), io_(0, 216), ACT.Copy, None, 0.0)
-    sel(A("BLK"), A("ONE"), [[-16, 8], [0, 16]], ALU.is_ge, 0.0, 0, 1)
-    sel(ident, A("ONE"), [[-1, 128]], ALU.is_equal, 0.0, 0, 1)
-    sel(A("BLK"), A("BLK"), [[16, 8], [0, 16]], ALU.is_ge, 0.0, 15, -1)
-    act(A("SRC", 1312, U), A("SRC", 0, 1312), ACT.Identity, col(9))
-    act(A("NEGI"), ident, ACT.Copy, None, -1.0)
-    for name, cols in (("WDL", (0, 12)), ("WDR", (1, 10)), ("WDZ", (2,))):
-        for c in cols:
-            act(S(name, c), g8)
-    act(A("WZ"), A("BLK"), ACT.Copy, None, 61.0)
-    act(S("FS", 16), g8, ACT.Copy, None, -256.0)
-    act(S("FV", 16), g8, ACT.Copy, None, 512.0)
-    load("g", A("STC", U, W), T.x[:, 0:W - U], "ld5")
-    ents({("MB", 16): ((0, 256), (11, 256), (12, -256), (1, -256), (9, -256), (10, 256), (3, 2 ** 17), (4, -2 ** 17),
-                       (8, 2 ** 16), (15, -2 ** 16)),
-          ("MAS", 16): ((1, 256), (9, 256), (10, -256), (3, -2 ** 17), (5, -2 ** 18), (6, -2 ** 18), (8, -2 ** 16)),
-          ("SLT", 16): ((13, 82), (5, -41 / 256), (7, -41 / 256), (6, 1)),
-          ("WQ", 6): ((0, 1), (11, 1), (12, -1), (1, -1), (9, -1), (10, 1)), ("WQ", 5): ((1, 1), (9, 1), (10, -1))})
-    sel(A("MAV"), A("MAS"), [[0, 144]], ALU.is_ge, 0.0, 0, 0)
-    iota(A("NKK", 0, 256, 1, 0, 1), [[0, 2], [-1, 128]], 0, 0)
-    ents({("MAV", 16): ((2, -256),)})
+        lin(A("SRC", n, 2 * n), A("SRC", 0, n), col(5 + i))
+    cp(A("OCU"), A("OCI"))
 
-    cp(IND(A("SC"), A("OCU", 0, 82)), A("SRC", 0, 1312))
-    cp(IND(A("SC"), A("OCU", 82, 164)), A("SRC", 1312, U))
+    scaled = {1: ident}
+    for w, name in ((-1, "NEGI"), (-1024, "N1K"), (256, "I256"), (-256, "N256"), (0.5, "HALF")):
+        mul(A(name), ident, float(w))
+        scaled[w] = A(name)
+    sums = {2: (1, 1), -2: (-1, -1), -0.5: (-1, 0.5), 2.5: (1, 1, 0.5), -2.5: (-1, -1, -1, 0.5), -255: (-256, 1)}
+    rare = []
 
-    def first_ends():
-        act(A("AS", 0, 32), A("XG", 0, U - 81, 82))
-        act(A("AS", 32, 64), A("XG", 40, U - 41, 82))
-        n0 = send(A("AS", 0, 72), "AL", 0, 72, "a0", rank + 1, "loc0")
-        g.sync.wait_ge(T.sem.loc0, n0)
-        fills = [("XS", c, min(U, XSW - c)) for c in range(0, XSW, U)] + [("MG", W, 144), ("SP", 1024, CAP)]
-        for name, c, n in fills:
-            sync("y", [], [A(name, c, c + n)], "ld6", 16 * len(fills))
-            g.sync.dma_start(T[name][:, c:c + n], T.x[:, 0:n]).then_inc(T.sem.ld6, 16)
+    def pick(f):
+        return g8 if f is None else S("IDW", 16 + f)
+
+    def weights(bank, width, table):
+        todo = []
+        for out, col_ents in table:
+            for f, w in col_ents:
+                if w in scaled or w in sums:
+                    todo += [(out, scaled[x], pick(f)) for x in sums.get(w, (w,))]
+                else:
+                    if (f, w) not in rare:
+                        rare.append((f, w))
+                        mul(B("SELW", len(rare) - 1, 8), pick(f), float(w))
+                    todo.append((out, ident, B("SELW", rare.index((f, w)), 8)))
+        k = len(calls)
+        mm(A("P%d" % bank, 0, width), one_row, R("ZR", 0, width), True, False)
+        group = [len(todo), "w%d" % bank]
+        for c in todo:
+            mm(c[0], c[1], c[2], False, False, group)
+        chain(k, "t")
+
+    def wc(name, c):
+        base, bank = PART[name][1], PART[name][3]
+        if name in ("WM", "WF"):
+            return A("P%d" % bank, base + 8 * c, base + 8 * c + 8)
+        return S("P%d" % bank, base + c)
+
+    def neg(e):
+        return tuple((f, -w) for f, w in e)
+
+    every = ((None, 1),)
+    weights(4, 512, [(wc("WDL", 0), every), (wc("WDL", 12), every), (wc("WDR", 1), every), (wc("WDR", 10), every),
+                     (wc("WDZ", 2), every), (wc("WDN", 1), every)])
+    mov(A("WA"), A("P4"))
+    low = ((1, 1), (9, 1), (10, -1), (3, -1024))
+    high = ((0, 1), (11, 1), (12, -1), (4, -1024))
+    bad = ((5, -1024), (6, -1024))
+    size = ((7, 1), (3, -1), (8, -0.5))
+    weights(5, 464, [(wc("WF", 0), neg(every)), (wc("WF", 1), neg(every)), (wc("WF", 2), ((None, 2),)),
+                     (wc("WF", 3), ((None, 2),)), (wc("WM", 0), low + bad), (wc("WM", 1), high + bad), (wc("WM", 2), size),
+                     (wc("WM", 3), low + bad + ((2, -1),)), (wc("WM", 4), high + bad + ((2, -1),)), (wc("WM", 5), size),
+                     (wc("WG1", 0), every), (wc("WG1", 2), every), (wc("WK", 1), neg(every)), (wc("WK", 3), neg(every)),
+                     (wc("WG2", 0), every), (wc("WG2", 3), ((None, -1 / 256),)),
+                     (wc("WG2", 4), ((None, -1 / 256),)), (wc("WG2", 6), ((None, 128),))])
+    mov(A("WC"), A("P5", 0, 464))
+    weights(7, 288, [(S("P7", 16), ((13, 256), (14, 1), (7, 1), (15, -2))),
+                     (S("P7", 160), ((13, 1), (5, -0.125), (7, -0.125)))])
+    mov(A("VLT"), A("P7", 144, 288))
+    mov(A("TGT"), A("P7", 0, 144))
+    side1 = ((8, -1), (9, -1), (0, -1), (1, 2), (10, 0.5), (3, -1))
+    side2 = ((9, 1), (8, -1), (0, -1), (10, 2.5), (6, -2))
+    weights(6, 512, [(wc("WQ1", c), ((f, 1),)) for c, f in ((4, 4), (5, 3), (6, 3), (12, 8), (13, 8), (14, 15))] + [
+        (wc("WQ2", 0), ((13, 131072),)), (wc("WQ2", 1), size), (wc("WQ2", 2), ((13, 82), (7, 1), (14, 1), (15, -2))),
+        (wc("WQ2", 3), low), (wc("WQ2", 4), high), (wc("WQ2", 5), ((13, 1),)), (wc("WQ2", 7), ((13, 1),)),
+        (wc("WC1", 3), side1), (wc("WC1", 4), neg(side1)), (wc("WC1", 5), ((8, 1), (10, 1), (3, -1), (12, -1))),
+        (wc("WC1", 6), ((9, -1), (10, 1), (2, -1), (3, 1))), (wc("WC1", 7), ((8, -1), (1, 1))), (wc("WC1", 8), ((3, 1),)),
+        (wc("WC1", 9), ((7, 1), (9, -256))), (wc("WC1", 10), ((9, -256),)), (wc("WC1", 11), ((7, 1), (8, 256))),
+        (wc("WC1", 12), ((8, 256),)), (wc("WC1", 14), ((8, 1), (1, -1))),
+        (wc("WC2", 3), side2), (wc("WC2", 4), neg(side2)), (wc("WC2", 6), ((10, 2), (0, -1), (6, -1))),
+        (wc("WC2", 7), ((9, 1), (8, -1), (10, 1), (6, -1))), (wc("WC2", 11), ((7, 1), (6, 256))),
+        (wc("WC2", 12), ((6, 256),)), (wc("WC2", 13), ((11, 1),)), (wc("WC2", 14), ((8, 1), (13, 1))),
+        (wc("WC2", 15), ((9, 1), (8, -1), (10, -255), (6, -1), (3, 256)))])
+    mov(A("WB", 0, 256), A("P6", 0, 256))
+    mov(A("WB", 256, 512), A("P6", 256, 512))
+
+    mul(A("WZ"), A("BLK"), 61.0)
+    gfill(A("XG", U, U + 8))
+    gfill(A("AD", 0, 1))
+    for t in range(3):
+        gfill(A("AS", 72 * t + 64, 72 * t + 72))
+        gfill(A("LS", 240 * t + CAP, 240 * t + 240))
+    iota(io_(16, 256), [[1, 240]], 16, 0)
+    iota(R("NKK"), [[-1, 128]], 0, 0)
+    gfill(A("STC", U, U + 368), 600)
+    gfill(A("MW", U + CAP, U + CAP + 416), 600)
+    twins = [("STC", U + 368 * k, 368, U) for k in (1, 2, 3)] + [("MW", U + CAP + 416 * k, 416, U + CAP) for k in (1, 2)]
+
+    def fill_twins():
+        for name, c, n, c0 in twins:
+            g.sync.dma_start(T[name][:, c:c + n], T[name][:, c0:c0 + n]).then_inc(T.sem.fill, 16)
+
+    note("y", fill_twins, [A("STC", U, U + 368), A("MW", U + CAP, U + CAP + 416)],
+         [A(name, c, c + n) for name, c, n, _ in twins], 0.25, "fill", 16 * len(twins), 2.5)
+    k0 = len(calls)
+    for c in range(0, U, 328):
+        iota(A("NO", c, c + 328), [[1, 328]], c, 0)
+    chain(k0, "g")
+    k0 = len(calls)
+    mul(R("ZR", 768, 896), one_row, -62.25)
+    mul(col(11), col(0), 128.0)
+    lin(col(12), col(0), 2048.0, 128.0)
+    lin(col(13), col(1), -32768.0, 8.0)
+    mul(col(27), col(0), 82.0)
+    lin(col(16), col(1), col(20))
+    lin(A("KW"), io_(0, 16), col(0), 16.0)
+    mov(A("IDF"), ident)
+    mul(A("INEG"), ident, -262144.0)
+    lin(A("UOH"), io_(0, 128), col(16))
+    iota(R("NJ", 0, 64), [[0, 2], [-8, 32]], 0, 0)
+    gfill(R("NJ", 66, 72))
+    gfill(R("NJ", 64, 66), 230400)
+    mul(R("NJ", 68, 70), R("ONE", 0, 2), -7.5)
+    gfill(R("CQ"))
+    gfill(A("ES"))
+    gfill(A("B32"))
+    gfill(col(26), -4)
+    gfill(R("CQ", 5, 118, 16), 1)
+    gfill(R("CQ", 7, 120, 16), -15)
+    mul(R("CQ", 1, 114, 16), R("ONE", 0, 8), 1.25)
+    for gm in range(2):
+        sel(B("WRG", gm), A("ONE"), [[-32, 4], [0, 32]], ALU.is_ge, 0.0, -16 * gm, 1)
+        sel(B("WRG", gm), B("WRG", gm), [[32, 4], [0, 32]], ALU.is_ge, 0.0, 16 * gm + 15, -1)
+        sel(B("WR", gm), A("B32"), [[-32, 4], [0, 32]], ALU.not_equal, 131072.0, -(16 * gm + 13), 1)
+    sel(A("TRI"), A("ONE"), [[1, 128]], ALU.is_ge, 0.0, 0, -1)
+    sel(A("TRI"), A("TRI"), [[-32, 4], [0, 32]], ALU.is_ge, 0.0, 0, 1)
+    sel(A("TRS"), A("TRI"), [[-1, 128]], ALU.not_equal, 0.0, 0, 1)
+    mul(A("TRN"), A("TRI"), -1024.0)
+    iota(A("EB"), [[40, 2], [1312, 2]], 41, 0)
+    lin(A("EB"), A("EB"), col(27))
+    gfill(A("SCL"), 256)
+    gfill(A("SCL", 2, 19, 16), 1)
+    gfill(A("SCL", 3, 20, 16), 1)
+    iota(A("K16"), [[16, 16]], 0, 0)
+    iota(A("ST", 0, 8), [[0, 4], [40, 2]], 32, 0)
+    iota(B("OW", 1), [[0, 8], [1, 16]], 1, 0)
+    for o, i, name, fill in ((B("OW", 0), A("ONE"), "CB", 0.0), (B("OW", 1), B("OW", 1), "CR", -100.0)):
+        sel(o, i, [[-32, 4], [0, 32]], ALU.is_ge, fill, 0, 1)
+        sel(o, o, [[32, 4], [0, 32]], ALU.is_ge, fill, 31, -1)
+        for gm in range(2):
+            sel(B(name, gm), o, [[0, 4], [1, 2], [0, 16]], ALU.is_equal, fill, -gm, 0)
+    gfill(A("OWN"))
+    gfill(sm(24), 40)
+    for c, v in ((8, 32), (9, 72), (10, 1), (12, 256)):
+        gfill(A("OWN", c, c + 17, 16), v)
+    mul(A("OWN", 11, 28, 16), A("ONE", 0, 2), col(1))
+    tr(A("OWR"), A("OWN"))
+    ts(col(14), col(1), 16.0, ALU.is_lt)
+    iota(i3, [[16, 4], [1, 16]], 0, 0)
+    lin(col(15), col(14), 1.0, -1.0)
+    lin(col(25), e16(9), e16(10))
+    mul(col(21), e16(5), 600.0)
+    mul(col(22), e16(15), -1000.0)
+    lin(col(4), col(25), col(21), -1e5)
+    lin(col(23), col(25), col(2), -256.0)
+    lin(col(28), e16(13), col(22), 32.0)
+    lin(col(24), col(23), e16(15))
+    lin(col(17), col(28), col(4))
+    lin(B("CT", 1, 32), io_(0, 32), col(4), 0.0)
+    mul(A("KT"), io_(0, CAP), col(24))
+    lin(A("CT", 96, 104), io_(0, 8), col(17), 0.0)
+    for h in range(2):
+        mul(col(29 + h), col(11 + h), 2.0)
+        mul(A("CWB", h, 4, 2), A("ONE", 0, 2), col(29 + h))
+    mul(col(18), col(1), 256.0)
+    lin(col(19), col(1), 128.0, 256.0)
+    gfill(A("CS", ZADDR, XSW), -1)
+    iota(A("CS", PARTS, PARTS + CAP), [[1, CAP]], U + 2 * CAP, 0)
+    iota(A("NUM"), [[1, 2 * CAP]], U, 0)
+    chain(k0, "g")
 
     def dist_a(src, c0, n, pb, d0):
-        if pb is None:
-            tt(A("DI", c0, c0 + n), A(src, c0, c0 + n), A(src, c0 + 1, c0 + n + 1), SUB)
-            act(A("AD", d0, d0 + n), A("DI", c0, c0 + n), ACT.Abs)
-            return
         mm(A(pb, 0, n), ident, A(src, c0, c0 + n), True, False)
         mm(A(pb, 0, n), A("NEGI"), A(src, c0 + 1, c0 + n + 1), False, True)
         act(A("AD", d0, d0 + n), A(pb, 0, n), ACT.Abs)
 
     def dist_b(src, c0, n, pb, d0, last):
-        mm(A(pb, 0, n), A("WDL"), A("AD", d0, d0 + n), True, False)
-        mm(A(pb, 0, n), A("WDR" if last else "WDN"), A("AD", d0 + 1, d0 + n + 1), False, False)
-        mm(A(pb, 0, n), A("WDZ"), A(src, c0, c0 + n), False, last)
+        mm(A(pb, 0, n), A("WDZ"), A(src, c0, c0 + n), True, False)
+        mm(A(pb, 0, n), A("WDL"), A("AD", d0, d0 + n), False, False)
+        mm(A(pb, 0, n), A("WDR" if last else "WDN"), A("AD", d0 + 1, d0 + n + 1), False, last)
 
     def lists(t):
         b = 72 * t
         for bit in range(2):
             for qq in range(4):
                 mm(A("P4", 4 * bit + qq, 256, 8), A("WZ"), A("AL", b + 32 * bit, b + 32 * bit + 32), True, True)
-        halves = ((0, 96), (96, 256))
-        for lo, hi in halves:
-            tt(A("MI", lo, hi), A("CDF", lo, hi), A("P4", lo, hi), ADD)
-        for lo, hi in halves:
+        for lo, hi in ((0, 96), (96, 256)):
+            tt(A("MI", lo, hi), A("CDI", lo, hi), A("P4", lo, hi), ADD)
             ts(A("MJ", lo, hi), A("MI", lo, hi), 4095, ALU.bitwise_and)
-        for lo, hi in halves:
             cp(A("MU", lo, hi), A("MJ", lo, hi))
-        ts(A("XH"), A("AL", b, b + 64), 0.5, MUL)
+        mul(A("XH"), A("AL", b, b + 64), 0.5)
 
-    def setup():
-        chunks = [(c, min(512, U - c)) for c in range(0, U, 512)]
-        for i in range(len(chunks) + 1):
-            if i < 3:
-                lo, hi = (0, 66, 130)[i], (66, 130, 164)[i]
-                act(A("XG", 16 * lo, 16 * hi), IND(A("X", 0, U), A("OCU", lo, hi)))
-            if i == 2:
-                first_ends()
-            if i < 3:
-                c, n = chunks[i]
-                dist_a("XG", c, n, "P%d" % (i % 2), c + 1)
-            if i == 3:
-                dist_a("XG", 1536, 512, None, 1537)
-                dist_a("XG", 2048, 576, None, 2049)
-            if i > 0:
-                c, n = chunks[i - 1]
-                dist_b("XG", c, n, "P%d" % (2 + i % 2), c, True)
-                (act if i != 4 else cp)(A("DS", c, c + n), A("P%d" % (2 + i % 2), 0, n))
-            if i == 3:
-                for name in ("VLT", "WG", "WC1", "WC2", "WB", "WDN", "TGT"):
-                    ms(A(name), 0.0)
-                for name, psi, phi, w in (
-                        ("WQ", 0, 3, 1), ("WQ", 3, 7, 1), ("WQ", 4, 9, 1), ("WQ", 11, 14, 1), ("WQ", 7, 13, 16384),
-                        ("WQ", 8, 13, 1), ("WC1", 10, 9, -256), ("WC1", 12, 8, 256), ("WC2", 12, 4, 256), ("WC2", 13, 11, 1)):
-                    ts(S(name, psi), S("IDW", 16 + phi), float(w), MUL)
-                wrap("P6", 164, "SLT", "SC", U)
-                cp(A("CDF"), A("CDI"))
-                ts(A("SLU"), A("P6", 0, 164), 9.0, ADD)
-            if i == 4:
-                lists(0)
-            if i == 5:
-                for a, b, c in ((19, 20, -103.5), (20, 21, 103.5), (21, 22, 33.0), (22, 23, -71.0), (23, 24, -32.0),
-                                (24, 29, -1e5), (30, 31, 32.0), (31, 32, -1e5)):
-                    ms(A("RW", a, b), c)
-                tt(A("RW", 16, 32), A("RW", 16, 32), A("E16"), MUL)
-                red(col(3), A("RW", 16, 32), ADD)
+    for lo, hi in ((0, 34), (34, 66), (66, 98), (98, 130), (130, 164)):
+        mov(A("XG", 16 * lo, 16 * hi), IND(A("X", 0, U), A("OCU", lo, hi)))
+    mov(A("AS", 0, 32), A("XG", 0, U - 81, 82))
+    mov(A("AS", 32, 64), A("XG", 40, U - 41, 82))
+    first = send(A("AS", 0, 72), A("AL", 0, 72), "a0", rank + 1, "loc0", 1.0)
+    fills = [("XS", c, min(U, XSW - c)) for c in range(0, XSW, U)] + [("MG", W, 144), ("SP", 1024, CAP)]
 
-    def later_weights():
-        iota(A("NJ", 0, 64, 1, 0, 1), [[0, 2], [-1, 32]], 0, 0)
-        for gm in range(2):
-            sel(B("WRG", gm), A("EIG"), [[-32, 4], [0, 32]], ALU.is_ge, 0.0, -16 * gm, 1)
-            sel(B("WR", gm), A("WC3"), [[-32, 4], [0, 32]], ALU.not_equal, 16384.0, -(16 * gm + 13), 1)
-        sel(A("TRI"), A("ONE"), [[1, 128]], ALU.is_ge, 0.0, 0, -1)
-        for gm in range(2):
-            sel(B("WRG", gm), B("WRG", gm), [[32, 4], [0, 32]], ALU.is_ge, 0.0, 16 * gm + 15, -1)
-        sel(A("TRI"), A("TRI"), [[-32, 4], [0, 32]], ALU.is_ge, 0.0, 0, 1)
-        ents({("VLT", 16): ((13, 1), (5, -0.125), (7, -0.125)), ("WQ", 1): ((7, 1), (3, -1)),
-              ("WQ", 2): ((13, 256), (14, 1), (7, 1))})
-        ents({("WC1", 3): ((8, -1), (9, -1), (0, -1), (1, 2), (10, 0.5), (3, -1)),
-              ("WC1", 5): ((8, 1), (10, 1), (3, -1), (12, -1)), ("WC1", 6): ((9, -1), (10, 1), (2, -1), (3, 1)),
-              ("WC1", 7): ((8, -1), (1, 1)), ("WC1", 14): ((8, 1), (1, -1), (3, 128)), ("WC1", 9): ((5, 1), (9, -256)),
-              ("WC1", 11): ((5, 1), (8, 256)), ("WC1", 15): ((9, 1), (0, 1), (1, -1)),
-              ("WC2", 3): ((9, 1), (8, -1), (0, -1), (10, 2.5), (4, -2)), ("WC2", 6): ((10, 2), (0, -1), (4, -1)),
-              ("WC2", 7): ((9, 1), (8, -1), (10, 1), (4, -1)), ("WC2", 9): ((10, 252), (3, 2)),
-              ("WC2", 15): ((0, 1), (10, -1), (4, 1)), ("WC2", 11): ((5, 1), (4, 256)), ("WC2", 14): ((8, 1), (6, 1))})
+    def fill_gaps():
+        g.sync.wait_ge(T.sem.loc0, len(engines(core, T.cores[(rank + 1) % n_ranks])))
+        for name, c, n in fills:
+            g.sync.dma_start(T[name][:, c:c + n], T.x[:, 0:n]).then_inc(T.sem.ld6, 16)
 
-    def rest_weights():
-        ents({("WC3", 6): ((9, 1), (8, -1), (10, -255), (4, -1), (3, 256)), ("WC3", 13): ((11, 2), (10, 1), (12, -1 / 256)),
-              ("TGT", 16): ((13, 128), (14, 1), (7, 1), (6, -2))})
-        iota(A3("I3", 0, 16), [[16, 4], [1, 16]], 0, 0)
-        iota(A("YO", 0, U), [[1, U]], 0, 0)
+    note("y", fill_gaps, [], [A(name, c, c + n) for name, c, n in fills], 0.3, "ld6", 16 * len(fills), 7.0, after=[first])
+    for i, (c, n) in enumerate(((0, 512), (512, 512), (1024, 288), (1312, 512), (1824, 512), (2336, 288))):
+        dist_a("XG", c, n, "P%d" % (i % 2), c + 1)
+        dist_b("XG", c, n, "P%d" % (2 + i % 2), c, True)
+        lin(A("DS", c, c + n), A("P%d" % (2 + i % 2), 0, n), col(9) if c >= 1312 else 0.0)
+        tt(IND(A("STC", 0, U), A("OCU", c // 16, (c + n) // 16)), A("DS", c, c + n), A("SRC", c % 1312, c % 1312 + n), ADD)
 
-    def feat_mm(t, j, last=False):
-        r, h = j % 16, j // 16
-        mm(B("P0", h), A("FS" if j < NS[t] else "FV", 16 - r, 144 - r), B("FD", j), False, last)
+    def spread(dst, src):
+        k = len(calls)
+        for i in range(41):
+            sel(A(dst, 32 + i, 8192, 128), A(src, i, U, 41), [[0, 64]], ALU.is_ge, 0.0, 0, 0)
+        chain(k, "g")
 
-    def feat(t, j, last=False, now=True):
-        for bit in range(2):
-            e = 2 * j + bit
-            o, i = B("FD", e, 64), IND(A("X"), B("MU", e, 4))
-            xe = B("AL", 72 * t + 32 * bit + j, 1)
-            if j < NS[t]:
-                act(o, i, ACT.Abs, xe, -1.0)
-            else:
-                ts(o, i, xe, MIN, B("XH", 32 * bit + j, 1), SUB)
-        if now:
-            feat_mm(t, j, last)
+    def score(t):
+        groups = [[33 if t else 32, "s%d%d" % (t, h)] for h in range(2)]
+        n = 3 if t else 2
+        for h in range(2):
+            mm(A("P%d" % h, 0, 384), one_row, R("ZR", 512, 896), True, False)
+        if t:
+            act(sm(48), A("AL", 72 * t + 64, 72 * t + 66), ACT.Abs)
+            for h in range(2):
+                mul(B("RH", h), ident, sm1(48, h))
+                mm(A("P%d" % h, 256, 384), A("ONE"), B("RH", h), False, False, groups[h])
 
-    def meta(t, j0, j1):
-        if t == 0:
-            act(A("MG", 128 * j0, 128 * j1), IND(A("STC"), A("MU", 8 * j0, 8 * j1)), ACT.Relu, col(3))
-        else:
+        def ends(j):
+            return [(B("FD", 2 * j + bit, 64)[0], IND(A("X"), B("MU", 2 * j + bit, 4))[0],
+                     B("AL", 72 * t + 32 * bit + j, 1)[0], B("XH", 32 * bit + j, 1)[0]) for bit in range(2)]
+
+        def by_scalar(j):
+            return [g.scalar.activation(o, i, ACT.Abs, bias=x, scale=-1.0) for o, i, x, _ in ends(j)]
+
+        def by_vector(j):
+            return [g.vector.tensor_scalar(o, i, x, xh, MIN, SUB) for o, i, x, xh in ends(j)]
+
+        who, k = [], len(calls)
+        for j in range(32):
+            who.append(either(lambda j=j: by_scalar(j), lambda j=j: by_vector(j),
+                              [IND(A("X"), B("MU", j, 8)), A("AL", 72 * t, 72 * t + 64), A("XH")], B("FD", j)))
+            alt = tuple((e, c + (0.065 if e == "s" else 0.05)) for e, c in who[j]["alt"])
+            who[j].update(alt=alt, cost=alt[0][1], n=2)
+            mm(A("P%d" % (j // 16), j % 16, 256, 16), B("FD", j), A("WF"), False, False, groups[j // 16],
+               lambda j=j: B("WF", 1 if who[j]["q"] == "v" else 0, 16))
+        chain(k, "s")
+        k = len(calls)
+        for j0, j1 in ((0, 4), (4, 8), (8, 12), (12, 16), (16, 20), (20, 24), (24, 28), (28, 30), (30, 32)):
+            relu(A("MG", 128 * j0, 128 * j1), IND(A("MW" if t else "STC"), A("MU", 8 * j0, 8 * j1)), 0.0 if t else col(3))
             for j in range(j0, j1):
-                act(B("MG", j), IND(A("MW"), B("MU", j, 8)), ACT.Relu, B("BT", j, 1))
-        for j in range(j0, j1):
-            r, h = j % 16, j // 16
-            mm(B("P0", h), A("MAS" if j < NS[t] else "MAV", 16 - r, 144 - r), B("MG", j), False, False)
-            mm(B("P1", h), A("MB", 16 - r, 144 - r), B("MG", j), r == 0, r == 15)
-
-    def scalar_feats(t, extra):
-        mm(A("P0", 0, 256), one_row, A("NKK", 0, 256, 1, 0, 1), True, False)
-        for j in range(NS1[t]):
-            feat(t, j)
-            if j in extra:
-                extra[j]()
-
-    def gathers(t, extra):
-        rest = list(range(NS[t], 32))
-        cuts = (0, 4, 8, 12, 16, 20, 24, 28, 30, 31, 32)
-        nv = NV[t]
-        per = [len(rest) * (c + 1) // nv - len(rest) * c // nv for c in range(nv)] + [0] * (10 - nv)
-        mine = []
-        for c in range(10):
-            meta(t, cuts[c], cuts[c + 1])
-            for j in mine:
-                feat_mm(t, j)
-            mine, rest = rest[:per[c]], rest[per[c]:]
-            for j in mine:
-                feat(t, j, False, False)
-        extra()
-        for j in range(NS1[t], NS[t]):
-            feat(t, j, j == NS[t] - 1)
-        ts(A("RR"), A("P1", 0, 256), 0.0, MAX)
+                mm(A("P%d" % (j // 16), j % 16, 128 * n, 16), B("MG", j), A("WM"), False, False, groups[j // 16],
+                   lambda j=j: A("WM", 24, 24 + 8 * n) if who[j]["q"] == "v" else A("WM", 0, 8 * n))
+        chain(k, "s")
+        for h in range(2):
+            pb = "P2" if h == 0 else "P7"
+            mm(B(pb, 0), one_row, R("NKK"), True, False)
+            relu(A("G", 384 * h, 384 * h + 128 * n), A("P%d" % h, 0, 128 * n))
+            for k in range(n):
+                mm(B(pb, 0), B("G", 3 * h + k), A("I256" if k < 2 else "INEG"), False, k == n - 1)
+            red(sm1(0, h), B(pb, 0), MAX)
 
     def q(i):
-        return A("TQ", i, i + 17, 16)
+        return A("TQ", 32 + i, 32 + i + 17, 16)
 
     def q1(i, gm):
-        return B("TQ", i + 16 * gm, 1)
+        return B("TQ", 32 + i + 16 * gm, 1)
 
     def state(par, gen):
         return 8 * gen + 4 * par
 
-    def choose(t, s_old, s_new, s_idle, fill=lambda: None):
+    def choose(t, s_old, s_new):
         par = 1 - t % 2
-        for h in range(2):
-            tt(B("KEY", h), B("P0", h), B("RR", h), ADD)
-        for h in range(2):
-            red(sm1(0, h), B("KEY", h), MAX)
-        for h in range(2):
-            ts(sm1(1, h), sm1(0, h), MAGIC, ADD, MAGIC, SUB)
+        win, base, top = (A("XG"), 41.0, U + 7) if t == 0 else (A("XS"), 128.0 * par, XSW - 1)
+        eb, lb, ab = 32 * t, 240 * t, 72 * (t + 1)
+        mm(A("P3", 0, 64), R("ZR", 0, 128), R("ONE", 0, 64), True, False)
+        mm(A("P5", 0, 64), one_row, R("NJ", 0, 64), True, False)
+        mm(A("P6", 0, 14), ident, A("KW", 0, 14), True, False)
+        ts(sm(1), sm(0), MAGIC, ADD, MAGIC, SUB)
+        tt(sm(2), sm(1), sm(0), SUB)
         for h in range(2):
             ts(B("OFF", h, 1), sm1(1, h), sm1(0, h), SUB, col(11 + h), ADD)
-        tt(sm(2), sm(1), sm(0), SUB)
-        cp(A("MBS"), IND(A("MG"), A("OFF", 0, 2)))
-        for h in range(2):
             act(B("GD", h, 16), A("E16"), ACT.Relu, None, sm1(1, h))
-        for h in range(2):
-            ts(B("GD", 2 + h, 16), A("E16"), sm1(2, h), MUL)
-        mm(A("P3", 0, 32), A("WG"), A("GD", 0, 32), True, False)
-        mm(A("P3", 0, 32), A("WQ"), A("MBS"), False, False)
-        mm(A("P3", 0, 32), A("WK"), A("GD", 32, 64), False, True)
-        mm(A("P5", 0, 64), one_row, A("NJ", 0, 64, 1, 0, 1), True, False)
+            lin(B("GD", 2 + h, 16), A("E16"), col(26), sm1(2, h))
+        mov(A("MBS"), IND(A("MG"), A("OFF", 0, 2)))
+        ga, gb = [6, "a%d" % t], [4, "b%d" % t]
+        mm(A("P3", 32, 64), R("CQ"), R("ONE", 0, 32), False, False, ga)
+        mm(A("P3", 0, 32), A("WG1"), A("GD", 0, 32), False, False, ga)
+        mm(A("P3", 32, 64), A("WG2"), A("GD", 0, 32), False, False, ga)
+        mm(A("P3", 0, 32), A("WK"), A("GD", 32, 64), False, False, ga)
+        mm(A("P3", 0, 32), A("WQ1"), A("MBS"), False, False, ga)
+        mm(A("P3", 32, 64), A("WQ2"), A("MBS"), False, False, ga)
         for gm in range(2):
-            mm(B("P5", gm, 32), B("WR", gm), A("MBS"), False, False)
-            mm(B("P5", gm, 32), B("WRG", gm), A("GD", 0, 32), False, gm == 1)
-        fill()
-        tr(A("TQ"), A("P3", 0, 32))
-        ts(sm(3), q(0), 0.0, ALU.is_gt)
-        if t > 0:
-            ts(sm(6), q(4), 253.0, ALU.is_ge, -2.0, MUL)
-            ts(sm(42), q(11), 128.0, ALU.is_ge, 128.0, MUL)
+            mm(B("P5", gm, 32), B("WRG", gm), A("GD", 0, 32), False, False, gb)
+            mm(B("P5", gm, 32), B("WR", gm), A("MBS"), False, False, gb)
+        tr(A("TQ"), A("P3", 0, 64))
+        mm(A("P3", 0, 8), one_row, R("NJ", 64, 72), True, False)
+        ts(A("B1"), A("TQ", 0, 32), 0.0, ALU.is_gt)
+        mov(A("DF", 32, 73, 40), q(6))
+        act(sm(6), q(1), ACT.Identity, MAGIC / 256)
+        act(sm(3), sm(6), ACT.Identity, -MAGIC / 256)
         for gm in range(2):
-            ts(B("DF", gm, 32), B("P5", gm, 32), q1(7, gm), SUB, col(13), ADD)
-        if t == 0:
-            ts(sm(4), sm(3), 2.0, MUL, -1.0, ADD)
-            ts(sm(43), sm(3), 0.5, MUL)
-        else:
-            ts(sm(7), sm(3), 2.0, MUL, -1.0, ADD)
-            tt(sm(8), sm(6), q(3), MUL)
-            ts(sm(9), sm(6), 1.0, ADD)
-            tt(sm(10), q(2), sm(42), SUB)
-            ts(sm(21), sm(42), -1 / 128, MUL, 0.5, ADD)
-            tt(sm(4), sm(7), sm(9), MUL)
-            tt(sm(5), sm(10), sm(8), ADD)
-            tt(sm(43), sm(21), sm(3), MUL)
+            ts(A("DF", 40 * gm, 40 * gm + 32), B("P5", gm, 32), q1(0, gm), SUB, col(13), ADD)
+            red(sm1(11, gm), A("DF", 40 * gm, 40 * gm + 33), MIN, True)
+            ts(B("WS", gm, 1), sm1(11, gm), 32768.0, ALU.is_ge, sm1(3, gm), MUL)
+        tt(A("B2", 0, 23), A("B1", 0, 23), A("B1", 8, 31), ALU.not_equal)
+        lin(sm(4), A("B2", 6, 23, 16), -1.0, 2.0)
+        lin(sm(5), A("B2", 6, 23, 16), 1.0, -2.0)
+        tt(A("CC", 0, 22), A("B2", 0, 22), A("SCL", 0, 22), MUL)
         for b in range(2):
             for gm in range(2):
-                act(B("SPT", 2 * b + gm, 16), B("IOT", b, 16), ACT.Identity, sm1(5, gm) if t else q1(2, gm), sm1(4, gm))
-        for gm in range(2):
-            red(sm1(11, gm), B("DF", gm, 32), MIN, True)
-        tt(sm(44), sm(43), q(1), ADD)
-        ts(sm(17), q(10), 64.0, ALU.is_lt)
-        if t < 2:
-            tt(sm(19), sm(3), q(6), MUL)
-        ts(sm(12), sm(44), 1.0, ADD, 0.0, MAX)
+                lin(B("SPT", 2 * b + gm, 16), B("IOT", b, 16), q1(2, gm), sm1(4, gm))
         tr(A("SPR"), A("SPT"))
-        if t > 0:
-            ts(sm(23), sm(21), 0.0, ALU.is_lt)
-        tt(sm(13), sm(12), q(9), MIN)
         for b in range(2):
-            ts(A("SPU", b, 64, 2), B("SPR", b, 32), 128.0 * par, ADD, float(XSW - 1), MIN)
-        act(A("SP", 0, 1024), IND(A("XS"), A("SPU")))
+            ts(A("SPU", b, 64, 2), B("SPR", b, 32), base, ADD, float(top), MIN)
+        for k in range(2):
+            mov(B("SP", k, 512), IND(win, B("SPU", k, 32)))
+        mm(A("P3", 0, 2), A("TRN"), A("WS"), False, False)
+        mm(A("P3", 6, 8), A("TRS"), A("WS"), False, False)
+        mm(A("P3", 2, 4), A("TRI"), A("WS"), False, False)
+        mm(A("P3", 4, 6), A("TRI"), A("WS"), False, True)
+        if t < 2:
+            tt(A("ES", eb + 7, eb + 24, 16), q(3), q(4), MAX)
+        ts(A("ES", eb + 6, eb + 23, 16), A("P3", 6, 8), 255.0, MIN)
         for gm in range(2):
-            ts(B("WS", gm, 1), sm1(11, gm), 4096.0, ALU.is_ge, sm1(13, gm), MUL)
-        eb = 32 * t
+            pre = A("PRE", 16 * gm, 16 * gm + 6)
+            ts(pre, A("CC", 16 * gm, 16 * gm + 6), B("WS", gm, 1), MIN)
+            ts(A("ES", eb + 16 * gm, eb + 16 * gm + 6), pre, B("P3", gm, 1), MIN, 0.0, MAX)
+        send(B("ES", t, 32), B("EL", t, 32), "e%d" % t, rank - 1 - t)
 
-        def ev(i):
-            return A("ES", eb + i, eb + i + 17, 16)
+        def dd(gm):
+            return A("ES", eb + 16 * gm + 4, eb + 16 * gm + 6)
 
         if t < 2:
-            tt(ev(5), sm(19), q(5), ADD)
-        if t > 0:
-            tt(sm(22), sm(3), sm(23), ALU.not_equal)
-        mm(A("P3", 0, 2), A("TRI"), A("WS"), True, True)
-        tt(sm(29), A("WS"), sm(17), MUL)
-        ts(sm(14), A("WS"), -1.0, MUL, 32.0, ADD)
-        ts(sm(16), A("P3", 0, 2), float(CAP), ALU.is_le)
-        tt(sm(18), A("P3", 0, 2), A("WS"), SUB)
-        ts(sm(45), A("P3", 0, 2), -7.5, ADD)
-        cp(sm(15), A("P3", 0, 2))
-        tt(ev(0), sm(16), A("WS"), MUL)
-        tt(ev(1), sm(16), sm(29), MUL)
-        tt(ev(2), sm(16), A("WS"), MIN)
-        tt(ev(3), sm(16), sm(29), MIN)
-        ts(ev(4), sm(18), 255.0, MIN)
-        send(B("ES", t, 32), "EL", eb, eb + 32, "e%d" % t, rank - 1 - t)
-        ts(sm(46), sm(45), MAGIC / 16, ADD, MAGIC / 16, SUB)
-        mm(A("P6", 0, 14), ident, A("KW", 0, 14), True, False)
-        tt(sm(1), sm(4), sm(22) if t > 0 else sm(3), MUL)
-        for gm in range(2):
-            ts(B("OH", gm), A("UOH"), q1(8, gm), ALU.is_equal, -1.0, MUL)
-        tt(sm(47), sm(15), sm(46), SUB)
-        tt(sm(2), sm(4), sm(1), SUB)
-        for gm in range(2):
-            ts(A("CMP", 32 * gm, 32 * gm + 14), A("K16", 0, 14), sm1(46, gm), ALU.is_gt, sm1(14, gm), MUL)
-            ts(A("CMP", 32 * gm + 16, 32 * gm + 30), A("K16", 0, 14), sm1(46, gm), ALU.is_equal, sm1(14, gm), MUL)
-        for gm in range(2):
-            ts(A("CMP", 64 + 128 * gm, 192 + 128 * gm), B("CR", gm), sm1(47, gm), ALU.is_gt)
-        for gm in range(2):
-            mm(A("P6", 0, 14), B("CB", gm), A("CMP", 32 * gm, 32 * gm + 14), False, False)
-            mm(A("P6", 0, 14), A("CMP", 64 + 128 * gm, 192 + 128 * gm), A("CMP", 32 * gm + 16, 32 * gm + 30), False, gm == 1)
-        tt(A("DD", 1, 4, 2), sm(1), ev(0), MUL)
-        tt(A("DD", 0, 3, 2), sm(2), ev(0), MUL)
-        cp(A("CU", 0, 14), A("P6", 0, 14))
-        mm(A("P5", 0, 4), ident, A("ST", s_old, s_old + 4), True, False)
-        for gm in range(2):
-            mm(B("P5", gm, 2), B("OH", gm), B("DD", gm, 2), False, gm == 1)
-        lb = 240 * t
-        if t < 2:
-            cp(A("CI", 0, 14), A("P6", 0, 14))
-        cp(A("LS", lb, lb + CAP), IND(A("SP"), A("CU", 0, 14)))
-        if t < 2:
-            for h in range(2):
-                act(B("SMK", h, 4), A("P5", 0, 4), ACT.Copy, None, col(14 + h))
-            ts(A("CI", 16, 30), A("CI", 0, 14), 5, ALU.arith_shift_right)
-            mm(A("P3", 0, 4), ident, B("CWB", par, 4), True, False)
+            mm(A("P5", 0, 4), A("IDF"), A("EB"), True, False)
             for gm in range(2):
                 for h in range(2):
-                    o = 16 - 16 * gm + 16 * h
-                    mm(A("P3", h, 4, 2), A("IDW", o, o + 128), B("SMK", 2 * h + gm, 2), False, gm == 1 and h == 1)
-            ab = 72 * (t + 1)
-            cp(A("EU"), A("P3", 0, 4))
-            cp(A("EW"), A("P3", 0, 4))
-            act(A("AS", ab, ab + 64), IND(A("XS"), A("EU")))
-            cp(A("LS", lb + CAP, lb + CAP + 14), A("CI", 16, 30))
+                    ts(B("OW", 2 * gm + h), B("CR", gm), q1(5 + 2 * h, gm), ALU.is_equal, sm1(5, gm), MUL)
+                    mm(A("P5", h, 4, 2), B("OW", 2 * gm + h), dd(gm), False, gm == 1 and h == 1)
+            cp(A("EU"), A("P5", 0, 4))
+            mov(A("EW"), A("P5", 0, 4))
+            mov(A("AS", ab, ab + 64), IND(win, A("EU")))
             tt(A("AS", ab + 64, ab + 66), A("EW", 2, 4), A("EW", 0, 2), SUB)
-            send(A("AS", ab, ab + 72), "AL", ab, ab + 72, "a%d" % (t + 1), rank + 2 + t)
-        send(A("LS", lb, lb + 240), "LL", lb, lb + 240, "l%d" % t, rank - 1 - t)
-        act(A("ST", s_new, s_new + 4), A("P5", 0, 4))
-        s_idle()
+            send(A("AS", ab, ab + 72), A("AL", ab, ab + 72), "a%d" % (t + 1), rank + 2 + t)
+        ts(sm(46), A("P3", 4, 6), MAGIC / 16, ADD, MAGIC / 16, SUB)
+        lin(sm(14), A("WS"), 32.0, -1.0)
+        for gm in range(2):
+            c1, c2, c3 = A("CMP", 32 * gm, 32 * gm + 14), A("CMP", 32 * gm + 16, 32 * gm + 30), A("CMP", 64 + 128 * gm, 192 + 128 * gm)
+            ts(c1, A("K16", 0, 14), sm1(46, gm), ALU.is_gt, sm1(14, gm), MUL)
+            ts(c2, A("K16", 0, 14), sm1(46, gm), ALU.is_equal, sm1(14, gm), MUL)
+            ts(c3, B("CR", gm), sm1(46, gm), ADD, B("P3", 2 + gm, 1), ALU.is_gt)
+            mm(A("P6", 0, 14), B("CB", gm), c1, False, False)
+            mm(A("P6", 0, 14), c3, c2, False, gm == 1)
+        cp(A("CU", 0, 14), A("P6", 0, 14))
+        mov(A("LS", lb, lb + CAP), IND(A("SP"), A("CU", 0, 14)))
+        if t < 2:
+            lin(A("SM", 100, 114), A("P6", 0, 14), -0.484375, 1 / 32)
+            ts(A("LS", lb + CAP, lb + CAP + 14), A("SM", 100, 114), MAGIC / 256, ADD, MAGIC / 256, SUB)
+        send(A("LS", lb, lb + 240), A("LL", lb, lb + 240), "l%d" % t, rank - 1 - t)
+        mm(A("P2", 0, 4), ident, A("ST", s_old, s_old + 4), True, False)
+        for gm in range(2):
+            ts(B("OH", gm), A("UOH"), q1(5, gm), ALU.is_equal, sm1(5, gm), MUL)
+            mm(B("P2", gm, 2), B("OH", gm), dd(gm), False, gm == 1)
+        mov(A("ST", s_new, s_new + 4), A("P2", 0, 4))
 
     def hd(s):
         return A("ST", s, s + 3, 2)
 
-    def own_vars(s, par):
-        cp(A("OWN", 8, 25, 16), hd(s))
-        cp(A("OWN", 9, 26, 16), hd(s + 1))
-        ms(A("OWN", 12, 29, 16), 256.0 * (1 - par))
-        tt(sm(24), hd(s + 1), hd(s), SUB)
-        tr(A("OWR"), A("OWN"))
-        act(B("CT", 1 - par, 32), io_(0, 32), ACT.Identity, col(4), 0.0)
+    def st1(s, gm):
+        return B("ST", s + 2 * gm, 1)
 
-    def arrive(t, s_old, s_new, more):
+    def arrive(t, s_old, s_new):
         par = t % 2
-        eb, lb, c0, ab = 32 * t, 240 * t, U + CAP * t, 72 * (t + 1)
+        eb, lb, c0 = 32 * t, 240 * t, U + CAP * t
 
-        def ev(i):
-            return A("EL", eb + i, eb + i + 17, 16)
+        def ev1(i, gm):
+            return B("EL", eb + i + 16 * gm, 1)
 
-        tr(A("ER"), B("EL", t, 32))
         mm(A("P7", 0, 32), A("WC1"), A("OWR"), True, False)
-        mm(A("P7", 0, 32), A("WC1"), A("ER"), False, True)
-        tt(ev(6), ev(3), sm(24), MUL)
-        cp(B("CT", par, 32), A("P7", 0, 32))
-        tr(A("ER"), B("EL", t, 32))
-        tt(A("MW", 0, 640), IND(A("CT", 0, 64), A("VLU", 0, 40)), A("STC", 0, 640), ADD)
+        tr(B("ER", 0, 32), B("EL", t, 32))
+        mm(A("P7", 0, 32), A("WC1"), B("ER", 0, 32), False, True)
+        mov(B("CT", par, 32), A("P7", 0, 32))
+        tt(A("EL", eb + 13, eb + 30, 16), A("EL", eb + 3, eb + 20, 16), sm(24), MUL)
+        tr(B("ER", 1, 32), B("EL", t, 32))
+        mm(A("P7", 0, 32), A("WC2"), A("OWR"), True, False)
+        mm(A("P7", 0, 32), A("WC2"), B("ER", 1, 32), False, True)
+        mov(A("CT", 64, 96), A("P7", 0, 32))
         lists(t + 1)
-        act(A("LIM", 0, 2), A("AL", ab + 64, ab + 66), ACT.Abs)
-        act(A("LIM", 2, 4), A("LIM", 0, 2), ACT.Identity, col(24))
-        act(A("X", c0, c0 + CAP), A("LL", lb, lb + CAP))
-        for h in range(2):
-            act(B("LD", h, 16), A("E16"), ACT.Copy, None, B("LIM", 2 + h, 1))
-        mm(A("P2", 0, 32), A("WB"), A("LD"), True, True)
+        for lo, hi in ((0, 40), (40, 82), (82, 124), (124, 164)):
+            tt(A("MW", 16 * lo, 16 * hi), IND(A("CT", 0, 64), A("VLU", lo, hi)), A("STC", 16 * lo, 16 * hi), ADD)
+        mov(A("X", c0, c0 + CAP), A("LL", lb, lb + CAP))
         dist_a("X", c0 - 1, CAP + 1, "P6", 0)
         dist_b("X", c0, CAP, "P3", 0, False)
         mm(A("P3", 0, CAP), ident, A("KT"), False, True)
-
-        def nd():
-            act(A("ND"), A("P3", 0, CAP))
-            for k, name in ((1, "WC2"), (2, "WC3")):
-                mm(B("P7", k, 32), A(name), A("OWR"), True, False)
-                mm(B("P7", k, 32), A(name), A("ER"), False, True)
-            act(A("BT"), A("P2", 0, 32))
-            act(A("CT", 64, 96), A("P7", 32, 64))
-            act(A("CT", 104, 136), A("P7", 64, 96))
-
-        scalar_feats(t + 1, {1: nd})
-        tt(A("MW", 640, U), IND(A("CT", 0, 64), A("VLU", 40, 164)), A("STC", 640, U), ADD)
+        mov(A("ND"), A("P3", 0, CAP))
         cp(A("OWU", 0, 14), A("LL", lb + CAP, lb + CAP + 14))
-        ts(sm(25), ev(1), -2.0, MUL)
-        tt(sm(26), ev(0), ev(6), SUB)
         tt(A("MW", c0, c0 + CAP), IND(A("CT", 64, 104), A("OWU", 0, 14)), A("ND"), ADD)
-        tt(A("TG"), IND(A("CT", 104, 144), A("OWU", 0, 14)), A("ND"), ADD)
-        tt(sm(27), sm(25), sm(26), ADD)
-        tt(hd(s_new), hd(s_old), ev(6), ADD)
-        ts(A("TGB"), A("TG"), 0.0, MAX)
+        for gm in range(2):
+            lin(sm1(25, gm), ev1(1, gm), ev1(0, gm), -2.0)
+            lin(st1(s_new, gm), ev1(13, gm), st1(s_old, gm))
+            lin(sm1(26, gm), ev1(13, gm), sm1(25, gm), -1.0)
+            lin(st1(s_new + 1, gm), sm1(26, gm), st1(s_old + 1, gm))
+        relu(A("TGB"), A("MW", c0, c0 + CAP))
         wrap("P6", 14, "TGT", "TGB", CAP)
-
-        def after():
-            cp(A("TU", 16 * t, 16 * t + 14), A("P6", 0, 14))
-            tt(hd(s_new + 1), hd(s_old + 1), sm(27), ADD)
-            cp(IND(A("XS"), A("TU", 16 * t, 16 * t + 14)), A("LL", lb, lb + CAP))
-            more()
-
-        gathers(t + 1, after)
+        tu = A("TU", 16 * t, 16 * t + 14)
+        ts(tu, A("P6", 0, 14), 128.0 * par, ADD)
+        cp(IND(A("XS"), tu), A("LL", lb, lb + CAP))
 
     def numbers(t):
-        ts(A("NUM"), io_(0, CAP), float(U + CAP * t), ADD)
-        cp(IND(A("CS"), A("TU", 16 * t, 16 * t + 14)), A("NUM"))
+        cp(IND(A("CS"), A("TU", 16 * t, 16 * t + 14)), B("NUM", t, CAP))
 
-    def final_lists(par):
+    def final_lists(par, k):
         for b in range(4):
-            tr(B("FT", b, 32), (T.FA[:, b, :], "FA", range(32 * b, 32 * b + 32)))
-        for b in range(4):
-            cp(A("FU", 4 * par + b, 256, 8), B("FT", b, 32))
-
-    def spread():
-        ts(col(11), col(0), 128.0, MUL)
-        ts(col(12), col(0), 128.0, MUL, 2048.0, ADD)
-        ts(col(13), col(1), -4096.0, ADD)
-        ts(col(14), col(1), 16.0, ALU.is_lt)
-        ts(col(15), col(1), 16.0, ALU.is_ge)
-        cp(col(20), A("PI", 0, 1))
-        ms(A("ES"), 0.0)
-        for t in range(3):
-            ms(A("LS", 240 * t + CAP, 240 * t + 240), 0.0)
-        tt(col(16), col(20), col(1), SUB)
-        ts(A("KW"), io_(0, 16), 16.0, MUL, col(0), ADD)
-        ms(A("ST", 0, 8, 2), 32.0)
-        ms(A("ST", 1, 8, 2), 72.0)
-        ts(A("UOH"), io_(0, 128), col(16), SUB)
-        ts(S("WG", 5), g8, -1 / 256, MUL)
-        ts(S("WG", 7), g8, 0.125, MUL)
-        cp(S("WG", 9), g8)
-        ts(A("K16"), io_(0, 16), 16.0, MUL)
-        for gm in range(2):
-            ts(B("OH", gm), A("UOH"), 1.0 - 16 * gm, ADD, 0.0, MAX)
-            ts(B("CB", gm), A("UOH"), 16.0 * gm + 16, ALU.is_lt)
-        cp(S("WK", 10), g8)
-        for par in range(2):
-            for h in range(2):
-                ts(A("CWB", 4 * par + h, 4 * par + 4, 2), A("ONE", 0, 2), col(11 + h), MUL)
-        tt(A("CR"), A("OH"), A("CB"), MUL)
-        ts(A("CWB", 0, 4), A("CWB", 0, 4), 2.0, MUL)
-        ts(A("CWB", 4, 8), A("CWB", 4, 8), 2.0, MUL, 128.0, ADD)
-        ms(A("XS", ZADDR, XSW), 0.0)
-        for i in range(41):
-            cp(A("XS", 32 + i, 8192, 128), A("XG", i, U, 41))
-        ts(A("CB"), A("CR"), 0.0, ALU.is_gt)
-
-    def fill0():
-        ms(col(24), -62.0)
-        tt(col(25), A("E16", 9, 10), A("E16", 10, 11), ADD)
-        ms(A("RW", 37, 38), 600.0)
-        ms(A("RW", 41, 43), -1e5)
-        ms(A("OWN"), 0.0)
-        ts(col(21), A("E16", 13, 14), 64.0, MUL)
-        ts(col(22), A("E16", 6, 7), -1000.0, MUL)
-
-    def idle0():
-        rest_weights()
-        act(S("WC1", 4), S("WC1", 3), ACT.Copy, None, -1.0)
-        act(S("WC1", 8), S("WC1", 7))
-        act(S("WC2", 8), S("WC2", 7))
-        act(S("WC2", 10), S("WC2", 9))
-        act(S("WB", 8), g8)
-        act(S("WB", 15), g8)
-        act(S("WDN", 1), g8)
-        act(S("WC2", 4), S("WC2", 3), ACT.Copy, None, -1.0)
-        act(S("WC3", 7), S("WC2", 7))
-        act(S("WC3", 14), S("WC2", 14))
-        tt(A("RW", 32, 48), A("RW", 32, 48), A("E16"), MUL)
-        ts(A("VLU"), A("P4", 0, 164), 32.0, ADD)
-        ms(A("OWN", 10, 27, 16), 1.0)
-        ts(A("OWN", 11, 28, 16), A("ONE", 0, 2), col(1), MUL)
-        red(col(4), A("RW", 32, 48), ADD)
-        ts(col(23), col(25), -256.0, MUL, col(2), ADD)
-        tt(col(17), col(21), col(22), ADD)
-        own_vars(state(0, 0), 0)
-        act(A("KT"), io_(0, CAP), ACT.Copy, None, col(23))
-        act(A("CT", 96, 104), io_(0, 8), ACT.Identity, col(4), 0.0)
-        act(A("CT", 136, 144), io_(0, 8), ACT.Identity, col(17), 0.0)
-        act(A("MW", U + CAP, W), A("X", U + CAP, W), ACT.Identity, col(4))
+            tr(B("FT", 4 * par + b, 32), (T.FA[:, 4 * k + b, :], "FA", range(128 * k + 32 * b, 128 * k + 32 * b + 32)))
+            ts(A("FU", 4 * par + b, 256, 8), B("FT", 4 * par + b, 32), float(ZADDR), MIN)
 
     def shape(s, k, par):
-        tt(sm(k), hd(s + 1), hd(s), SUB)
-        ts(sm(k + 5), hd(s), col(18 + par), ADD)
-        ts(sm(k + 1), sm(k), 0.0, ALU.is_gt, 2.0, MUL)
-        ts(sm(k + 2), sm(k + 1), -1.0, ADD)
-        tt(sm(k + 3), sm(k), sm(k + 2), MUL)
-        ts(sm(k + 4), sm(k + 3), 1.0, ADD)
-
-    def fill1():
-        ms(A("CS", ZADDR, XSW), -1.0)
-        ts(A("CS", PARTS, PARTS + CAP), io_(0, CAP), float(U + 2 * CAP), ADD)
-
-    def idle1():
-        own_vars(state(1, 1), 1)
-        ts(A("MW", U, U + CAP), A("X", W - CAP, W), col(4), ADD)
-        act(A("OCR", 0, 2048), IND(A("YO", 0, U), A("OCU", 0, 128)))
-        numbers(0)
-        cp(A("OCR", 2048, U), IND(A("YO", 0, U), A("OCU", 128, 164)))
-        for i in range(41):
-            sel(A("CS", 32 + i, 8192, 128), A("OCR", i, U, 41), [[0, 64]], ALU.is_ge, 0.0, 0, 0)
-
-    def even_own():
-        ts(col(18), col(1), 256.0, MUL)
-        ts(col(19), col(1), 256.0, MUL, 128.0, ADD)
-        shape(state(0, 2), 36, 0)
-        ts(sm(28), sm(40), -float(PARTS), ADD)
         for gm in range(2):
-            ts(H("FP", gm), H("I3", 0), sm1(40, gm), ALU.is_lt, -16384.0, MUL)
+            lin(sm1(k, gm), st1(s, gm), st1(s + 1, gm), -1.0)
+        act(sm(k + 1), sm(k), ACT.Sign)
+        act(sm(k + 2), sm(k), ACT.Abs)
+        lin(sm(k + 3), hd(s), col(18 + par))
+
+    lists(0)
+    score(0)
+    wrap("P4", 164, "VLT", "STC", U)
+    ts(A("VLU"), A("P4", 0, 164), 32.0, ADD)
+    choose(0, state(1, 0), state(1, 1))
+    v = S("WQ2", 2)
+    sel(v, v, [[-16, 8]], ALU.not_equal, 256.0, -13, 1)
+    ms(A("XS", ZADDR, XSW), 0.0)
+    spread("XS", "XG")
+    k0 = len(calls)
+    for lo, hi in ((0, 32), (32, 64), (64, 98), (98, 132), (132, 164)):
+        mov(A("OCR", 16 * lo, 16 * hi), IND(A("NO"), A("OCU", lo, hi)))
+    chain(k0, "s")
+    arrive(0, state(0, 0), state(0, 1))
+    s = state(0, 1)
+    mm(A("P5", 0, 4), ident, A("CWB"), True, False)
+    for h in range(2):
+        mul(B("SMK", h, 4), A("ST", s, s + 4), col(14 + h))
         for gm in range(2):
-            tt(H("FP", gm), H("FP", gm), H("I3", 0), ADD)
-        numbers(1)
-
-    def odd_final():
-        shape(state(1, 0), 30, 1)
-        for gm in range(2):
-            ts(H("FB", gm), H("I3", 0), sm1(32, gm), MUL, sm1(35, gm), ADD)
-            ts(H("FC", gm), H("I3", 0), sm1(34, gm), ALU.is_ge, float(ZADDR), MUL)
-        tt(A3("FA", 0, 32), A3("FB", 0, 32), A3("FC", 0, 32), MAX)
-        final_lists(1)
-
-    setup()
-    later_weights()
-    scalar_feats(0, {9: lambda: wrap("P4", 164, "VLT", "SC", U)})
-    tt(A("STC", 0, U), IND(A("DS"), A("SLU")), A("SC"), ADD)
-    gathers(0, spread)
-    choose(0, state(1, 0), state(1, 1), idle0, fill0)
-    arrive(0, state(0, 0), state(0, 1), lambda: None)
-    choose(1, state(0, 1), state(0, 2), idle1, fill1)
-    arrive(1, state(1, 1), state(1, 2), even_own)
-    choose(2, state(1, 2), state(1, 0), odd_final)
-
-    def ev2(i):
-        return A("EL", 64 + i, 64 + i + 17, 16)
-
-    tt(sm(2), ev2(4), sm(28), SUB)
-    tt(sm(0), ev2(3), sm(36), MUL)
-    ts(sm(1), ev2(3), -2.0, MUL, 1.0, ADD)
-    tt(sm(3), ev2(0), sm(40), ADD)
-    tt(sm(4), sm(0), sm(41), ADD)
-    tt(sm(5), sm(1), sm(38), MUL)
+            o = 16 - 16 * gm + 16 * h
+            mm(A("P5", h, 4, 2), A("IDW", o, o + 128), B("SMK", 2 * h + gm, 2), False, gm == 1 and h == 1)
+    mov(A("EB"), A("P5", 0, 4))
+    s = state(1, 1)
+    mov(A("OWN", 8, 25, 16), hd(s))
+    mov(A("OWN", 9, 26, 16), hd(s + 1))
+    gfill(A("OWN", 12, 29, 16))
     for gm in range(2):
-        act(H("FP", gm), H("FP", gm), ACT.Identity, sm1(2, gm))
-        ts(H("FC", gm), H("I3", 0), sm1(3, gm), ALU.is_ge, float(ZADDR), MUL)
+        lin(sm1(24, gm), st1(s, gm), st1(s + 1, gm), -1.0)
+    tr(A("OWR"), A("OWN"))
+    score(1)
+    lin(B("CT", 0, 32), io_(0, 32), col(4), 0.0)
+    gfill(A("MW", U, U + CAP), 600)
+    choose(1, state(0, 1), state(0, 2))
+    numbers(0)
+    spread("CS", "OCR")
+    arrive(1, state(1, 1), state(1, 2))
+    shape(state(0, 2), 36, 0)
+    lin(sm(28), sm(38), float(PARTS - 1), -1.0)
+    mul(sm(29), sm(37), -2.0)
+    lin(sm(27), sm(38), 16384.0, 16384.0)
+    mul(sm(35), sm(38), -16384.0)
     for gm in range(2):
-        ts(H("FB", gm), H("I3", 0), sm1(5, gm), MUL, sm1(4, gm), ADD)
-    tt(A3("FC", 0, 32), A3("FC", 0, 32), A3("FP", 0, 32), MAX)
-    tt(A3("FA", 0, 32), A3("FB", 0, 32), A3("FC", 0, 32), MAX)
-    final_lists(0)
-    act(A("XS", PARTS, PARTS + CAP), A("LL", 480, 480 + CAP))
+        lin(F(0, gm), i3, sm1(28, gm))
+        act(F(1, gm), i3, ACT.Relu, sm1(27, gm), -16384.0)
+    tt(F(2), F(0), F(1), SUB)
+    score(2)
+    numbers(1)
+    choose(2, state(1, 2), state(1, 0))
+    shape(state(1, 0), 30, 1)
+    mul(sm(34), sm(32), -16384.0)
+    for gm in range(2):
+        lin(F(0, gm), i3, sm1(33, gm), sm1(31, gm))
+        lin(F(1, gm), i3, sm1(34, gm), 16384.0)
+    tt(F(3), F(0), F(1), MAX)
+    final_lists(1, 3)
+
+    def ev2(i, gm):
+        return B("EL", 64 + i + 16 * gm, 1)
+
+    for gm in range(2):
+        lin(sm1(7, gm), ev2(3, gm), sm1(39, gm), sm1(36, gm))
+        lin(sm1(8, gm), ev2(3, gm), sm1(37, gm), sm1(29, gm))
+        lin(sm1(9, gm), ev2(0, gm), sm1(35, gm), -16384.0)
+        lin(F(2, gm), F(2, gm), ev2(6, gm))
+        lin(F(4, gm), i3, sm1(7, gm), sm1(8, gm))
+        lin(F(5, gm), i3, sm1(9, gm), 16384.0)
+    tt(F(5), F(5), F(2), MAX)
+    tt(F(6), F(4), F(5), MAX)
+    final_lists(0, 6)
+    mov(A("XS", PARTS, PARTS + CAP), A("LL", 480, 480 + CAP))
     nout = [0]
 
-    def store(dst, src):
+    def store(dst, src, late):
         nout[0] += 16
-        sync("y", [src], [], "out0", 10 ** 6)
-        g.sync.dma_start(dst, src[0]).then_inc(T.sem.out0, 16)
+        note("y", lambda: g.sync.dma_start(dst, src[0]).then_inc(T.sem.out0, 16), [src], [], 0.05, "out0", 10 ** 6, late)
 
-    for c in range(8):
-        (cp if c % 2 else act)(B("FD", c, 512), IND(A("XS"), B("FU", c, 32)))
-        store(T.y[:, 512 * c:512 * c + 512], B("FD", c, 512))
+    k0 = len(calls)
     for c in range(4):
-        lo, hi = 1024 * c, 1024 * c + 1024
-        (cp if c % 2 else act)(A("YO", lo, hi), IND(A("CS"), B("FU", c, 64)))
-        store(T.yo[:, lo:hi], (T.YO[0:128:16, lo:hi], "YO", range(lo, hi)))
+        mov(B("YO", c, 1024), IND(A("CS"), B("FU", c, 64)))
+        store(T.yo[:, 1024 * c:1024 * c + 1024],
+              (T.YO[0:128:16, 1024 * c:1024 * c + 1024], "YO", range(1024 * c, 1024 * c + 1024)), 1.8)
+    for c in range(8):
+        mov(B("FD", c, 512), IND(A("XS"), B("FU", c, 32)))
+        store(T.y[:, 512 * c:512 * c + 512], B("FD", c, 512), 2.6)
+    chain(k0, "s")
+
+    if not ORDER:
+        ORDER.extend(schedule(calls, lanes))
+    cnt = {"v": 0, "s": 0, "t": 0, "g": 0}
+    seen = {k: {} for k in eng}
+    acc = {}
+
+    def wait(q, sem, val):
+        if seen[q].get(sem, 0) < val:
+            eng[q].wait_ge(T.sem[sem], val)
+            seen[q][sem] = val
+
+    for t in range(3):
+        for name, n, sem, src in (("AL", 72, "a", rank - 1 - t), ("EL", 32, "e", rank + 1 + t), ("LL", 240, "l", rank + 1 + t)):
+            acc.setdefault(name, []).append([bits(range(n * t, n * t + n), True), True, sem + str(t),
+                                             len(engines(T.cores[src % n_ranks], core)), "r"])
+    for i, qn in ORDER:
+        calls[i]["q"] = qn
+    for i, _ in ORDER:
+        c = calls[i]
+        qn, items, need = c["q"], touched(c), {}
+        if c["dma"]:
+            sem, val = c["sem"], c["val"]
+        else:
+            cnt[qn] += c["n"]
+            sem, val = "q" + qn, cnt[qn]
+        for name, m, w, psum in items:
+            for e in acc.get(name, []):
+                if e[0] & m and (w or e[1] or (psum and e[4] != qn)) and not (qn == "t" and e[4] == "t"):
+                    need[e[2]] = max(need.get(e[2], 0), e[3])
+        for s in need:
+            wait(qn, s, need[s])
+        for name, m, w, psum in items:
+            lst = acc.setdefault(name, [])
+            lst[:] = [e for e in lst if not ((w or (e[4] == qn and not e[1] and not c["dma"])) and e[0] & ~m == 0)]
+            lst.append([m, w, sem, val, qn])
+        done = c["fn"]()
+        if not c["dma"]:
+            for ins in (done if c["n"] > 1 else [done]):
+                ins.then_inc(T.sem["q" + qn], 1)
     g.sync.wait_ge(T.sem.out0, nout[0])
     g.wait_ge(T.sem.loc, sent[0])
     for k in ("v", "s", "t", "g"):

@@ -3,27 +3,32 @@ from concourse.mybir import AluOpType, AxisListType, ActivationFunctionType
 ALU = AluOpType
 ACT = ActivationFunctionType
 U, CAP, W = 2624, 224, 4096
-PARTS, ZADDR, XSW = 8576, 8896, 8912
+XSW, FW = 8544, 2640
 MAGIC = 3221225472.0
-CYC, GAT, SCA, HOP, FAR = 0.00083, 1.4, 3.0, 0.12, 1.9
-TRIES, SHAKE, SPARE, TEMP = 1200, 2.0, 0.1, 0.2
+CASES = ((0.00098, 1.5, 3.6, 0.21, 0.9, 2.6, 1.0, 0.06), (0.00083, 1.3, 2.8, 0.18, 0.8, 2.3, 0.8, 0.1),
+         (0.0012, 1.15, 3.0, 0.16, 0.65, 1.9, 0.8, 0.03))
+TRIES, SHAKE, SPARE, TEMP, TURNS, TEMP2 = 6500, 3.0, 0.1, 0.6, 3000, 0.1
 BF, F32, I32, U16 = "bfloat16", "float32", "int32", "uint16"
 SCRATCH = {}
 for _d, _l in (
-        (BF, dict(X=W, XG=U + 8, AD=U + 8, MW=W, MG=W + 144, FD=W, XS=XSW, IDW=160, NEGI=128, I256=128, INEG=128,
+        (BF, dict(X=W + 16, XG=U + 8, AD=U + 8, MW=W, MG=W + 144, FD=W, XS=XSW, IDW=160, NEGI=128, I256=128, INEG=128,
                   BLK=128, WZ=128, WA=512, WB=512, WC=464, HALF=128, N256=128, N1K=128, SELW=64, B32=128, TGT=144, G=768,
-                  RH=256, ZR=896, CQ=128, CB=256, CR=256, K16=16, TRI=128, TRN=128, TRS=128, UOH=128, WR=256, WRG=256,
+                  RH=256, ZR=896, CQ=128, CB=256, UW=512, K16=16, TRI=128, TRN=128, TRS=128, UOH=128, WR=256, WRG=256,
                   E16=16, IOT=256, NKK=128, ONE=128, KT=CAP, KW=16, CWB=4, NJ=72, AS=216, AL=216, ES=96, EL=96, LS=720,
                   LL=720, XH=64, MBS=32, GD=64, WS=2, CMP=320, SP=1024 + CAP, OH=256, OW=512, ST=24, SMK=8, OWN=32,
-                  OWR=32, ER=64, TGB=CAP, B1=32, B2=32, SCL=32, CC=32, PRE=32)),
-        (F32, dict(STC=W, CS=XSW, YO=W, NO=U, OCR=U, SRC=U // 2, DS=U, B82=176, COL=40, RW=32, SM=120, TQ=64, DF=80,
-                   SPT=64, SPR=64, EW=4, EB=4, CT=104, ND=CAP, NUM=2 * CAP, FT=256, IDF=128, VLT=144)),
+                  OWR=32, ER=64, TGB=CAP, B1=32, B2=32, SCL=32, CC=32, PRE=32, I16K=128, ITB=256, WN=1536, VV=64, VR=64,
+                  LH=16)),
+        (F32, dict(STC=W, FS=FW, OCT=192, GN=512, JF=128, BASE=32, WCL=16, NA=1024, SRC=U // 2, DS=U, B82=176, COL=40,
+                   RW=32, SM=120, TQ=64, DF=80, SPT=64, SPR=64, EW=4, EB=4, CT=104, ND=CAP, IDF=128, VLT=144)),
         (I32, dict(OCI=164, CDI=256, MI=256, MJ=256, PI=4)),
-        (U16, dict(OCU=164, VLU=164, MU=256, OFF=4, CU=16, SPU=64, EU=4, OWU=16, TU=32, FU=256))):
+        (U16, dict(OCU=164, VLU=164, MU=256, OFF=4, CU=16, SPU=64, EU=4, OWU=16, TU=32, FU=256, NU=32))):
     for _k in _l:
         SCRATCH[_k] = ("sbuf", [128, _l[_k]], _d)
-SCRATCH["I3"] = ("sbuf", [128, 4, 16], F32)
-SCRATCH["FA"] = ("sbuf", [128, 28, 32], F32)
+SCRATCH["OC3"] = ("sbuf", [128, 6, 32], F32)
+SCRATCH["OC4"] = ("sbuf", [128, 12, 16], F32)
+SCRATCH["YT"] = ("sbuf", [128, 8, 32], F32)
+SCRATCH["YU"] = ("sbuf", [128, 16, 16], F32)
+SCRATCH["D1"] = ("dram", [8, 3088], F32)
 for _k in range(8):
     SCRATCH["P%d" % _k] = ("psum", [128, 512], F32)
 PART = dict(WDL=("WA", 0, 128, 4), WDR=("WA", 128, 128, 4), WDZ=("WA", 256, 128, 4), WDN=("WA", 384, 128, 4),
@@ -31,7 +36,7 @@ PART = dict(WDL=("WA", 0, 128, 4), WDR=("WA", 128, 128, 4), WDZ=("WA", 256, 128,
             WG1=("WC", 0, 128, 5), WG2=("WC", 128, 128, 5), WK=("WC", 256, 128, 5), WM=("WC", 384, 48, 5),
             WF=("WC", 432, 32, 5))
 SEMAPHORES = ["qv", "qs", "qt", "qg", "ld0", "ld1", "ld2", "ld3", "ld4", "ld6", "loc", "loc0", "a0", "a1", "a2",
-              "e0", "e1", "e2", "l0", "l1", "l2", "out0", "fill"]
+              "e0", "e1", "e2", "l0", "l1", "l2", "out0", "fill", "d1", "fs"]
 ORDER = []
 
 
@@ -73,21 +78,48 @@ def schedule(calls, lanes):
         pred[i] |= set(c["after"])
         pred[i].discard(i)
 
-    def gap(a, b):
-        return calls[a]["late"] + (0.0 if calls[a]["q"] == "t" == calls[b]["q"] else HOP)
+    def price(c, q, case):
+        fixed, cycles, gathered, scattered, sends = c["cost"][q]
+        return fixed * (1 if q == "y" else case[0] / 0.00083) + (case[7] if q == "s" and cycles else 0) + \
+            (cycles + gathered * case[1] + scattered * case[2]) * case[0] + sends * case[4]
 
-    cost, queue = [c["cost"] for c in calls], [c["q"] for c in calls]
-    before = [[(p, gap(p, i)) for p in pred[i]] for i in range(n)]
+    def gap(a, b, case):
+        return calls[a]["late"] + calls[a]["cost"][calls[a]["q"]][4] * case[5] + \
+            (0.0 if calls[a]["q"] == "t" == calls[b]["q"] else case[3])
+
+    prices = [[{q: price(c, q, case) for q in c["cost"]} for c in calls] for case in CASES]
+    waits = [[[(p, gap(p, i, case)) for p in pred[i]] for i in range(n)] for case in CASES]
+    queue = [c["q"] for c in calls]
+    cost, before = [prices[0][i][queue[i]] for i in range(n)], waits[0]
     after = [[] for _ in calls]
     for i in range(n):
         for p, d in before[i]:
             after[p].append((i, d))
+    tails = [i for i in range(n) if not after[i]]
 
-    def place(turn, deps, lead, choose=False):
+    def span(order, k):
+        end, why, last, wk, pk = [0.0] * n, [-1] * n, {}, waits[k], prices[k]
+        for i in order:
+            q = queue[i]
+            p0 = last.get(q, -1)
+            t = end[p0] if p0 >= 0 else 0.0
+            for p, d in wk[i]:
+                if end[p] + d > t:
+                    t, p0 = end[p] + d, p
+            end[i], why[i], last[q] = t + pk[i][q], p0, i
+        i = max(tails, key=lambda i: end[i] + late[i])
+        total, pairs = end[i] + late[i], []
+        while why[i] >= 0:
+            if why[i] not in pred[i]:
+                pairs.append((why[i], i))
+            i = why[i]
+        return total, pairs
+
+    def place(turn, deps, lead, choose=()):
         start, busy = [0.0] * n, {q: ([], []) for q in "vstgy"}
         for i in turn:
             t0, found = max([start[p] + cost[p] + d for p, d in deps[i]] + [lead[i]]), None
-            for q, c in (calls[i]["alt"] if choose and calls[i]["alt"] else ((queue[i], cost[i]),)):
+            for q, c in (prices[0][i].items() if i in choose else ((queue[i], cost[i]),)):
                 t, (begins, ends) = t0, busy[q]
                 lo, hi = 0, len(ends)
                 while lo < hi:
@@ -96,7 +128,7 @@ def schedule(calls, lanes):
                 while lo < len(ends) and begins[lo] < t + c - 1e-9:
                     t = max(t, ends[lo])
                     lo += 1
-                end = t + c + (SPARE if q == "v" else 0)
+                end = t + c + (choose.get(i, 0) if q == "v" and choose else 0)
                 if found is None or end < found[0]:
                     found = (end, t, q, c, lo)
             _, t, queue[i], cost[i], lo = found
@@ -119,28 +151,112 @@ def schedule(calls, lanes):
                     key[i] = key[p] + 1e-6
         return sorted(range(n), key=lambda i: key[i])
 
-    seed = [12345]
+    seed = [777]
 
     def rand():
         seed[0] = (seed[0] * 1103515245 + 12345) % 2147483648
         return seed[0] / 2147483648
 
-    def polish(start):
-        back = place(sorted(range(n), key=lambda i: -start[i] - cost[i]), after, late)
-        start = place(sorted(range(n), key=lambda i: -back[i] - cost[i]), before, zero, True)
-        return max(start[i] + cost[i] + late[i] for i in range(n)), start, list(queue), list(cost)
+    def worth(order, start=None):
+        spans = [span(order, k) for k in range(len(CASES))]
+        value = sum(case[6] * s[0] for case, s in zip(CASES, spans))
+        return value, start or order, list(queue), list(cost), [s[1] for s in spans]
 
-    best = now = polish(place(in_turn([-x for x in prio]), before, zero))
+    def by_start(start):
+        return sorted(range(n), key=lambda i: start[i])
+
+    def polish(start, choose):
+        back = place(sorted(range(n), key=lambda i: -start[i] - cost[i]), after, late)
+        return place(sorted(range(n), key=lambda i: -back[i] - cost[i]), before, zero, choose)
+
+    start = place(in_turn([-x for x in prio]), before, zero)
+    best = None
+    for k in range(6):
+        start = polish(start, {i: SPARE for i in range(n)})
+        new = worth(by_start(start), start)
+        if best is None or new[0] < best[0]:
+            best = new
+    now = best
     for k in range(TRIES):
         queue[:], cost[:] = now[2], now[3]
-        t0, width, size = rand() * now[0], 2 + 6 * rand(), SHAKE * rand()
-        key = [s + (size * (rand() - 0.5) if t0 - width < s < t0 else 0) for s in now[1]]
-        new = polish(place(in_turn(key), before, zero, True))
+        key, some = list(now[1]), {}
+        if rand() < 0.7:
+            pairs = now[4][int(rand() * len(CASES))]
+            j = int(rand() * len(pairs))
+            a, b = pairs[j]
+            kind = rand()
+            if kind < 0.35:
+                a = pairs[min(len(pairs) - 1, j + int(6 * rand() ** 2))][0]
+                key[b] = key[a] - 1e-4
+                for p, _ in before[b]:
+                    key[p] = min(key[p], key[b] - 1e-4)
+            elif kind < 0.7:
+                b = pairs[max(0, j - int(6 * rand() ** 2))][1]
+                key[a] = key[b] + 1e-4 + rand() ** 2
+            else:
+                a = a if rand() < 0.5 else b
+                some = {a: -9 if queue[a] == "s" else 9}
+        else:
+            t0, width, size = rand() * max(now[1]), 0.5 + 5 * rand(), SHAKE * rand()
+            for i in range(n):
+                if t0 - width < key[i] < t0:
+                    if rand() < 0.3:
+                        some[i] = 0.4 * rand() - 0.1
+                    if rand() < 0.2:
+                        key[i] += size * (rand() - 0.5)
+        start = place(in_turn(key), before, zero, some)
+        if rand() < 0.03:
+            start = polish(start, some)
+        new = worth(by_start(start), start)
         if new[0] < now[0] + TEMP * rand() * (1 - k / TRIES):
             now = new
         if new[0] < best[0]:
             best = new
-    return [(i, best[2][i]) for i in sorted(range(n), key=lambda i: best[1][i])]
+    queue[:] = best[2]
+    best = now = worth(by_start(best[1]))
+    for k in range(TURNS):
+        queue[:] = now[2]
+        order = list(now[1])
+        pairs = now[4][int(rand() * len(CASES))]
+        j = int(rand() * len(pairs))
+        a, b = pairs[j]
+        kind = rand()
+        if kind < 0.75:
+            if kind < 0.35:
+                a = pairs[min(len(pairs) - 1, j + int(5 * rand() ** 3))][0]
+            else:
+                b = pairs[max(0, j - int(5 * rand() ** 3))][1]
+            ia, ib = order.index(a), order.index(b)
+            piece = order[ia:ib + 1]
+            if kind < 0.35:
+                moved = {b}
+                for i in reversed(piece):
+                    if i in moved:
+                        moved |= pred[i]
+                order[ia:ib + 1] = [i for i in piece if i in moved] + [i for i in piece if i not in moved]
+            else:
+                moved = {a}
+                for i in piece:
+                    if pred[i] & moved:
+                        moved.add(i)
+                order[ia:ib + 1] = [i for i in piece if i not in moved] + [i for i in piece if i in moved]
+        else:
+            a = a if rand() < 0.5 else b
+            if len(prices[0][a]) < 2:
+                continue
+            queue[a] = "v" if queue[a] == "s" else "s"
+            if rand() < 0.5:
+                ia = order.index(a)
+                near = [i for i in order[max(0, ia - 25):ia + 25] if i != a and queue[i] == queue[a] and len(prices[0][i]) > 1]
+                if near:
+                    i = near[int(rand() * len(near))]
+                    queue[i] = "v" if queue[i] == "s" else "s"
+        new = worth(order)
+        if new[0] < now[0] + TEMP2 * rand() * (1 - k / TURNS):
+            now = new
+        if now[0] < best[0]:
+            best = now
+    return [(i, best[2][i]) for i in best[1]]
 
 
 def rank_program(g, core, T, topo):
@@ -165,8 +281,8 @@ def rank_program(g, core, T, topo):
         n = SCRATCH[name][1][2]
         return (T[name][:, b0:b1, c0:c1], name, [n * b + c for b in range(b0, b1) for c in range(c0, c1)])
 
-    def F(k, gm=None):
-        return A3("FA", 0, 32, 4 * k, 4 * k + 4) if gm is None else A3("FA", 16 * gm, 16 * gm + 16, 4 * k, 4 * k + 4)
+    def row3(name, b):
+        return (T[name][:, b, :], name, range(32 * b, 32 * b + 32))
 
     def B(name, k, n=128):
         return A(name, n * k, n * k + n)
@@ -181,26 +297,28 @@ def rank_program(g, core, T, topo):
         return (win[0].indirect(off[0]), win[1], win[2], off)
 
     def note(q, fn, reads, writes, cost, sem=None, val=0, late=0.0, any_order=None, far=(), after=(), alt=None):
-        calls.append(dict(q=q, fn=fn, r=[a for a in reads if isinstance(a, tuple)], w=writes, cost=cost, sem=sem, val=val,
-                          dma=sem is not None, late=late, any=any_order, far=far, after=after, alt=alt, n=1))
+        calls.append(dict(q=q, fn=fn, r=[a for a in reads if isinstance(a, tuple)], w=writes, cost=alt or {q: cost}, sem=sem,
+                          val=val, dma=sem is not None, late=late, any=any_order, far=far, after=after, alt=alt, n=1))
         return len(calls) - 1
 
-    def price(reads, o, rate=None):
+    def price(reads, o, rate=None, n=1):
         aps = [a for a in reads if isinstance(a, tuple)] + [o]
         ind = [a for a in aps if len(a) > 3]
         if ind:
-            return (0.065 if rate else 0.05) + 16 * len(ind[0][3][2]) * (SCA if ind[0] is o else GAT) * CYC
+            k = 16 * len(ind[0][3][2])
+            return ((0.065 if rate else 0.05) * n, 0, 0 if ind[0] is o else k, k if ind[0] is o else 0, 0)
         if rate is None:
             rate = 0.5 if all(SCRATCH[a[1]][2] in (BF, U16) or len(a[2]) == 1 for a in aps) else 1
-        return 0.03 + max(64, len(reads[0][2] if reads else o[2]) * rate) * CYC
+        return (0.005, max(64, len(reads[0][2] if reads else o[2]) * rate), 0, 0, 0)
 
     def op(q, fn, reads, o, rate=None):
         note(q, fn, reads, [o], price(reads, o, rate))
 
-    def either(fs, fv, reads, o):
+    def either(fs, fv, reads, o, n=1):
         k = len(calls)
-        cs, cv = price(reads, o, 1), price(reads, o)
-        note("s", lambda: fs() if calls[k]["q"] == "s" else fv(), reads, [o], cs, alt=(("s", cs), ("v", cv)))
+        note("s", lambda: fs() if calls[k]["q"] == "s" else fv(), reads, [o], None,
+             alt={"s": price(reads, o, 1, n), "v": price(reads, o, None, n)})
+        calls[k]["n"] = n
         return calls[k]
 
     def ap(x):
@@ -254,15 +372,16 @@ def rank_program(g, core, T, topo):
             if group:
                 group[0] -= 1
             return g.tensor.matmul(o[0], l[0], (part() if part else r)[0], start, group[0] == 0 if group else stop)
-        cost = max(min(64, len(l[2])), len(r[2])) * (4 if SCRATCH[l[1]][2] == F32 else 1) * CYC / 2
-        note("t", fn, [l, r], [o], cost, any_order=group and group[1])
+        cost = max(min(64, len(l[2])), len(r[2])) * (4 if SCRATCH[l[1]][2] == F32 else 1) * 0.55
+        note("t", fn, [l, r], [o], (0, cost, 0, 0, 0), any_order=group and group[1])
 
     def iota(o, pat, base, cm, small=True):
         note("g", lambda: g.iota(o[0], pat, base, cm, allow_small_or_imprecise_dtypes=True) if small else
-             g.iota(o[0], pat, base, cm), [], [o], 0.13 + 2 * len(o[2]) * CYC)
+             g.iota(o[0], pat, base, cm), [], [o], (0.13, 2 * len(o[2]), 0, 0, 0))
 
     def sel(o, i, pat, cmp, fill, base, cm):
-        note("g", lambda: g.affine_select(o[0], i[0], pat, cmp, float(fill), base, cm), [i], [o], 0.17 + 2 * len(o[2]) * CYC)
+        note("g", lambda: g.affine_select(o[0], i[0], pat, cmp, float(fill), base, cm), [i], [o],
+             (0.17, 2 * len(o[2]), 0, 0, 0))
 
     def gfill(o, v=0):
         iota(o, [[0, len(o[2])]], v, 0)
@@ -272,7 +391,7 @@ def rank_program(g, core, T, topo):
             mm(A(pb, 0, n), A(name, 16 - r, 144 - r), A(src, r, width, 16), r == 0, r == 15)
 
     def load(q, o, src, sem, late):
-        note(q, lambda: eng[q].dma_start(o[0], src).then_inc(T.sem[sem], 16), [], [o], 0.05, sem, 16, late)
+        note(q, lambda: eng[q].dma_start(o[0], src).then_inc(T.sem[sem], 16), [], [o], (0.05, 0, 0, 0, 0), sem, 16, late)
 
     def engines(src, dst):
         return topo.engines(src, dst)[:8]
@@ -284,7 +403,7 @@ def rank_program(g, core, T, topo):
         if loc == "loc":
             sent[0] += len(es)
         return note("g", lambda: g.remote_dma(dst[0], src[0], T.sem[sem], T.sem[loc], pid, rid, sum(1 << e for e in es)),
-                    [src], [], 0.5 + first, loc, 10 ** 6, FAR - 0.5, far=[dst])
+                    [src], [], (first, 0, 0, 0, 1), loc, 10 ** 6, far=[dst])
 
     def chain(first, qn):
         lanes.append([k for k in range(first, len(calls)) if calls[k]["q"] == qn])
@@ -308,7 +427,6 @@ def rank_program(g, core, T, topo):
     ident = A("IDW", 16, 144)
     g8 = S("BLK", 0)
     one_row = R("ONE")
-    i3 = A3("I3", 0, 16, 0, 4)
 
     load("y", A("OCI"), T.oc[:, :], "ld0", 2.7)
     load("y", A("X", 0, 1312), T.x[:, 0:1312], "ld1", 3.7)
@@ -407,15 +525,16 @@ def rank_program(g, core, T, topo):
     mov(A("TGT"), A("P7", 0, 144))
     side1 = ((8, -1), (9, -1), (0, -1), (1, 2), (10, 0.5), (3, -1))
     side2 = ((9, 1), (8, -1), (0, -1), (10, 2.5), (6, -2))
+    joint = ((7, 1), (14, 1))
     weights(6, 512, [(wc("WQ1", c), ((f, 1),)) for c, f in ((4, 4), (5, 3), (6, 3), (12, 8), (13, 8), (14, 15))] + [
         (wc("WQ2", 0), ((13, 131072),)), (wc("WQ2", 1), size), (wc("WQ2", 2), ((13, 82), (7, 1), (14, 1), (15, -2))),
-        (wc("WQ2", 3), low), (wc("WQ2", 4), high), (wc("WQ2", 5), ((13, 1),)), (wc("WQ2", 7), ((13, 1),)),
+        (wc("WQ2", 3), low), (wc("WQ2", 4), high), (wc("WQ2", 5), ((13, 1),)),
         (wc("WC1", 3), side1), (wc("WC1", 4), neg(side1)), (wc("WC1", 5), ((8, 1), (10, 1), (3, -1), (12, -1))),
         (wc("WC1", 6), ((9, -1), (10, 1), (2, -1), (3, 1))), (wc("WC1", 7), ((8, -1), (1, 1))), (wc("WC1", 8), ((3, 1),)),
-        (wc("WC1", 9), ((7, 1), (9, -256))), (wc("WC1", 10), ((9, -256),)), (wc("WC1", 11), ((7, 1), (8, 256))),
+        (wc("WC1", 9), joint + ((9, -256),)), (wc("WC1", 10), ((9, -256),)), (wc("WC1", 11), joint + ((8, 256),)),
         (wc("WC1", 12), ((8, 256),)), (wc("WC1", 14), ((8, 1), (1, -1))),
         (wc("WC2", 3), side2), (wc("WC2", 4), neg(side2)), (wc("WC2", 6), ((10, 2), (0, -1), (6, -1))),
-        (wc("WC2", 7), ((9, 1), (8, -1), (10, 1), (6, -1))), (wc("WC2", 11), ((7, 1), (6, 256))),
+        (wc("WC2", 7), ((9, 1), (8, -1), (10, 1), (6, -1))), (wc("WC2", 11), joint + ((6, 256),)),
         (wc("WC2", 12), ((6, 256),)), (wc("WC2", 13), ((11, 1),)), (wc("WC2", 14), ((8, 1), (13, 1))),
         (wc("WC2", 15), ((9, 1), (8, -1), (10, -255), (6, -1), (3, 256)))])
     mov(A("WB", 0, 256), A("P6", 0, 256))
@@ -438,11 +557,7 @@ def rank_program(g, core, T, topo):
             g.sync.dma_start(T[name][:, c:c + n], T[name][:, c0:c0 + n]).then_inc(T.sem.fill, 16)
 
     note("y", fill_twins, [A("STC", U, U + 368), A("MW", U + CAP, U + CAP + 416)],
-         [A(name, c, c + n) for name, c, n, _ in twins], 0.25, "fill", 16 * len(twins), 2.5)
-    k0 = len(calls)
-    for c in range(0, U, 328):
-        iota(A("NO", c, c + 328), [[1, 328]], c, 0)
-    chain(k0, "g")
+         [A(name, c, c + n) for name, c, n, _ in twins], (0.25, 0, 0, 0, 0), "fill", 16 * len(twins), 3.5)
     k0 = len(calls)
     mul(R("ZR", 768, 896), one_row, -62.25)
     mul(col(11), col(0), 128.0)
@@ -463,7 +578,6 @@ def rank_program(g, core, T, topo):
     gfill(A("B32"))
     gfill(col(26), -4)
     gfill(R("CQ", 5, 118, 16), 1)
-    gfill(R("CQ", 7, 120, 16), -15)
     mul(R("CQ", 1, 114, 16), R("ONE", 0, 8), 1.25)
     for gm in range(2):
         sel(B("WRG", gm), A("ONE"), [[-32, 4], [0, 32]], ALU.is_ge, 0.0, -16 * gm, 1)
@@ -481,11 +595,13 @@ def rank_program(g, core, T, topo):
     iota(A("K16"), [[16, 16]], 0, 0)
     iota(A("ST", 0, 8), [[0, 4], [40, 2]], 32, 0)
     iota(B("OW", 1), [[0, 8], [1, 16]], 1, 0)
-    for o, i, name, fill in ((B("OW", 0), A("ONE"), "CB", 0.0), (B("OW", 1), B("OW", 1), "CR", -100.0)):
+    for o, i, name, fill in ((B("OW", 0), A("ONE"), "CB", 0.0), (B("OW", 1), B("OW", 1), "UW", -100.0)):
         sel(o, i, [[-32, 4], [0, 32]], ALU.is_ge, fill, 0, 1)
         sel(o, o, [[32, 4], [0, 32]], ALU.is_ge, fill, 31, -1)
         for gm in range(2):
-            sel(B(name, gm), o, [[0, 4], [1, 2], [0, 16]], ALU.is_equal, fill, -gm, 0)
+            sel(B(name, gm if name == "CB" else 2 * gm), o, [[0, 4], [1, 2], [0, 16]], ALU.is_equal, fill, -gm, 0)
+    for gm in range(2):
+        lin(B("UW", 2 * gm + 1), B("UW", 2 * gm), 16.0)
     gfill(A("OWN"))
     gfill(sm(24), 40)
     for c, v in ((8, 32), (9, 72), (10, 1), (12, 256)):
@@ -493,7 +609,6 @@ def rank_program(g, core, T, topo):
     mul(A("OWN", 11, 28, 16), A("ONE", 0, 2), col(1))
     tr(A("OWR"), A("OWN"))
     ts(col(14), col(1), 16.0, ALU.is_lt)
-    iota(i3, [[16, 4], [1, 16]], 0, 0)
     lin(col(15), col(14), 1.0, -1.0)
     lin(col(25), e16(9), e16(10))
     mul(col(21), e16(5), 600.0)
@@ -509,11 +624,7 @@ def rank_program(g, core, T, topo):
     for h in range(2):
         mul(col(29 + h), col(11 + h), 2.0)
         mul(A("CWB", h, 4, 2), A("ONE", 0, 2), col(29 + h))
-    mul(col(18), col(1), 256.0)
-    lin(col(19), col(1), 128.0, 256.0)
-    gfill(A("CS", ZADDR, XSW), -1)
-    iota(A("CS", PARTS, PARTS + CAP), [[1, CAP]], U + 2 * CAP, 0)
-    iota(A("NUM"), [[1, 2 * CAP]], U, 0)
+    gfill(A("X", W, W + 16))
     chain(k0, "g")
 
     def dist_a(src, c0, n, pb, d0):
@@ -531,36 +642,40 @@ def rank_program(g, core, T, topo):
         for bit in range(2):
             for qq in range(4):
                 mm(A("P4", 4 * bit + qq, 256, 8), A("WZ"), A("AL", b + 32 * bit, b + 32 * bit + 32), True, True)
-        for lo, hi in ((0, 96), (96, 256)):
-            tt(A("MI", lo, hi), A("CDI", lo, hi), A("P4", lo, hi), ADD)
-            ts(A("MJ", lo, hi), A("MI", lo, hi), 4095, ALU.bitwise_and)
-            cp(A("MU", lo, hi), A("MJ", lo, hi))
+        steps = []
+        for f in (lambda a, b: g.vector.tensor_tensor(T.MI[:, a:b], T.CDI[:, a:b], T.P4[:, a:b], ADD),
+                  lambda a, b: g.vector.tensor_scalar(T.MJ[:, a:b], T.MI[:, a:b], 4095, None, ALU.bitwise_and),
+                  lambda a, b: g.vector.tensor_copy(T.MU[:, a:b], T.MJ[:, a:b])):
+            steps += [lambda f=f: f(0, 128), lambda f=f: f(128, 256)]
+        k = note("v", steps, [A("CDI"), A("P4")], [A("MI"), A("MJ"), A("MU")], (0.3, 768, 0, 0, 0))
+        calls[k]["n"] = 6
         mul(A("XH"), A("AL", b, b + 64), 0.5)
+        return k
 
-    for lo, hi in ((0, 34), (34, 66), (66, 98), (98, 130), (130, 164)):
+    for lo, hi in ((0, 14), (14, 42), (42, 84), (84, 124), (124, 164)):
         mov(A("XG", 16 * lo, 16 * hi), IND(A("X", 0, U), A("OCU", lo, hi)))
     mov(A("AS", 0, 32), A("XG", 0, U - 81, 82))
     mov(A("AS", 32, 64), A("XG", 40, U - 41, 82))
-    first = send(A("AS", 0, 72), A("AL", 0, 72), "a0", rank + 1, "loc0", 1.0)
-    fills = [("XS", c, min(U, XSW - c)) for c in range(0, XSW, U)] + [("MG", W, 144), ("SP", 1024, CAP)]
+    first = send(A("AS", 0, 72), A("AL", 0, 72), "a0", rank + 1, "loc0", 2.0)
+    fills = [("XS", c, min(4272, XSW - c)) for c in range(0, XSW, 4272)]
+    fills += [("MG", W, 144), ("SP", 1024, CAP)]
 
     def fill_gaps():
         g.sync.wait_ge(T.sem.loc0, len(engines(core, T.cores[(rank + 1) % n_ranks])))
         for name, c, n in fills:
-            g.sync.dma_start(T[name][:, c:c + n], T.x[:, 0:n]).then_inc(T.sem.ld6, 16)
+            g.sync.dma_start(T[name][:, c:c + n], T.X[:, 0:n] if n <= W else T.STC[:, 0:n]).then_inc(T.sem.ld6, 16)
 
-    note("y", fill_gaps, [], [A(name, c, c + n) for name, c, n in fills], 0.3, "ld6", 16 * len(fills), 7.0, after=[first])
-    for i, (c, n) in enumerate(((0, 512), (512, 512), (1024, 288), (1312, 512), (1824, 512), (2336, 288))):
+    fills[:2] = [("XS", 0, W), ("XS", W, W), ("XS", 2 * W, XSW - 2 * W)]
+    note("y", fill_gaps, [A("X", 0, W)], [A(name, c, c + n) for name, c, n in fills], (0.3, 0, 0, 0, 0), "ld6",
+         16 * len(fills), 9.0, after=[first])
+    k0 = lists(0)
+    for i, (c, n) in enumerate(((0, 192), (192, 448), (640, 352), (992, 320), (1312, 512), (1824, 512), (2336, 288))):
         dist_a("XG", c, n, "P%d" % (i % 2), c + 1)
         dist_b("XG", c, n, "P%d" % (2 + i % 2), c, True)
         lin(A("DS", c, c + n), A("P%d" % (2 + i % 2), 0, n), col(9) if c >= 1312 else 0.0)
         tt(IND(A("STC", 0, U), A("OCU", c // 16, (c + n) // 16)), A("DS", c, c + n), A("SRC", c % 1312, c % 1312 + n), ADD)
-
-    def spread(dst, src):
-        k = len(calls)
-        for i in range(41):
-            sel(A(dst, 32 + i, 8192, 128), A(src, i, U, 41), [[0, 64]], ALU.is_ge, 0.0, 0, 0)
-        chain(k, "g")
+        if i == 5:
+            calls[-1]["after"] = [k0]
 
     def score(t):
         groups = [[33 if t else 32, "s%d%d" % (t, h)] for h in range(2)]
@@ -574,7 +689,7 @@ def rank_program(g, core, T, topo):
                 mm(A("P%d" % h, 256, 384), A("ONE"), B("RH", h), False, False, groups[h])
 
         def ends(j):
-            return [(B("FD", 2 * j + bit, 64)[0], IND(A("X"), B("MU", 2 * j + bit, 4))[0],
+            return [(B("FD", 2 * j + bit, 64)[0], IND(A("X", 0, W), B("MU", 2 * j + bit, 4))[0],
                      B("AL", 72 * t + 32 * bit + j, 1)[0], B("XH", 32 * bit + j, 1)[0]) for bit in range(2)]
 
         def by_scalar(j):
@@ -586,14 +701,12 @@ def rank_program(g, core, T, topo):
         who, k = [], len(calls)
         for j in range(32):
             who.append(either(lambda j=j: by_scalar(j), lambda j=j: by_vector(j),
-                              [IND(A("X"), B("MU", j, 8)), A("AL", 72 * t, 72 * t + 64), A("XH")], B("FD", j)))
-            alt = tuple((e, c + (0.065 if e == "s" else 0.05)) for e, c in who[j]["alt"])
-            who[j].update(alt=alt, cost=alt[0][1], n=2)
+                              [IND(A("X", 0, W), B("MU", j, 8)), A("AL", 72 * t, 72 * t + 64), A("XH")], B("FD", j), 2))
             mm(A("P%d" % (j // 16), j % 16, 256, 16), B("FD", j), A("WF"), False, False, groups[j // 16],
                lambda j=j: B("WF", 1 if who[j]["q"] == "v" else 0, 16))
         chain(k, "s")
         k = len(calls)
-        for j0, j1 in ((0, 4), (4, 8), (8, 12), (12, 16), (16, 20), (20, 24), (24, 28), (28, 30), (30, 32)):
+        for j0, j1 in ((0, 6), (6, 11), (11, 16), (16, 22), (22, 27), (27, 30), (30, 32)):
             relu(A("MG", 128 * j0, 128 * j1), IND(A("MW" if t else "STC"), A("MU", 8 * j0, 8 * j1)), 0.0 if t else col(3))
             for j in range(j0, j1):
                 mm(A("P%d" % (j // 16), j % 16, 128 * n, 16), B("MG", j), A("WM"), False, False, groups[j // 16],
@@ -644,8 +757,7 @@ def rank_program(g, core, T, topo):
         mm(A("P3", 0, 8), one_row, R("NJ", 64, 72), True, False)
         ts(A("B1"), A("TQ", 0, 32), 0.0, ALU.is_gt)
         mov(A("DF", 32, 73, 40), q(6))
-        act(sm(6), q(1), ACT.Identity, MAGIC / 256)
-        act(sm(3), sm(6), ACT.Identity, -MAGIC / 256)
+        ts(sm(3), q(1), MAGIC / 256, ADD, MAGIC / 256, SUB)
         for gm in range(2):
             ts(A("DF", 40 * gm, 40 * gm + 32), B("P5", gm, 32), q1(0, gm), SUB, col(13), ADD)
             red(sm1(11, gm), A("DF", 40 * gm, 40 * gm + 33), MIN, True)
@@ -663,12 +775,13 @@ def rank_program(g, core, T, topo):
         for k in range(2):
             mov(B("SP", k, 512), IND(win, B("SPU", k, 32)))
         mm(A("P3", 0, 2), A("TRN"), A("WS"), False, False)
-        mm(A("P3", 6, 8), A("TRS"), A("WS"), False, False)
+        mm(A("P7", 0, 2), A("TRS"), A("WS"), True, True)
         mm(A("P3", 2, 4), A("TRI"), A("WS"), False, False)
         mm(A("P3", 4, 6), A("TRI"), A("WS"), False, True)
         if t < 2:
-            tt(A("ES", eb + 7, eb + 24, 16), q(3), q(4), MAX)
-        ts(A("ES", eb + 6, eb + 23, 16), A("P3", 6, 8), 255.0, MIN)
+            relu(A("ES", eb + 7, eb + 24, 16), q(3))
+            relu(A("ES", eb + 14, eb + 31, 16), q(4))
+        mov(A("ES", eb + 6, eb + 23, 16), A("P7", 0, 2))
         for gm in range(2):
             pre = A("PRE", 16 * gm, 16 * gm + 6)
             ts(pre, A("CC", 16 * gm, 16 * gm + 6), B("WS", gm, 1), MIN)
@@ -681,13 +794,14 @@ def rank_program(g, core, T, topo):
         if t < 2:
             mm(A("P5", 0, 4), A("IDF"), A("EB"), True, False)
             for gm in range(2):
+                ts(B("OW", gm, 256), B("UW", gm, 256), q1(5, gm), ALU.is_equal, sm1(5, gm), MUL)
                 for h in range(2):
-                    ts(B("OW", 2 * gm + h), B("CR", gm), q1(5 + 2 * h, gm), ALU.is_equal, sm1(5, gm), MUL)
                     mm(A("P5", h, 4, 2), B("OW", 2 * gm + h), dd(gm), False, gm == 1 and h == 1)
             cp(A("EU"), A("P5", 0, 4))
             mov(A("EW"), A("P5", 0, 4))
             mov(A("AS", ab, ab + 64), IND(win, A("EU")))
-            tt(A("AS", ab + 64, ab + 66), A("EW", 2, 4), A("EW", 0, 2), SUB)
+            for h in range(2):
+                lin(B("AS", ab + 64 + h, 1), B("EW", h, 1), B("EW", 2 + h, 1), -1.0)
             send(A("AS", ab, ab + 72), A("AL", ab, ab + 72), "a%d" % (t + 1), rank + 2 + t)
         ts(sm(46), A("P3", 4, 6), MAGIC / 16, ADD, MAGIC / 16, SUB)
         lin(sm(14), A("WS"), 32.0, -1.0)
@@ -695,7 +809,7 @@ def rank_program(g, core, T, topo):
             c1, c2, c3 = A("CMP", 32 * gm, 32 * gm + 14), A("CMP", 32 * gm + 16, 32 * gm + 30), A("CMP", 64 + 128 * gm, 192 + 128 * gm)
             ts(c1, A("K16", 0, 14), sm1(46, gm), ALU.is_gt, sm1(14, gm), MUL)
             ts(c2, A("K16", 0, 14), sm1(46, gm), ALU.is_equal, sm1(14, gm), MUL)
-            ts(c3, B("CR", gm), sm1(46, gm), ADD, B("P3", 2 + gm, 1), ALU.is_gt)
+            ts(c3, B("UW", 2 * gm), sm1(46, gm), ADD, B("P3", 2 + gm, 1), ALU.is_gt)
             mm(A("P6", 0, 14), B("CB", gm), c1, False, False)
             mm(A("P6", 0, 14), c3, c2, False, gm == 1)
         cp(A("CU", 0, 14), A("P6", 0, 14))
@@ -753,35 +867,128 @@ def rank_program(g, core, T, topo):
         ts(tu, A("P6", 0, 14), 128.0 * par, ADD)
         cp(IND(A("XS"), tu), A("LL", lb, lb + CAP))
 
-    def numbers(t):
-        cp(IND(A("CS"), A("TU", 16 * t, 16 * t + 14)), B("NUM", t, CAP))
-
-    def final_lists(par, k):
-        for b in range(4):
-            tr(B("FT", 4 * par + b, 32), (T.FA[:, 4 * k + b, :], "FA", range(128 * k + 32 * b, 128 * k + 32 * b + 32)))
-            ts(A("FU", 4 * par + b, 256, 8), B("FT", 4 * par + b, 32), float(ZADDR), MIN)
-
-    def shape(s, k, par):
+    def number_tables():
+        gfill(A("OCT"))
+        for b in range(6):
+            cp(A("OCT", 32 * b, 32 * b + len(range(b, 164, 6))), A("OCI", b, 164, 6))
+        for b in range(6):
+            tr(row3("OC3", b), B("OCT", b, 32))
         for gm in range(2):
-            lin(sm1(k, gm), st1(s, gm), st1(s + 1, gm), -1.0)
-        act(sm(k + 1), sm(k), ACT.Sign)
-        act(sm(k + 2), sm(k), ACT.Abs)
-        lin(sm(k + 3), hd(s), col(18 + par))
+            mov(A3("OC4", 0, 16, 6 * gm, 6 * gm + 6), A3("OC3", 16 * gm, 16 * gm + 16, 0, 6))
 
-    lists(0)
+        def rows():
+            for gm in range(2):
+                g.sync.dma_start(T.D1[gm:8:2, 16:3088], T.OC4[:, 6 * gm:6 * gm + 6, :]).then_inc(T.sem.d1, 16)
+            g.sync.dma_start(T.D1[:, 0:16], T.OC3[0:8, 0, 0:16]).then_inc(T.sem.d1, 16)
+
+        def shifts():
+            g.sync.wait_ge(T.sem.d1, 48)
+            for s in range(16):
+                g.sync.dma_start(T.FS[s:128:16, :], T.D1[:, s:s + FW]).then_inc(T.sem.fs, 16)
+
+        k = note("y", rows, [A3("OC4", 0, 16, 0, 12), A3("OC3", 0, 16, 0, 1)], [], (0.15, 0, 0, 0, 0), "d1", 48, 2.5)
+        note("y", shifts, [A("LL", 0, 8)], [A("FS")], (0.8, 0, 0, 0, 0), "fs", 256, 12.0, after=[k])
+        for par in range(2):
+            iota(A("BASE", 16 * par, 16 * par + 8), [[16, 4], [1312, 2]], 41 * par - 16, 0)
+            iota(A("BASE", 16 * par + 8, 16 * par + 16), [[-16, 4], [1312, 2]], 41 * par - 31, 0)
+        lin(A("BASE"), A("BASE"), col(27))
+        iota(B("ITB", 0), [[16, 4], [0, 32]], 0, 0)
+        lin(B("ITB", 0), B("ITB", 0), col(0))
+        mul(B("ITB", 1), B("ITB", 0), -1.0)
+        mul(A("I16K"), ident, 16384.0)
+        gfill(A("JF"), 1)
+        sel(A("JF"), A("JF"), [[-16, 8], [1, 16]], ALU.is_equal, 0.0, -15, 1)
+        gfill(A("VV"))
+        for c in (10, 13):
+            gfill(A("VV", c, 64, 16), 1)
+        for par in range(2):
+            gfill(A("VV", 32 * par + 11, 32 * par + 28, 16), 10 + par)
+            gfill(A("VV", 32 * par + 12, 32 * par + 29, 16), 63 - 32 * par)
+        big, n1k = A("I16K"), A("N1K")
+        parts = {1: [ident], -1: [A("NEGI")], 256: [A("I256")], 16384: [big], -16384: [n1k] * 16, -8192: [n1k] * 8,
+                 8192: [big] + [n1k] * 8, 3072: [A("I256")] * 12}
+        won = ((2, 1), (6, 1), (7, 16384), (10, -16384), (11, 256), (12, 1))
+        table = (((0, 8192), (10, -8192)), ((0, -8192), (10, -8192)), won, ((2, 16384), (10, -8192)),
+                 won + ((3, 1),), ((2, 16384), (3, 16384), (10, -8192)), ((3, -1), (13, 3072), (10, -1)),
+                 ((3, -16384), (10, -8192)), ((3, -16384),), ((3, 16384),), ((6, 1),), ((0, -16384),))
+        todo = [(c, m, f) for c, col_ents in enumerate(table) for f, w in col_ents for m in parts[w]]
+        mm(A("P4", 0, 16), one_row, R("ZR", 0, 16), True, False)
+        group = [len(todo), "wn"]
+        for c, m, f in todo:
+            mm(B("P4", c, 1), m, e16(f), False, False, group)
+        mov(A("WCL"), A("P4", 0, 16))
+        for c in range(12):
+            mul(B("WN", c), A("BLK"), B("WCL", c, 1))
+
+    def vv(par, i):
+        return A("VV", 32 * par + i, 32 * par + i + 17, 16)
+
+    def lookups(par, s, t, yj, pl):
+        k = 30 + 4 * par
+        tt(sm(k), hd(s + 1), hd(s), SUB)
+        act(vv(par, 0), sm(k), ACT.Sign)
+        act(vv(par, 3), sm(k), ACT.Abs)
+        tt(sm(k + 1), hd(s), yj, SUB)
+        tt(vv(par, 2), sm(k + 1), vv(par, 0), MUL)
+        mov(vv(par, 6), A("EL", 32 * t + 6, 32 * t + 23, 16))
+        mov(vv(par, 7), A("EL", 32 * t + 2, 32 * t + 19, 16))
+        tt(A("LH", 0, 3, 2), hd(s), hd(s + 1), MIN)
+        tt(A("LH", 1, 4, 2), hd(s), hd(s + 1), MAX)
+        mm(A(pl, 0, 16), A("IDF"), B("BASE", par, 16), True, False)
+        group = [16, "l%d" % par]
+        for h in range(2):
+            mul(B("LH", 1 + h, 4), A("LH", 0, 4), col(14 + h))
+            for gm in range(2):
+                o = 16 - 16 * gm + 16 * h
+                for b in range(4):
+                    mm(A(pl, 2 * b + h, 16, 8), A("IDW", o, o + 128), B("LH", 2 + 2 * h + gm, 2), False, False, group)
+        ts(B("NU", par, 16), A(pl, 0, 16), 0.0, MAX, float(FW - 1), MIN)
+        mov(B("GN", par, 256), IND(A("FS"), B("NU", par, 16)))
+        tr(B("VR", par, 32), B("VV", par, 32))
+
+    def spread_over(bank, k, c, x, group):
+        for b in range(4):
+            mm(B(bank, 4 * k + b, 32), B("WN", c), x, False, False, group)
+
+    def own(par, turned, bank, out):
+        group = [20, "o%d%d" % (par, turned)]
+        mm(A(bank), one_row, R("ZR", 0, 512), True, False)
+        mm(B(bank, 0), A("IDF"), B("GN", 2 * par), False, False, group)
+        mm(B(bank, 1), A("JF"), B("GN", 2 * par + 1), False, False, group)
+        mm(B(bank, 2), ident, B("ITB", turned), False, False, group)
+        mm(B(bank, 3), A("I16K"), B("ITB", turned), False, False, group)
+        for k, c in enumerate((turned, 1 - turned, 2 + 2 * turned, 3 + 2 * turned)):
+            spread_over(bank, k, c, B("VR", par, 32), group)
+        mov(out, B(bank, 2))
+        for k, o in ((3, MIN), (0, MAX), (1, MAX)):
+            tt(out, B(bank, k), out, o)
+
+    def results(par, number, empty):
+        n1, n2 = B("NA", 4 + 2 * par), B("NA", 5 + 2 * par)
+        tt(n1, empty, number, MAX)
+        for b in range(4):
+            ts(A("FU", 4 * par + b, 256, 8), B("NA", 4 * (4 + 2 * par) + b, 32), float(W), MIN)
+        ts(n2, empty, -1.0, MUL, -1.0, MAX)
+        tt(n2, n2, number, MIN)
+        for b in range(4):
+            tr(row3("YT", 4 * par + b), B("NA", 4 * (5 + 2 * par) + b, 32))
+
+    def spread(par):
+        k = len(calls)
+        for i in range(41):
+            sel(A("XS", 128 * par + 32 + i, 8192, 256), A("XG", 41 * par + i, U, 82), [[0, 32]], ALU.is_ge, 0.0, 0, 0)
+        chain(k, "g")
+
     score(0)
     wrap("P4", 164, "VLT", "STC", U)
     ts(A("VLU"), A("P4", 0, 164), 32.0, ADD)
     choose(0, state(1, 0), state(1, 1))
     v = S("WQ2", 2)
     sel(v, v, [[-16, 8]], ALU.not_equal, 256.0, -13, 1)
-    ms(A("XS", ZADDR, XSW), 0.0)
-    spread("XS", "XG")
-    k0 = len(calls)
-    for lo, hi in ((0, 32), (32, 64), (64, 98), (98, 132), (132, 164)):
-        mov(A("OCR", 16 * lo, 16 * hi), IND(A("NO"), A("OCU", lo, hi)))
-    chain(k0, "s")
+    spread(0)
     arrive(0, state(0, 0), state(0, 1))
+    number_tables()
+    lin(sm(40), A("EL", 13, 30, 16), 72.0, -1.0)
     s = state(0, 1)
     mm(A("P5", 0, 4), ident, A("CWB"), True, False)
     for h in range(2):
@@ -801,57 +1008,55 @@ def rank_program(g, core, T, topo):
     lin(B("CT", 0, 32), io_(0, 32), col(4), 0.0)
     gfill(A("MW", U, U + CAP), 600)
     choose(1, state(0, 1), state(0, 2))
-    numbers(0)
-    spread("CS", "OCR")
+    spread(1)
     arrive(1, state(1, 1), state(1, 2))
-    shape(state(0, 2), 36, 0)
-    lin(sm(28), sm(38), float(PARTS - 1), -1.0)
-    mul(sm(29), sm(37), -2.0)
-    lin(sm(27), sm(38), 16384.0, 16384.0)
-    mul(sm(35), sm(38), -16384.0)
-    for gm in range(2):
-        lin(F(0, gm), i3, sm1(28, gm))
-        act(F(1, gm), i3, ACT.Relu, sm1(27, gm), -16384.0)
-    tt(F(2), F(0), F(1), SUB)
+    tt(sm(41), hd(state(1, 1) + 1), A("EL", 45, 62, 16), SUB)
+    lookups(0, state(0, 2), 0, sm(40), "P4")
+    own(0, 0, "P4", B("NA", 0))
+    own(0, 1, "P5", B("NA", 1))
+    mm(B("P5", 0), A("I16K"), B("ITB", 0), True, False)
+    spread_over("P5", 0, 7, B("VR", 0, 32), [4, "p"])
+    mov(B("NA", 2), B("P5", 0))
+    lin(B("NA", 1), B("NA", 1), -16384.0)
+    final = [28, "q"]
+    mm(A("P4"), one_row, R("ZR", 0, 512), True, False)
+    for k in range(2):
+        mm(B("P4", k), A("IDF"), B("NA", k), False, False, final)
+    mm(B("P4", 2), ident, B("ITB", 0), False, False, final)
+    mm(B("P4", 3), A("I16K"), B("ITB", 0), False, False, final)
+    spread_over("P4", 2, 6, B("VR", 0, 32), final)
+    spread_over("P4", 3, 7, B("VR", 0, 32), final)
     score(2)
-    numbers(1)
     choose(2, state(1, 2), state(1, 0))
-    shape(state(1, 0), 30, 1)
-    mul(sm(34), sm(32), -16384.0)
-    for gm in range(2):
-        lin(F(0, gm), i3, sm1(33, gm), sm1(31, gm))
-        lin(F(1, gm), i3, sm1(34, gm), 16384.0)
-    tt(F(3), F(0), F(1), MAX)
-    final_lists(1, 3)
-
-    def ev2(i, gm):
-        return B("EL", 64 + i + 16 * gm, 1)
-
-    for gm in range(2):
-        lin(sm1(7, gm), ev2(3, gm), sm1(39, gm), sm1(36, gm))
-        lin(sm1(8, gm), ev2(3, gm), sm1(37, gm), sm1(29, gm))
-        lin(sm1(9, gm), ev2(0, gm), sm1(35, gm), -16384.0)
-        lin(F(2, gm), F(2, gm), ev2(6, gm))
-        lin(F(4, gm), i3, sm1(7, gm), sm1(8, gm))
-        lin(F(5, gm), i3, sm1(9, gm), 16384.0)
-    tt(F(5), F(5), F(2), MAX)
-    tt(F(6), F(4), F(5), MAX)
-    final_lists(0, 6)
-    mov(A("XS", PARTS, PARTS + CAP), A("LL", 480, 480 + CAP))
+    lookups(1, state(1, 0), 1, sm(41), "P2")
+    own(1, 0, "P5", B("NA", 3))
+    mm(B("P2", 0), A("I16K"), B("ITB", 0), True, False)
+    spread_over("P2", 0, 7, B("VR", 1, 32), [4, "r"])
+    results(1, B("NA", 3), B("P2", 0))
+    tr(B("ER", 0, 32), B("EL", 2, 32))
+    for k, c in ((2, 10), (0, 8), (1, 9), (3, 11)):
+        spread_over("P4", k, c, B("ER", 0, 32), final)
+    tt(B("NA", 2), B("P4", 2), B("NA", 2), MIN)
+    tt(B("NA", 2), B("P4", 0), B("NA", 2), MAX)
+    tt(B("NA", 2), B("P4", 1), B("NA", 2), MAX)
+    results(0, B("NA", 2), B("P4", 3))
+    mov(A("X", U + 2 * CAP, U + 3 * CAP), A("LL", 480, 480 + CAP))
     nout = [0]
 
-    def store(dst, src, late):
+    def store(dst, src, time):
         nout[0] += 16
-        note("y", lambda: g.sync.dma_start(dst, src[0]).then_inc(T.sem.out0, 16), [src], [], 0.05, "out0", 10 ** 6, late)
+        note("y", lambda: g.sync.dma_start(dst, src[0]).then_inc(T.sem.out0, 16), [src], [], (time, 0, 0, 0, 0), "out0",
+             10 ** 6, 1.7)
 
+    for gm in range(2):
+        mov(A3("YU", 0, 16, 8 * gm, 8 * gm + 8), A3("YT", 16 * gm, 16 * gm + 16, 0, 8))
+        store(T.yo[gm:8:2, :], A3("YU", 0, 16, 8 * gm, 8 * gm + 8), 0.3)
     k0 = len(calls)
-    for c in range(4):
-        mov(B("YO", c, 1024), IND(A("CS"), B("FU", c, 64)))
-        store(T.yo[:, 1024 * c:1024 * c + 1024],
-              (T.YO[0:128:16, 1024 * c:1024 * c + 1024], "YO", range(1024 * c, 1024 * c + 1024)), 1.8)
-    for c in range(8):
-        mov(B("FD", c, 512), IND(A("XS"), B("FU", c, 32)))
-        store(T.y[:, 512 * c:512 * c + 512], B("FD", c, 512), 2.6)
+    for a, b in ((0, 640), (640, 1536), (1536, 2432), (2432, 3328), (3328, W)):
+        h = (a + b) // 2
+        mov(A("FD", a, h), IND(A("X"), A("FU", a // 16, h // 16)))
+        mov(A("FD", h, b), IND(A("X"), A("FU", h // 16, b // 16)))
+        store(T.y[:, a:b], A("FD", a, b), 0.25 + (b - a) * 0.0006)
     chain(k0, "s")
 
     if not ORDER:
@@ -889,6 +1094,12 @@ def rank_program(g, core, T, topo):
             lst = acc.setdefault(name, [])
             lst[:] = [e for e in lst if not ((w or (e[4] == qn and not e[1] and not c["dma"])) and e[0] & ~m == 0)]
             lst.append([m, w, sem, val, qn])
+        if isinstance(c["fn"], list):
+            for k, step in enumerate(c["fn"]):
+                if k >= 2:
+                    wait(qn, sem, val - c["n"] + k - 1)
+                step().then_inc(T.sem[sem], 1)
+            continue
         done = c["fn"]()
         if not c["dma"]:
             for ins in (done if c["n"] > 1 else [done]):

from concourse.mybir import AluOpType, AxisListType, ActivationFunctionType

ALU = AluOpType
ACT = ActivationFunctionType
U, CAP, W = 2624, 224, 4096
XSW, FW = 8544, 2640
MAGIC = 3221225472.0
CASES = ((0.00098, 1.5, 3.6, 0.21, 0.9, 2.6, 1.0, 0.06), (0.00083, 1.3, 2.8, 0.18, 0.8, 2.3, 0.8, 0.1),
         (0.0012, 1.15, 3.0, 0.16, 0.65, 1.9, 0.8, 0.03))
TRIES, SHAKE, SPARE, TEMP, TURNS, TEMP2 = 6500, 3.0, 0.1, 0.6, 3000, 0.1
BF, F32, I32, U16 = "bfloat16", "float32", "int32", "uint16"
SCRATCH = {}
for _d, _l in (
        (BF, dict(X=W + 16, XG=U + 8, AD=U + 8, MW=W, MG=W + 144, FD=W, XS=XSW, IDW=160, NEGI=128, I256=128, INEG=128,
                  BLK=128, WZ=128, WA=512, WB=512, WC=464, HALF=128, N256=128, N1K=128, SELW=64, B32=128, TGT=144, G=768,
                  RH=256, ZR=896, CQ=128, CB=256, UW=512, K16=16, TRI=128, TRN=128, TRS=128, UOH=128, WR=256, WRG=256,
                  E16=16, IOT=256, NKK=128, ONE=128, KT=CAP, KW=16, CWB=4, NJ=72, AS=216, AL=216, ES=96, EL=96, LS=720,
                  LL=720, XH=64, MBS=32, GD=64, WS=2, CMP=320, SP=1024 + CAP, OH=256, OW=512, ST=24, SMK=8, OWN=32,
                  OWR=32, ER=64, TGB=CAP, B1=32, B2=32, SCL=32, CC=32, PRE=32, I16K=128, ITB=256, WN=1536, VV=64, VR=64,
                  LH=16)),
        (F32, dict(STC=W, FS=FW, OCT=192, GN=512, JF=128, BASE=32, WCL=16, NA=1024, SRC=U // 2, DS=U, B82=176, COL=40,
                   RW=32, SM=120, TQ=64, DF=80, SPT=64, SPR=64, EW=4, EB=4, CT=104, ND=CAP, IDF=128, VLT=144)),
        (I32, dict(OCI=164, CDI=256, MI=256, MJ=256, PI=4)),
        (U16, dict(OCU=164, VLU=164, MU=256, OFF=4, CU=16, SPU=64, EU=4, OWU=16, TU=32, FU=256, NU=32))):
    for _k in _l:
        SCRATCH[_k] = ("sbuf", [128, _l[_k]], _d)
SCRATCH["OC3"] = ("sbuf", [128, 6, 32], F32)
SCRATCH["OC4"] = ("sbuf", [128, 12, 16], F32)
SCRATCH["YT"] = ("sbuf", [128, 8, 32], F32)
SCRATCH["YU"] = ("sbuf", [128, 16, 16], F32)
SCRATCH["D1"] = ("dram", [8, 3088], F32)
for _k in range(8):
    SCRATCH["P%d" % _k] = ("psum", [128, 512], F32)
PART = dict(WDL=("WA", 0, 128, 4), WDR=("WA", 128, 128, 4), WDZ=("WA", 256, 128, 4), WDN=("WA", 384, 128, 4),
            WQ1=("WB", 0, 128, 6), WQ2=("WB", 128, 128, 6), WC1=("WB", 256, 128, 6), WC2=("WB", 384, 128, 6),
            WG1=("WC", 0, 128, 5), WG2=("WC", 128, 128, 5), WK=("WC", 256, 128, 5), WM=("WC", 384, 48, 5),
            WF=("WC", 432, 32, 5))
SEMAPHORES = ["qv", "qs", "qt", "qg", "ld0", "ld1", "ld2", "ld3", "ld4", "ld6", "loc", "loc0", "a0", "a1", "a2",
              "e0", "e1", "e2", "l0", "l1", "l2", "out0", "fill", "d1", "fs"]
ORDER = []


def bits(cols, wide):
    if wide:
        cols = range(cols[0] // 8 * 8, cols[-1] // 8 * 8 + 8)
    if isinstance(cols, range) and cols.step == 1:
        return ((1 << len(cols)) - 1) << cols[0]
    return sum(1 << c for c in cols)


def touched(c):
    items = []
    for lst, w in ((c["r"], False), (c["w"], True)):
        for a in lst:
            psum = SCRATCH[a[1]][0] == "psum"
            items.append((a[1], 1 if psum else bits(a[2], c["dma"]), w, psum))
            if len(a) > 3:
                items.append((a[3][1], bits(a[3][2], False), False, False))
    return items


def schedule(calls, lanes):
    n = len(calls)
    pred, acc = [set() for _ in calls], {}
    for i, c in enumerate(calls):
        items = touched(c) + [(a[1], bits(a[2], True), True, False) for a in c["far"]]
        for name, m, w, psum in items:
            for e in acc.get(name, []):
                o = calls[e[2]]
                if e[0] & m and (w or e[1] or (psum and (o["q"] != c["q"] or c["alt"] or o["alt"]))) \
                        and not (c["any"] and o["any"] == c["any"]):
                    pred[i].add(e[2])
        for name, m, w, psum in items:
            lst = acc.setdefault(name, [])
            if w and not c["any"]:
                lst[:] = [e for e in lst if e[0] & ~m]
            lst.append((m, w, i))
        pred[i] |= set(c["after"])
        pred[i].discard(i)

    def price(c, q, case):
        fixed, cycles, gathered, scattered, sends = c["cost"][q]
        return fixed * (1 if q == "y" else case[0] / 0.00083) + (case[7] if q == "s" and cycles else 0) + \
            (cycles + gathered * case[1] + scattered * case[2]) * case[0] + sends * case[4]

    def gap(a, b, case):
        return calls[a]["late"] + calls[a]["cost"][calls[a]["q"]][4] * case[5] + \
            (0.0 if calls[a]["q"] == "t" == calls[b]["q"] else case[3])

    prices = [[{q: price(c, q, case) for q in c["cost"]} for c in calls] for case in CASES]
    waits = [[[(p, gap(p, i, case)) for p in pred[i]] for i in range(n)] for case in CASES]
    queue = [c["q"] for c in calls]
    cost, before = [prices[0][i][queue[i]] for i in range(n)], waits[0]
    after = [[] for _ in calls]
    for i in range(n):
        for p, d in before[i]:
            after[p].append((i, d))
    tails = [i for i in range(n) if not after[i]]

    def span(order, k):
        end, why, last, wk, pk = [0.0] * n, [-1] * n, {}, waits[k], prices[k]
        for i in order:
            q = queue[i]
            p0 = last.get(q, -1)
            t = end[p0] if p0 >= 0 else 0.0
            for p, d in wk[i]:
                if end[p] + d > t:
                    t, p0 = end[p] + d, p
            end[i], why[i], last[q] = t + pk[i][q], p0, i
        i = max(tails, key=lambda i: end[i] + late[i])
        total, pairs = end[i] + late[i], []
        while why[i] >= 0:
            if why[i] not in pred[i]:
                pairs.append((why[i], i))
            i = why[i]
        return total, pairs

    def place(turn, deps, lead, choose=()):
        start, busy = [0.0] * n, {q: ([], []) for q in "vstgy"}
        for i in turn:
            t0, found = max([start[p] + cost[p] + d for p, d in deps[i]] + [lead[i]]), None
            for q, c in (prices[0][i].items() if i in choose else ((queue[i], cost[i]),)):
                t, (begins, ends) = t0, busy[q]
                lo, hi = 0, len(ends)
                while lo < hi:
                    mid = (lo + hi) // 2
                    lo, hi = (mid + 1, hi) if ends[mid] <= t else (lo, mid)
                while lo < len(ends) and begins[lo] < t + c - 1e-9:
                    t = max(t, ends[lo])
                    lo += 1
                end = t + c + (choose.get(i, 0) if q == "v" and choose else 0)
                if found is None or end < found[0]:
                    found = (end, t, q, c, lo)
            _, t, queue[i], cost[i], lo = found
            busy[queue[i]][0].insert(lo, t)
            busy[queue[i]][1].insert(lo, t + cost[i])
            start[i] = t
        return start

    late, zero, prio = [c["late"] for c in calls], [0.0] * n, [0.0] * n
    nxt = {a: b for lane in lanes for a, b in zip(lane, lane[1:])}
    for _ in range(3):
        for i in range(n - 1, -1, -1):
            prio[i] = cost[i] + max([d + prio[s] for s, d in after[i]] + [late[i], prio[nxt[i]] if i in nxt else 0])

    def in_turn(key):
        key = list(key)
        for i in range(n):
            for p, _ in before[i]:
                if key[p] >= key[i]:
                    key[i] = key[p] + 1e-6
        return sorted(range(n), key=lambda i: key[i])

    seed = [777]

    def rand():
        seed[0] = (seed[0] * 1103515245 + 12345) % 2147483648
        return seed[0] / 2147483648

    def worth(order, start=None):
        spans = [span(order, k) for k in range(len(CASES))]
        value = sum(case[6] * s[0] for case, s in zip(CASES, spans))
        return value, start or order, list(queue), list(cost), [s[1] for s in spans]

    def by_start(start):
        return sorted(range(n), key=lambda i: start[i])

    def polish(start, choose):
        back = place(sorted(range(n), key=lambda i: -start[i] - cost[i]), after, late)
        return place(sorted(range(n), key=lambda i: -back[i] - cost[i]), before, zero, choose)

    start = place(in_turn([-x for x in prio]), before, zero)
    best = None
    for k in range(6):
        start = polish(start, {i: SPARE for i in range(n)})
        new = worth(by_start(start), start)
        if best is None or new[0] < best[0]:
            best = new
    now = best
    for k in range(TRIES):
        queue[:], cost[:] = now[2], now[3]
        key, some = list(now[1]), {}
        if rand() < 0.7:
            pairs = now[4][int(rand() * len(CASES))]
            j = int(rand() * len(pairs))
            a, b = pairs[j]
            kind = rand()
            if kind < 0.35:
                a = pairs[min(len(pairs) - 1, j + int(6 * rand() ** 2))][0]
                key[b] = key[a] - 1e-4
                for p, _ in before[b]:
                    key[p] = min(key[p], key[b] - 1e-4)
            elif kind < 0.7:
                b = pairs[max(0, j - int(6 * rand() ** 2))][1]
                key[a] = key[b] + 1e-4 + rand() ** 2
            else:
                a = a if rand() < 0.5 else b
                some = {a: -9 if queue[a] == "s" else 9}
        else:
            t0, width, size = rand() * max(now[1]), 0.5 + 5 * rand(), SHAKE * rand()
            for i in range(n):
                if t0 - width < key[i] < t0:
                    if rand() < 0.3:
                        some[i] = 0.4 * rand() - 0.1
                    if rand() < 0.2:
                        key[i] += size * (rand() - 0.5)
        start = place(in_turn(key), before, zero, some)
        if rand() < 0.03:
            start = polish(start, some)
        new = worth(by_start(start), start)
        if new[0] < now[0] + TEMP * rand() * (1 - k / TRIES):
            now = new
        if new[0] < best[0]:
            best = new
    queue[:] = best[2]
    best = now = worth(by_start(best[1]))
    for k in range(TURNS):
        queue[:] = now[2]
        order = list(now[1])
        pairs = now[4][int(rand() * len(CASES))]
        j = int(rand() * len(pairs))
        a, b = pairs[j]
        kind = rand()
        if kind < 0.75:
            if kind < 0.35:
                a = pairs[min(len(pairs) - 1, j + int(5 * rand() ** 3))][0]
            else:
                b = pairs[max(0, j - int(5 * rand() ** 3))][1]
            ia, ib = order.index(a), order.index(b)
            piece = order[ia:ib + 1]
            if kind < 0.35:
                moved = {b}
                for i in reversed(piece):
                    if i in moved:
                        moved |= pred[i]
                order[ia:ib + 1] = [i for i in piece if i in moved] + [i for i in piece if i not in moved]
            else:
                moved = {a}
                for i in piece:
                    if pred[i] & moved:
                        moved.add(i)
                order[ia:ib + 1] = [i for i in piece if i not in moved] + [i for i in piece if i in moved]
        else:
            a = a if rand() < 0.5 else b
            if len(prices[0][a]) < 2:
                continue
            queue[a] = "v" if queue[a] == "s" else "s"
            if rand() < 0.5:
                ia = order.index(a)
                near = [i for i in order[max(0, ia - 25):ia + 25] if i != a and queue[i] == queue[a] and len(prices[0][i]) > 1]
                if near:
                    i = near[int(rand() * len(near))]
                    queue[i] = "v" if queue[i] == "s" else "s"
        new = worth(order)
        if new[0] < now[0] + TEMP2 * rand() * (1 - k / TURNS):
            now = new
        if now[0] < best[0]:
            best = now
    return [(i, best[2][i]) for i in best[1]]


def rank_program(g, core, T, topo):
    rank = T.rank_of(core)
    if rank is None:
        return
    n_ranks = len(T.cores)
    eng = {"v": g.vector, "s": g.scalar, "t": g.tensor, "g": g, "y": g.sync}
    calls, lanes = [], []
    sent = [0]

    def A(name, c0=0, c1=None, st=1, p0=0, p1=128):
        if name in PART:
            name, base, n = PART[name][:3]
            c0, c1 = base + c0, base + (n if c1 is None else c1)
        if c1 is None:
            c1 = SCRATCH[name][1][1]
        ap = T[name][p0:p1, c0:c1] if st == 1 else T[name][p0:p1, c0:c1:st]
        return (ap, name, range(c0, c1, st))

    def A3(name, c0, c1, b0, b1):
        n = SCRATCH[name][1][2]
        return (T[name][:, b0:b1, c0:c1], name, [n * b + c for b in range(b0, b1) for c in range(c0, c1)])

    def row3(name, b):
        return (T[name][:, b, :], name, range(32 * b, 32 * b + 32))

    def B(name, k, n=128):
        return A(name, n * k, n * k + n)

    def S(name, c):
        return A(name, c, c + 113, 16)

    def R(name, c0=0, c1=None, st=1):
        return A(name, c0, c1, st, 0, 1)

    def IND(win, off):
        return (win[0].indirect(off[0]), win[1], win[2], off)

    def note(q, fn, reads, writes, cost, sem=None, val=0, late=0.0, any_order=None, far=(), after=(), alt=None):
        calls.append(dict(q=q, fn=fn, r=[a for a in reads if isinstance(a, tuple)], w=writes, cost=alt or {q: cost}, sem=sem,
                          val=val, dma=sem is not None, late=late, any=any_order, far=far, after=after, alt=alt, n=1))
        return len(calls) - 1

    def price(reads, o, rate=None, n=1):
        aps = [a for a in reads if isinstance(a, tuple)] + [o]
        ind = [a for a in aps if len(a) > 3]
        if ind:
            k = 16 * len(ind[0][3][2])
            return ((0.065 if rate else 0.05) * n, 0, 0 if ind[0] is o else k, k if ind[0] is o else 0, 0)
        if rate is None:
            rate = 0.5 if all(SCRATCH[a[1]][2] in (BF, U16) or len(a[2]) == 1 for a in aps) else 1
        return (0.005, max(64, len(reads[0][2] if reads else o[2]) * rate), 0, 0, 0)

    def op(q, fn, reads, o, rate=None):
        note(q, fn, reads, [o], price(reads, o, rate))

    def either(fs, fv, reads, o, n=1):
        k = len(calls)
        note("s", lambda: fs() if calls[k]["q"] == "s" else fv(), reads, [o], None,
             alt={"s": price(reads, o, 1, n), "v": price(reads, o, None, n)})
        calls[k]["n"] = n
        return calls[k]

    def ap(x):
        return x[0] if isinstance(x, tuple) else x

    def ts(o, i, s1, o0, s2=None, o1=None):
        if o1 is None:
            op("v", lambda: g.vector.tensor_scalar(o[0], i[0], ap(s1), None, o0), [i, s1], o)
        else:
            op("v", lambda: g.vector.tensor_scalar(o[0], i[0], ap(s1), ap(s2), o0, o1), [i, s1, s2], o)

    def tt(o, a, b, o0):
        op("v", lambda: g.vector.tensor_tensor(o[0], a[0], b[0], o0), [a, b], o,
           2 if SCRATCH[a[1]][0] == SCRATCH[b[1]][0] else 1)

    def cp(o, i):
        op("v", lambda: g.vector.tensor_copy(o[0], i[0]), [i], o)

    def ms(o, c):
        op("v", lambda: g.vector.memset(o[0], c), [], o)

    def red(o, i, o0, ab=False):
        op("v", lambda: g.vector.tensor_reduce(o[0], i[0], AxisListType.X, o0, apply_absolute_value=ab), [i], o, 1)

    def tr(o, i):
        op("v", lambda: g.vector.transpose(o[0], i[0]), [i], o)

    def act(o, i, f, bias=None, scale=1.0):
        if bias is None:
            op("s", lambda: g.scalar.activation(o[0], i[0], f, scale=ap(scale)), [i, scale], o, 1)
        else:
            op("s", lambda: g.scalar.activation(o[0], i[0], f, bias=ap(bias), scale=ap(scale)), [i, bias, scale], o, 1)

    def lin(o, i, bias, scale=1.0):
        either(lambda: g.scalar.activation(o[0], i[0], ACT.Identity, bias=ap(bias), scale=ap(scale)),
               lambda: g.vector.tensor_scalar(o[0], i[0], ap(scale), ap(bias), ALU.mult, ALU.add), [i, bias, scale], o)

    def mul(o, i, scale):
        either(lambda: g.scalar.activation(o[0], i[0], ACT.Copy, scale=ap(scale)),
               lambda: g.vector.tensor_scalar(o[0], i[0], ap(scale), None, ALU.mult), [i, scale], o)

    def mov(o, i):
        either(lambda: g.scalar.activation(o[0], i[0], ACT.Copy), lambda: g.vector.tensor_copy(o[0], i[0]), [i], o)

    def relu(o, i, bias=0.0):
        either(lambda: g.scalar.activation(o[0], i[0], ACT.Relu, bias=ap(bias)),
               lambda: g.vector.tensor_scalar(o[0], i[0], ap(bias), 0.0, ALU.add, ALU.max), [i, bias], o)

    def mm(o, l, r, start, stop, group=None, part=None):
        def fn():
            if group:
                group[0] -= 1
            return g.tensor.matmul(o[0], l[0], (part() if part else r)[0], start, group[0] == 0 if group else stop)
        cost = max(min(64, len(l[2])), len(r[2])) * (4 if SCRATCH[l[1]][2] == F32 else 1) * 0.55
        note("t", fn, [l, r], [o], (0, cost, 0, 0, 0), any_order=group and group[1])

    def iota(o, pat, base, cm, small=True):
        note("g", lambda: g.iota(o[0], pat, base, cm, allow_small_or_imprecise_dtypes=True) if small else
             g.iota(o[0], pat, base, cm), [], [o], (0.13, 2 * len(o[2]), 0, 0, 0))

    def sel(o, i, pat, cmp, fill, base, cm):
        note("g", lambda: g.affine_select(o[0], i[0], pat, cmp, float(fill), base, cm), [i], [o],
             (0.17, 2 * len(o[2]), 0, 0, 0))

    def gfill(o, v=0):
        iota(o, [[0, len(o[2])]], v, 0)

    def wrap(pb, n, name, src, width):
        for r in range(16):
            mm(A(pb, 0, n), A(name, 16 - r, 144 - r), A(src, r, width, 16), r == 0, r == 15)

    def load(q, o, src, sem, late):
        note(q, lambda: eng[q].dma_start(o[0], src).then_inc(T.sem[sem], 16), [], [o], (0.05, 0, 0, 0, 0), sem, 16, late)

    def engines(src, dst):
        return topo.engines(src, dst)[:8]

    def send(src, dst, sem, to_rank, loc="loc", first=0.0):
        to = T.cores[to_rank % n_ranks]
        es = engines(core, to)
        rid, pid, _ = topo.addr(to)
        if loc == "loc":
            sent[0] += len(es)
        return note("g", lambda: g.remote_dma(dst[0], src[0], T.sem[sem], T.sem[loc], pid, rid, sum(1 << e for e in es)),
                    [src], [], (first, 0, 0, 0, 1), loc, 10 ** 6, far=[dst])

    def chain(first, qn):
        lanes.append([k for k in range(first, len(calls)) if calls[k]["q"] == qn])

    def col(i):
        return A("COL", i, i + 1)

    def e16(i):
        return A("E16", i, i + 1)

    def sm(i):
        return A("SM", 2 * i, 2 * i + 2)

    def sm1(i, k):
        return A("SM", 2 * i + k, 2 * i + k + 1)

    def io_(a, b):
        return A("IOT", a, b)

    ADD, SUB, MUL, MAX, MIN = ALU.add, ALU.subtract, ALU.mult, ALU.max, ALU.min
    ident = A("IDW", 16, 144)
    g8 = S("BLK", 0)
    one_row = R("ONE")

    load("y", A("OCI"), T.oc[:, :], "ld0", 2.7)
    load("y", A("X", 0, 1312), T.x[:, 0:1312], "ld1", 3.7)
    load("s", A("X", 1312, U), T.x[:, 1312:U], "ld2", 3.7)
    load("y", A("CDI"), T.cd[:, :], "ld3", 4.2)
    load("y", A("X", U, W), T.x[:, 0:W - U], "ld4", 5.0)
    lanes.append([0, 1, 3, 4])
    ms(A("ONE"), 1.0)
    ms(A("IDW"), 0.0)
    ms(R("ZR", 0, 768), 0.0)
    iota(A("PI", 0, 1), [[0, 1]], 0, 1, False)
    iota(io_(0, 16), [[1, 16]], 0, 0)
    iota(A("B82", 0, 82), [[0, 2], [1, 41]], 32, 0)
    iota(A("B82", 88, 170), [[-1, 2], [0, 41]], 1, 0)
    sel(ident, A("ONE"), [[-1, 128]], ALU.is_equal, 0.0, 0, 1)
    sel(A("BLK"), A("ONE"), [[-16, 8], [0, 16]], ALU.is_ge, 0.0, 0, 1)
    iota(col(20), [[0, 1]], 1, -1)
    sel(A("BLK"), A("BLK"), [[16, 8], [0, 16]], ALU.is_ge, 0.0, 15, -1)
    ms(A("RW"), 0.0)
    ts(A("PI", 1, 2), A("PI", 0, 1), 15, ALU.bitwise_and)
    ts(A("PI", 2, 3), A("PI", 0, 1), 31, ALU.bitwise_and)
    cp(A("COL", 0, 2), A("PI", 1, 3))
    for a, b, c in ((3, 4, 2.0), (4, 5, -2.0), (5, 6, -1.0), (6, 8, 1.0), (9, 11, 256.0), (11, 13, -256.0),
                    (19, 20, -103.5), (20, 21, 103.5), (21, 22, 33.0), (22, 23, -71.0), (23, 24, -32.0), (25, 29, -1e5)):
        ms(A("RW", a, b), c)
    ts(A("E16"), io_(0, 16), col(0), ALU.is_equal)
    for k in range(2):
        tt(B("RW", k, 16), B("RW", k, 16), A("E16"), MUL)
        red(col(2 + k), B("RW", k, 16), ADD)
    mul(col(10), e16(5), 256.0)
    for i in range(5):
        mul(col(5 + i), e16(13), float(1 << i))
    mul(A("B82", 88, 170), A("B82", 88, 170), col(10))
    mul(A("B82", 0, 82), A("B82", 0, 82), col(2))
    tt(A("SRC", 0, 82), A("B82", 0, 82), A("B82", 88, 170), ADD)
    for i in range(4):
        n = 82 << i
        lin(A("SRC", n, 2 * n), A("SRC", 0, n), col(5 + i))
    cp(A("OCU"), A("OCI"))

    scaled = {1: ident}
    for w, name in ((-1, "NEGI"), (-1024, "N1K"), (256, "I256"), (-256, "N256"), (0.5, "HALF")):
        mul(A(name), ident, float(w))
        scaled[w] = A(name)
    sums = {2: (1, 1), -2: (-1, -1), -0.5: (-1, 0.5), 2.5: (1, 1, 0.5), -2.5: (-1, -1, -1, 0.5), -255: (-256, 1)}
    rare = []

    def pick(f):
        return g8 if f is None else S("IDW", 16 + f)

    def weights(bank, width, table):
        todo = []
        for out, col_ents in table:
            for f, w in col_ents:
                if w in scaled or w in sums:
                    todo += [(out, scaled[x], pick(f)) for x in sums.get(w, (w,))]
                else:
                    if (f, w) not in rare:
                        rare.append((f, w))
                        mul(B("SELW", len(rare) - 1, 8), pick(f), float(w))
                    todo.append((out, ident, B("SELW", rare.index((f, w)), 8)))
        k = len(calls)
        mm(A("P%d" % bank, 0, width), one_row, R("ZR", 0, width), True, False)
        group = [len(todo), "w%d" % bank]
        for c in todo:
            mm(c[0], c[1], c[2], False, False, group)
        chain(k, "t")

    def wc(name, c):
        base, bank = PART[name][1], PART[name][3]
        if name in ("WM", "WF"):
            return A("P%d" % bank, base + 8 * c, base + 8 * c + 8)
        return S("P%d" % bank, base + c)

    def neg(e):
        return tuple((f, -w) for f, w in e)

    every = ((None, 1),)
    weights(4, 512, [(wc("WDL", 0), every), (wc("WDL", 12), every), (wc("WDR", 1), every), (wc("WDR", 10), every),
                     (wc("WDZ", 2), every), (wc("WDN", 1), every)])
    mov(A("WA"), A("P4"))
    low = ((1, 1), (9, 1), (10, -1), (3, -1024))
    high = ((0, 1), (11, 1), (12, -1), (4, -1024))
    bad = ((5, -1024), (6, -1024))
    size = ((7, 1), (3, -1), (8, -0.5))
    weights(5, 464, [(wc("WF", 0), neg(every)), (wc("WF", 1), neg(every)), (wc("WF", 2), ((None, 2),)),
                     (wc("WF", 3), ((None, 2),)), (wc("WM", 0), low + bad), (wc("WM", 1), high + bad), (wc("WM", 2), size),
                     (wc("WM", 3), low + bad + ((2, -1),)), (wc("WM", 4), high + bad + ((2, -1),)), (wc("WM", 5), size),
                     (wc("WG1", 0), every), (wc("WG1", 2), every), (wc("WK", 1), neg(every)), (wc("WK", 3), neg(every)),
                     (wc("WG2", 0), every), (wc("WG2", 3), ((None, -1 / 256),)),
                     (wc("WG2", 4), ((None, -1 / 256),)), (wc("WG2", 6), ((None, 128),))])
    mov(A("WC"), A("P5", 0, 464))
    weights(7, 288, [(S("P7", 16), ((13, 256), (14, 1), (7, 1), (15, -2))),
                     (S("P7", 160), ((13, 1), (5, -0.125), (7, -0.125)))])
    mov(A("VLT"), A("P7", 144, 288))
    mov(A("TGT"), A("P7", 0, 144))
    side1 = ((8, -1), (9, -1), (0, -1), (1, 2), (10, 0.5), (3, -1))
    side2 = ((9, 1), (8, -1), (0, -1), (10, 2.5), (6, -2))
    joint = ((7, 1), (14, 1))
    weights(6, 512, [(wc("WQ1", c), ((f, 1),)) for c, f in ((4, 4), (5, 3), (6, 3), (12, 8), (13, 8), (14, 15))] + [
        (wc("WQ2", 0), ((13, 131072),)), (wc("WQ2", 1), size), (wc("WQ2", 2), ((13, 82), (7, 1), (14, 1), (15, -2))),
        (wc("WQ2", 3), low), (wc("WQ2", 4), high), (wc("WQ2", 5), ((13, 1),)),
        (wc("WC1", 3), side1), (wc("WC1", 4), neg(side1)), (wc("WC1", 5), ((8, 1), (10, 1), (3, -1), (12, -1))),
        (wc("WC1", 6), ((9, -1), (10, 1), (2, -1), (3, 1))), (wc("WC1", 7), ((8, -1), (1, 1))), (wc("WC1", 8), ((3, 1),)),
        (wc("WC1", 9), joint + ((9, -256),)), (wc("WC1", 10), ((9, -256),)), (wc("WC1", 11), joint + ((8, 256),)),
        (wc("WC1", 12), ((8, 256),)), (wc("WC1", 14), ((8, 1), (1, -1))),
        (wc("WC2", 3), side2), (wc("WC2", 4), neg(side2)), (wc("WC2", 6), ((10, 2), (0, -1), (6, -1))),
        (wc("WC2", 7), ((9, 1), (8, -1), (10, 1), (6, -1))), (wc("WC2", 11), joint + ((6, 256),)),
        (wc("WC2", 12), ((6, 256),)), (wc("WC2", 13), ((11, 1),)), (wc("WC2", 14), ((8, 1), (13, 1))),
        (wc("WC2", 15), ((9, 1), (8, -1), (10, -255), (6, -1), (3, 256)))])
    mov(A("WB", 0, 256), A("P6", 0, 256))
    mov(A("WB", 256, 512), A("P6", 256, 512))

    mul(A("WZ"), A("BLK"), 61.0)
    gfill(A("XG", U, U + 8))
    gfill(A("AD", 0, 1))
    for t in range(3):
        gfill(A("AS", 72 * t + 64, 72 * t + 72))
        gfill(A("LS", 240 * t + CAP, 240 * t + 240))
    iota(io_(16, 256), [[1, 240]], 16, 0)
    iota(R("NKK"), [[-1, 128]], 0, 0)
    gfill(A("STC", U, U + 368), 600)
    gfill(A("MW", U + CAP, U + CAP + 416), 600)
    twins = [("STC", U + 368 * k, 368, U) for k in (1, 2, 3)] + [("MW", U + CAP + 416 * k, 416, U + CAP) for k in (1, 2)]

    def fill_twins():
        for name, c, n, c0 in twins:
            g.sync.dma_start(T[name][:, c:c + n], T[name][:, c0:c0 + n]).then_inc(T.sem.fill, 16)

    note("y", fill_twins, [A("STC", U, U + 368), A("MW", U + CAP, U + CAP + 416)],
         [A(name, c, c + n) for name, c, n, _ in twins], (0.25, 0, 0, 0, 0), "fill", 16 * len(twins), 3.5)
    k0 = len(calls)
    mul(R("ZR", 768, 896), one_row, -62.25)
    mul(col(11), col(0), 128.0)
    lin(col(12), col(0), 2048.0, 128.0)
    lin(col(13), col(1), -32768.0, 8.0)
    mul(col(27), col(0), 82.0)
    lin(col(16), col(1), col(20))
    lin(A("KW"), io_(0, 16), col(0), 16.0)
    mov(A("IDF"), ident)
    mul(A("INEG"), ident, -262144.0)
    lin(A("UOH"), io_(0, 128), col(16))
    iota(R("NJ", 0, 64), [[0, 2], [-8, 32]], 0, 0)
    gfill(R("NJ", 66, 72))
    gfill(R("NJ", 64, 66), 230400)
    mul(R("NJ", 68, 70), R("ONE", 0, 2), -7.5)
    gfill(R("CQ"))
    gfill(A("ES"))
    gfill(A("B32"))
    gfill(col(26), -4)
    gfill(R("CQ", 5, 118, 16), 1)
    mul(R("CQ", 1, 114, 16), R("ONE", 0, 8), 1.25)
    for gm in range(2):
        sel(B("WRG", gm), A("ONE"), [[-32, 4], [0, 32]], ALU.is_ge, 0.0, -16 * gm, 1)
        sel(B("WRG", gm), B("WRG", gm), [[32, 4], [0, 32]], ALU.is_ge, 0.0, 16 * gm + 15, -1)
        sel(B("WR", gm), A("B32"), [[-32, 4], [0, 32]], ALU.not_equal, 131072.0, -(16 * gm + 13), 1)
    sel(A("TRI"), A("ONE"), [[1, 128]], ALU.is_ge, 0.0, 0, -1)
    sel(A("TRI"), A("TRI"), [[-32, 4], [0, 32]], ALU.is_ge, 0.0, 0, 1)
    sel(A("TRS"), A("TRI"), [[-1, 128]], ALU.not_equal, 0.0, 0, 1)
    mul(A("TRN"), A("TRI"), -1024.0)
    iota(A("EB"), [[40, 2], [1312, 2]], 41, 0)
    lin(A("EB"), A("EB"), col(27))
    gfill(A("SCL"), 256)
    gfill(A("SCL", 2, 19, 16), 1)
    gfill(A("SCL", 3, 20, 16), 1)
    iota(A("K16"), [[16, 16]], 0, 0)
    iota(A("ST", 0, 8), [[0, 4], [40, 2]], 32, 0)
    iota(B("OW", 1), [[0, 8], [1, 16]], 1, 0)
    for o, i, name, fill in ((B("OW", 0), A("ONE"), "CB", 0.0), (B("OW", 1), B("OW", 1), "UW", -100.0)):
        sel(o, i, [[-32, 4], [0, 32]], ALU.is_ge, fill, 0, 1)
        sel(o, o, [[32, 4], [0, 32]], ALU.is_ge, fill, 31, -1)
        for gm in range(2):
            sel(B(name, gm if name == "CB" else 2 * gm), o, [[0, 4], [1, 2], [0, 16]], ALU.is_equal, fill, -gm, 0)
    for gm in range(2):
        lin(B("UW", 2 * gm + 1), B("UW", 2 * gm), 16.0)
    gfill(A("OWN"))
    gfill(sm(24), 40)
    for c, v in ((8, 32), (9, 72), (10, 1), (12, 256)):
        gfill(A("OWN", c, c + 17, 16), v)
    mul(A("OWN", 11, 28, 16), A("ONE", 0, 2), col(1))
    tr(A("OWR"), A("OWN"))
    ts(col(14), col(1), 16.0, ALU.is_lt)
    lin(col(15), col(14), 1.0, -1.0)
    lin(col(25), e16(9), e16(10))
    mul(col(21), e16(5), 600.0)
    mul(col(22), e16(15), -1000.0)
    lin(col(4), col(25), col(21), -1e5)
    lin(col(23), col(25), col(2), -256.0)
    lin(col(28), e16(13), col(22), 32.0)
    lin(col(24), col(23), e16(15))
    lin(col(17), col(28), col(4))
    lin(B("CT", 1, 32), io_(0, 32), col(4), 0.0)
    mul(A("KT"), io_(0, CAP), col(24))
    lin(A("CT", 96, 104), io_(0, 8), col(17), 0.0)
    for h in range(2):
        mul(col(29 + h), col(11 + h), 2.0)
        mul(A("CWB", h, 4, 2), A("ONE", 0, 2), col(29 + h))
    gfill(A("X", W, W + 16))
    chain(k0, "g")

    def dist_a(src, c0, n, pb, d0):
        mm(A(pb, 0, n), ident, A(src, c0, c0 + n), True, False)
        mm(A(pb, 0, n), A("NEGI"), A(src, c0 + 1, c0 + n + 1), False, True)
        act(A("AD", d0, d0 + n), A(pb, 0, n), ACT.Abs)

    def dist_b(src, c0, n, pb, d0, last):
        mm(A(pb, 0, n), A("WDZ"), A(src, c0, c0 + n), True, False)
        mm(A(pb, 0, n), A("WDL"), A("AD", d0, d0 + n), False, False)
        mm(A(pb, 0, n), A("WDR" if last else "WDN"), A("AD", d0 + 1, d0 + n + 1), False, last)

    def lists(t):
        b = 72 * t
        for bit in range(2):
            for qq in range(4):
                mm(A("P4", 4 * bit + qq, 256, 8), A("WZ"), A("AL", b + 32 * bit, b + 32 * bit + 32), True, True)
        steps = []
        for f in (lambda a, b: g.vector.tensor_tensor(T.MI[:, a:b], T.CDI[:, a:b], T.P4[:, a:b], ADD),
                  lambda a, b: g.vector.tensor_scalar(T.MJ[:, a:b], T.MI[:, a:b], 4095, None, ALU.bitwise_and),
                  lambda a, b: g.vector.tensor_copy(T.MU[:, a:b], T.MJ[:, a:b])):
            steps += [lambda f=f: f(0, 128), lambda f=f: f(128, 256)]
        k = note("v", steps, [A("CDI"), A("P4")], [A("MI"), A("MJ"), A("MU")], (0.3, 768, 0, 0, 0))
        calls[k]["n"] = 6
        mul(A("XH"), A("AL", b, b + 64), 0.5)
        return k

    for lo, hi in ((0, 14), (14, 42), (42, 84), (84, 124), (124, 164)):
        mov(A("XG", 16 * lo, 16 * hi), IND(A("X", 0, U), A("OCU", lo, hi)))
    mov(A("AS", 0, 32), A("XG", 0, U - 81, 82))
    mov(A("AS", 32, 64), A("XG", 40, U - 41, 82))
    first = send(A("AS", 0, 72), A("AL", 0, 72), "a0", rank + 1, "loc0", 2.0)
    fills = [("XS", c, min(4272, XSW - c)) for c in range(0, XSW, 4272)]
    fills += [("MG", W, 144), ("SP", 1024, CAP)]

    def fill_gaps():
        g.sync.wait_ge(T.sem.loc0, len(engines(core, T.cores[(rank + 1) % n_ranks])))
        for name, c, n in fills:
            g.sync.dma_start(T[name][:, c:c + n], T.X[:, 0:n] if n <= W else T.STC[:, 0:n]).then_inc(T.sem.ld6, 16)

    fills[:2] = [("XS", 0, W), ("XS", W, W), ("XS", 2 * W, XSW - 2 * W)]
    note("y", fill_gaps, [A("X", 0, W)], [A(name, c, c + n) for name, c, n in fills], (0.3, 0, 0, 0, 0), "ld6",
         16 * len(fills), 9.0, after=[first])
    k0 = lists(0)
    for i, (c, n) in enumerate(((0, 192), (192, 448), (640, 352), (992, 320), (1312, 512), (1824, 512), (2336, 288))):
        dist_a("XG", c, n, "P%d" % (i % 2), c + 1)
        dist_b("XG", c, n, "P%d" % (2 + i % 2), c, True)
        lin(A("DS", c, c + n), A("P%d" % (2 + i % 2), 0, n), col(9) if c >= 1312 else 0.0)
        tt(IND(A("STC", 0, U), A("OCU", c // 16, (c + n) // 16)), A("DS", c, c + n), A("SRC", c % 1312, c % 1312 + n), ADD)
        if i == 5:
            calls[-1]["after"] = [k0]

    def score(t):
        groups = [[33 if t else 32, "s%d%d" % (t, h)] for h in range(2)]
        n = 3 if t else 2
        for h in range(2):
            mm(A("P%d" % h, 0, 384), one_row, R("ZR", 512, 896), True, False)
        if t:
            act(sm(48), A("AL", 72 * t + 64, 72 * t + 66), ACT.Abs)
            for h in range(2):
                mul(B("RH", h), ident, sm1(48, h))
                mm(A("P%d" % h, 256, 384), A("ONE"), B("RH", h), False, False, groups[h])

        def ends(j):
            return [(B("FD", 2 * j + bit, 64)[0], IND(A("X", 0, W), B("MU", 2 * j + bit, 4))[0],
                     B("AL", 72 * t + 32 * bit + j, 1)[0], B("XH", 32 * bit + j, 1)[0]) for bit in range(2)]

        def by_scalar(j):
            return [g.scalar.activation(o, i, ACT.Abs, bias=x, scale=-1.0) for o, i, x, _ in ends(j)]

        def by_vector(j):
            return [g.vector.tensor_scalar(o, i, x, xh, MIN, SUB) for o, i, x, xh in ends(j)]

        who, k = [], len(calls)
        for j in range(32):
            who.append(either(lambda j=j: by_scalar(j), lambda j=j: by_vector(j),
                              [IND(A("X", 0, W), B("MU", j, 8)), A("AL", 72 * t, 72 * t + 64), A("XH")], B("FD", j), 2))
            mm(A("P%d" % (j // 16), j % 16, 256, 16), B("FD", j), A("WF"), False, False, groups[j // 16],
               lambda j=j: B("WF", 1 if who[j]["q"] == "v" else 0, 16))
        chain(k, "s")
        k = len(calls)
        for j0, j1 in ((0, 6), (6, 11), (11, 16), (16, 22), (22, 27), (27, 30), (30, 32)):
            relu(A("MG", 128 * j0, 128 * j1), IND(A("MW" if t else "STC"), A("MU", 8 * j0, 8 * j1)), 0.0 if t else col(3))
            for j in range(j0, j1):
                mm(A("P%d" % (j // 16), j % 16, 128 * n, 16), B("MG", j), A("WM"), False, False, groups[j // 16],
                   lambda j=j: A("WM", 24, 24 + 8 * n) if who[j]["q"] == "v" else A("WM", 0, 8 * n))
        chain(k, "s")
        for h in range(2):
            pb = "P2" if h == 0 else "P7"
            mm(B(pb, 0), one_row, R("NKK"), True, False)
            relu(A("G", 384 * h, 384 * h + 128 * n), A("P%d" % h, 0, 128 * n))
            for k in range(n):
                mm(B(pb, 0), B("G", 3 * h + k), A("I256" if k < 2 else "INEG"), False, k == n - 1)
            red(sm1(0, h), B(pb, 0), MAX)

    def q(i):
        return A("TQ", 32 + i, 32 + i + 17, 16)

    def q1(i, gm):
        return B("TQ", 32 + i + 16 * gm, 1)

    def state(par, gen):
        return 8 * gen + 4 * par

    def choose(t, s_old, s_new):
        par = 1 - t % 2
        win, base, top = (A("XG"), 41.0, U + 7) if t == 0 else (A("XS"), 128.0 * par, XSW - 1)
        eb, lb, ab = 32 * t, 240 * t, 72 * (t + 1)
        mm(A("P3", 0, 64), R("ZR", 0, 128), R("ONE", 0, 64), True, False)
        mm(A("P5", 0, 64), one_row, R("NJ", 0, 64), True, False)
        mm(A("P6", 0, 14), ident, A("KW", 0, 14), True, False)
        ts(sm(1), sm(0), MAGIC, ADD, MAGIC, SUB)
        tt(sm(2), sm(1), sm(0), SUB)
        for h in range(2):
            ts(B("OFF", h, 1), sm1(1, h), sm1(0, h), SUB, col(11 + h), ADD)
            act(B("GD", h, 16), A("E16"), ACT.Relu, None, sm1(1, h))
            lin(B("GD", 2 + h, 16), A("E16"), col(26), sm1(2, h))
        mov(A("MBS"), IND(A("MG"), A("OFF", 0, 2)))
        ga, gb = [6, "a%d" % t], [4, "b%d" % t]
        mm(A("P3", 32, 64), R("CQ"), R("ONE", 0, 32), False, False, ga)
        mm(A("P3", 0, 32), A("WG1"), A("GD", 0, 32), False, False, ga)
        mm(A("P3", 32, 64), A("WG2"), A("GD", 0, 32), False, False, ga)
        mm(A("P3", 0, 32), A("WK"), A("GD", 32, 64), False, False, ga)
        mm(A("P3", 0, 32), A("WQ1"), A("MBS"), False, False, ga)
        mm(A("P3", 32, 64), A("WQ2"), A("MBS"), False, False, ga)
        for gm in range(2):
            mm(B("P5", gm, 32), B("WRG", gm), A("GD", 0, 32), False, False, gb)
            mm(B("P5", gm, 32), B("WR", gm), A("MBS"), False, False, gb)
        tr(A("TQ"), A("P3", 0, 64))
        mm(A("P3", 0, 8), one_row, R("NJ", 64, 72), True, False)
        ts(A("B1"), A("TQ", 0, 32), 0.0, ALU.is_gt)
        mov(A("DF", 32, 73, 40), q(6))
        ts(sm(3), q(1), MAGIC / 256, ADD, MAGIC / 256, SUB)
        for gm in range(2):
            ts(A("DF", 40 * gm, 40 * gm + 32), B("P5", gm, 32), q1(0, gm), SUB, col(13), ADD)
            red(sm1(11, gm), A("DF", 40 * gm, 40 * gm + 33), MIN, True)
            ts(B("WS", gm, 1), sm1(11, gm), 32768.0, ALU.is_ge, sm1(3, gm), MUL)
        tt(A("B2", 0, 23), A("B1", 0, 23), A("B1", 8, 31), ALU.not_equal)
        lin(sm(4), A("B2", 6, 23, 16), -1.0, 2.0)
        lin(sm(5), A("B2", 6, 23, 16), 1.0, -2.0)
        tt(A("CC", 0, 22), A("B2", 0, 22), A("SCL", 0, 22), MUL)
        for b in range(2):
            for gm in range(2):
                lin(B("SPT", 2 * b + gm, 16), B("IOT", b, 16), q1(2, gm), sm1(4, gm))
        tr(A("SPR"), A("SPT"))
        for b in range(2):
            ts(A("SPU", b, 64, 2), B("SPR", b, 32), base, ADD, float(top), MIN)
        for k in range(2):
            mov(B("SP", k, 512), IND(win, B("SPU", k, 32)))
        mm(A("P3", 0, 2), A("TRN"), A("WS"), False, False)
        mm(A("P7", 0, 2), A("TRS"), A("WS"), True, True)
        mm(A("P3", 2, 4), A("TRI"), A("WS"), False, False)
        mm(A("P3", 4, 6), A("TRI"), A("WS"), False, True)
        if t < 2:
            relu(A("ES", eb + 7, eb + 24, 16), q(3))
            relu(A("ES", eb + 14, eb + 31, 16), q(4))
        mov(A("ES", eb + 6, eb + 23, 16), A("P7", 0, 2))
        for gm in range(2):
            pre = A("PRE", 16 * gm, 16 * gm + 6)
            ts(pre, A("CC", 16 * gm, 16 * gm + 6), B("WS", gm, 1), MIN)
            ts(A("ES", eb + 16 * gm, eb + 16 * gm + 6), pre, B("P3", gm, 1), MIN, 0.0, MAX)
        send(B("ES", t, 32), B("EL", t, 32), "e%d" % t, rank - 1 - t)

        def dd(gm):
            return A("ES", eb + 16 * gm + 4, eb + 16 * gm + 6)

        if t < 2:
            mm(A("P5", 0, 4), A("IDF"), A("EB"), True, False)
            for gm in range(2):
                ts(B("OW", gm, 256), B("UW", gm, 256), q1(5, gm), ALU.is_equal, sm1(5, gm), MUL)
                for h in range(2):
                    mm(A("P5", h, 4, 2), B("OW", 2 * gm + h), dd(gm), False, gm == 1 and h == 1)
            cp(A("EU"), A("P5", 0, 4))
            mov(A("EW"), A("P5", 0, 4))
            mov(A("AS", ab, ab + 64), IND(win, A("EU")))
            for h in range(2):
                lin(B("AS", ab + 64 + h, 1), B("EW", h, 1), B("EW", 2 + h, 1), -1.0)
            send(A("AS", ab, ab + 72), A("AL", ab, ab + 72), "a%d" % (t + 1), rank + 2 + t)
        ts(sm(46), A("P3", 4, 6), MAGIC / 16, ADD, MAGIC / 16, SUB)
        lin(sm(14), A("WS"), 32.0, -1.0)
        for gm in range(2):
            c1, c2, c3 = A("CMP", 32 * gm, 32 * gm + 14), A("CMP", 32 * gm + 16, 32 * gm + 30), A("CMP", 64 + 128 * gm, 192 + 128 * gm)
            ts(c1, A("K16", 0, 14), sm1(46, gm), ALU.is_gt, sm1(14, gm), MUL)
            ts(c2, A("K16", 0, 14), sm1(46, gm), ALU.is_equal, sm1(14, gm), MUL)
            ts(c3, B("UW", 2 * gm), sm1(46, gm), ADD, B("P3", 2 + gm, 1), ALU.is_gt)
            mm(A("P6", 0, 14), B("CB", gm), c1, False, False)
            mm(A("P6", 0, 14), c3, c2, False, gm == 1)
        cp(A("CU", 0, 14), A("P6", 0, 14))
        mov(A("LS", lb, lb + CAP), IND(A("SP"), A("CU", 0, 14)))
        if t < 2:
            lin(A("SM", 100, 114), A("P6", 0, 14), -0.484375, 1 / 32)
            ts(A("LS", lb + CAP, lb + CAP + 14), A("SM", 100, 114), MAGIC / 256, ADD, MAGIC / 256, SUB)
        send(A("LS", lb, lb + 240), A("LL", lb, lb + 240), "l%d" % t, rank - 1 - t)
        mm(A("P2", 0, 4), ident, A("ST", s_old, s_old + 4), True, False)
        for gm in range(2):
            ts(B("OH", gm), A("UOH"), q1(5, gm), ALU.is_equal, sm1(5, gm), MUL)
            mm(B("P2", gm, 2), B("OH", gm), dd(gm), False, gm == 1)
        mov(A("ST", s_new, s_new + 4), A("P2", 0, 4))

    def hd(s):
        return A("ST", s, s + 3, 2)

    def st1(s, gm):
        return B("ST", s + 2 * gm, 1)

    def arrive(t, s_old, s_new):
        par = t % 2
        eb, lb, c0 = 32 * t, 240 * t, U + CAP * t

        def ev1(i, gm):
            return B("EL", eb + i + 16 * gm, 1)

        mm(A("P7", 0, 32), A("WC1"), A("OWR"), True, False)
        tr(B("ER", 0, 32), B("EL", t, 32))
        mm(A("P7", 0, 32), A("WC1"), B("ER", 0, 32), False, True)
        mov(B("CT", par, 32), A("P7", 0, 32))
        tt(A("EL", eb + 13, eb + 30, 16), A("EL", eb + 3, eb + 20, 16), sm(24), MUL)
        tr(B("ER", 1, 32), B("EL", t, 32))
        mm(A("P7", 0, 32), A("WC2"), A("OWR"), True, False)
        mm(A("P7", 0, 32), A("WC2"), B("ER", 1, 32), False, True)
        mov(A("CT", 64, 96), A("P7", 0, 32))
        lists(t + 1)
        for lo, hi in ((0, 40), (40, 82), (82, 124), (124, 164)):
            tt(A("MW", 16 * lo, 16 * hi), IND(A("CT", 0, 64), A("VLU", lo, hi)), A("STC", 16 * lo, 16 * hi), ADD)
        mov(A("X", c0, c0 + CAP), A("LL", lb, lb + CAP))
        dist_a("X", c0 - 1, CAP + 1, "P6", 0)
        dist_b("X", c0, CAP, "P3", 0, False)
        mm(A("P3", 0, CAP), ident, A("KT"), False, True)
        mov(A("ND"), A("P3", 0, CAP))
        cp(A("OWU", 0, 14), A("LL", lb + CAP, lb + CAP + 14))
        tt(A("MW", c0, c0 + CAP), IND(A("CT", 64, 104), A("OWU", 0, 14)), A("ND"), ADD)
        for gm in range(2):
            lin(sm1(25, gm), ev1(1, gm), ev1(0, gm), -2.0)
            lin(st1(s_new, gm), ev1(13, gm), st1(s_old, gm))
            lin(sm1(26, gm), ev1(13, gm), sm1(25, gm), -1.0)
            lin(st1(s_new + 1, gm), sm1(26, gm), st1(s_old + 1, gm))
        relu(A("TGB"), A("MW", c0, c0 + CAP))
        wrap("P6", 14, "TGT", "TGB", CAP)
        tu = A("TU", 16 * t, 16 * t + 14)
        ts(tu, A("P6", 0, 14), 128.0 * par, ADD)
        cp(IND(A("XS"), tu), A("LL", lb, lb + CAP))

    def number_tables():
        gfill(A("OCT"))
        for b in range(6):
            cp(A("OCT", 32 * b, 32 * b + len(range(b, 164, 6))), A("OCI", b, 164, 6))
        for b in range(6):
            tr(row3("OC3", b), B("OCT", b, 32))
        for gm in range(2):
            mov(A3("OC4", 0, 16, 6 * gm, 6 * gm + 6), A3("OC3", 16 * gm, 16 * gm + 16, 0, 6))

        def rows():
            for gm in range(2):
                g.sync.dma_start(T.D1[gm:8:2, 16:3088], T.OC4[:, 6 * gm:6 * gm + 6, :]).then_inc(T.sem.d1, 16)
            g.sync.dma_start(T.D1[:, 0:16], T.OC3[0:8, 0, 0:16]).then_inc(T.sem.d1, 16)

        def shifts():
            g.sync.wait_ge(T.sem.d1, 48)
            for s in range(16):
                g.sync.dma_start(T.FS[s:128:16, :], T.D1[:, s:s + FW]).then_inc(T.sem.fs, 16)

        k = note("y", rows, [A3("OC4", 0, 16, 0, 12), A3("OC3", 0, 16, 0, 1)], [], (0.15, 0, 0, 0, 0), "d1", 48, 2.5)
        note("y", shifts, [A("LL", 0, 8)], [A("FS")], (0.8, 0, 0, 0, 0), "fs", 256, 12.0, after=[k])
        for par in range(2):
            iota(A("BASE", 16 * par, 16 * par + 8), [[16, 4], [1312, 2]], 41 * par - 16, 0)
            iota(A("BASE", 16 * par + 8, 16 * par + 16), [[-16, 4], [1312, 2]], 41 * par - 31, 0)
        lin(A("BASE"), A("BASE"), col(27))
        iota(B("ITB", 0), [[16, 4], [0, 32]], 0, 0)
        lin(B("ITB", 0), B("ITB", 0), col(0))
        mul(B("ITB", 1), B("ITB", 0), -1.0)
        mul(A("I16K"), ident, 16384.0)
        gfill(A("JF"), 1)
        sel(A("JF"), A("JF"), [[-16, 8], [1, 16]], ALU.is_equal, 0.0, -15, 1)
        gfill(A("VV"))
        for c in (10, 13):
            gfill(A("VV", c, 64, 16), 1)
        for par in range(2):
            gfill(A("VV", 32 * par + 11, 32 * par + 28, 16), 10 + par)
            gfill(A("VV", 32 * par + 12, 32 * par + 29, 16), 63 - 32 * par)
        big, n1k = A("I16K"), A("N1K")
        parts = {1: [ident], -1: [A("NEGI")], 256: [A("I256")], 16384: [big], -16384: [n1k] * 16, -8192: [n1k] * 8,
                 8192: [big] + [n1k] * 8, 3072: [A("I256")] * 12}
        won = ((2, 1), (6, 1), (7, 16384), (10, -16384), (11, 256), (12, 1))
        table = (((0, 8192), (10, -8192)), ((0, -8192), (10, -8192)), won, ((2, 16384), (10, -8192)),
                 won + ((3, 1),), ((2, 16384), (3, 16384), (10, -8192)), ((3, -1), (13, 3072), (10, -1)),
                 ((3, -16384), (10, -8192)), ((3, -16384),), ((3, 16384),), ((6, 1),), ((0, -16384),))
        todo = [(c, m, f) for c, col_ents in enumerate(table) for f, w in col_ents for m in parts[w]]
        mm(A("P4", 0, 16), one_row, R("ZR", 0, 16), True, False)
        group = [len(todo), "wn"]
        for c, m, f in todo:
            mm(B("P4", c, 1), m, e16(f), False, False, group)
        mov(A("WCL"), A("P4", 0, 16))
        for c in range(12):
            mul(B("WN", c), A("BLK"), B("WCL", c, 1))

    def vv(par, i):
        return A("VV", 32 * par + i, 32 * par + i + 17, 16)

    def lookups(par, s, t, yj, pl):
        k = 30 + 4 * par
        tt(sm(k), hd(s + 1), hd(s), SUB)
        act(vv(par, 0), sm(k), ACT.Sign)
        act(vv(par, 3), sm(k), ACT.Abs)
        tt(sm(k + 1), hd(s), yj, SUB)
        tt(vv(par, 2), sm(k + 1), vv(par, 0), MUL)
        mov(vv(par, 6), A("EL", 32 * t + 6, 32 * t + 23, 16))
        mov(vv(par, 7), A("EL", 32 * t + 2, 32 * t + 19, 16))
        tt(A("LH", 0, 3, 2), hd(s), hd(s + 1), MIN)
        tt(A("LH", 1, 4, 2), hd(s), hd(s + 1), MAX)
        mm(A(pl, 0, 16), A("IDF"), B("BASE", par, 16), True, False)
        group = [16, "l%d" % par]
        for h in range(2):
            mul(B("LH", 1 + h, 4), A("LH", 0, 4), col(14 + h))
            for gm in range(2):
                o = 16 - 16 * gm + 16 * h
                for b in range(4):
                    mm(A(pl, 2 * b + h, 16, 8), A("IDW", o, o + 128), B("LH", 2 + 2 * h + gm, 2), False, False, group)
        ts(B("NU", par, 16), A(pl, 0, 16), 0.0, MAX, float(FW - 1), MIN)
        mov(B("GN", par, 256), IND(A("FS"), B("NU", par, 16)))
        tr(B("VR", par, 32), B("VV", par, 32))

    def spread_over(bank, k, c, x, group):
        for b in range(4):
            mm(B(bank, 4 * k + b, 32), B("WN", c), x, False, False, group)

    def own(par, turned, bank, out):
        group = [20, "o%d%d" % (par, turned)]
        mm(A(bank), one_row, R("ZR", 0, 512), True, False)
        mm(B(bank, 0), A("IDF"), B("GN", 2 * par), False, False, group)
        mm(B(bank, 1), A("JF"), B("GN", 2 * par + 1), False, False, group)
        mm(B(bank, 2), ident, B("ITB", turned), False, False, group)
        mm(B(bank, 3), A("I16K"), B("ITB", turned), False, False, group)
        for k, c in enumerate((turned, 1 - turned, 2 + 2 * turned, 3 + 2 * turned)):
            spread_over(bank, k, c, B("VR", par, 32), group)
        mov(out, B(bank, 2))
        for k, o in ((3, MIN), (0, MAX), (1, MAX)):
            tt(out, B(bank, k), out, o)

    def results(par, number, empty):
        n1, n2 = B("NA", 4 + 2 * par), B("NA", 5 + 2 * par)
        tt(n1, empty, number, MAX)
        for b in range(4):
            ts(A("FU", 4 * par + b, 256, 8), B("NA", 4 * (4 + 2 * par) + b, 32), float(W), MIN)
        ts(n2, empty, -1.0, MUL, -1.0, MAX)
        tt(n2, n2, number, MIN)
        for b in range(4):
            tr(row3("YT", 4 * par + b), B("NA", 4 * (5 + 2 * par) + b, 32))

    def spread(par):
        k = len(calls)
        for i in range(41):
            sel(A("XS", 128 * par + 32 + i, 8192, 256), A("XG", 41 * par + i, U, 82), [[0, 32]], ALU.is_ge, 0.0, 0, 0)
        chain(k, "g")

    score(0)
    wrap("P4", 164, "VLT", "STC", U)
    ts(A("VLU"), A("P4", 0, 164), 32.0, ADD)
    choose(0, state(1, 0), state(1, 1))
    v = S("WQ2", 2)
    sel(v, v, [[-16, 8]], ALU.not_equal, 256.0, -13, 1)
    spread(0)
    arrive(0, state(0, 0), state(0, 1))
    number_tables()
    lin(sm(40), A("EL", 13, 30, 16), 72.0, -1.0)
    s = state(0, 1)
    mm(A("P5", 0, 4), ident, A("CWB"), True, False)
    for h in range(2):
        mul(B("SMK", h, 4), A("ST", s, s + 4), col(14 + h))
        for gm in range(2):
            o = 16 - 16 * gm + 16 * h
            mm(A("P5", h, 4, 2), A("IDW", o, o + 128), B("SMK", 2 * h + gm, 2), False, gm == 1 and h == 1)
    mov(A("EB"), A("P5", 0, 4))
    s = state(1, 1)
    mov(A("OWN", 8, 25, 16), hd(s))
    mov(A("OWN", 9, 26, 16), hd(s + 1))
    gfill(A("OWN", 12, 29, 16))
    for gm in range(2):
        lin(sm1(24, gm), st1(s, gm), st1(s + 1, gm), -1.0)
    tr(A("OWR"), A("OWN"))
    score(1)
    lin(B("CT", 0, 32), io_(0, 32), col(4), 0.0)
    gfill(A("MW", U, U + CAP), 600)
    choose(1, state(0, 1), state(0, 2))
    spread(1)
    arrive(1, state(1, 1), state(1, 2))
    tt(sm(41), hd(state(1, 1) + 1), A("EL", 45, 62, 16), SUB)
    lookups(0, state(0, 2), 0, sm(40), "P4")
    own(0, 0, "P4", B("NA", 0))
    own(0, 1, "P5", B("NA", 1))
    mm(B("P5", 0), A("I16K"), B("ITB", 0), True, False)
    spread_over("P5", 0, 7, B("VR", 0, 32), [4, "p"])
    mov(B("NA", 2), B("P5", 0))
    lin(B("NA", 1), B("NA", 1), -16384.0)
    final = [28, "q"]
    mm(A("P4"), one_row, R("ZR", 0, 512), True, False)
    for k in range(2):
        mm(B("P4", k), A("IDF"), B("NA", k), False, False, final)
    mm(B("P4", 2), ident, B("ITB", 0), False, False, final)
    mm(B("P4", 3), A("I16K"), B("ITB", 0), False, False, final)
    spread_over("P4", 2, 6, B("VR", 0, 32), final)
    spread_over("P4", 3, 7, B("VR", 0, 32), final)
    score(2)
    choose(2, state(1, 2), state(1, 0))
    lookups(1, state(1, 0), 1, sm(41), "P2")
    own(1, 0, "P5", B("NA", 3))
    mm(B("P2", 0), A("I16K"), B("ITB", 0), True, False)
    spread_over("P2", 0, 7, B("VR", 1, 32), [4, "r"])
    results(1, B("NA", 3), B("P2", 0))
    tr(B("ER", 0, 32), B("EL", 2, 32))
    for k, c in ((2, 10), (0, 8), (1, 9), (3, 11)):
        spread_over("P4", k, c, B("ER", 0, 32), final)
    tt(B("NA", 2), B("P4", 2), B("NA", 2), MIN)
    tt(B("NA", 2), B("P4", 0), B("NA", 2), MAX)
    tt(B("NA", 2), B("P4", 1), B("NA", 2), MAX)
    results(0, B("NA", 2), B("P4", 3))
    mov(A("X", U + 2 * CAP, U + 3 * CAP), A("LL", 480, 480 + CAP))
    nout = [0]

    def store(dst, src, time):
        nout[0] += 16
        note("y", lambda: g.sync.dma_start(dst, src[0]).then_inc(T.sem.out0, 16), [src], [], (time, 0, 0, 0, 0), "out0",
             10 ** 6, 1.7)

    for gm in range(2):
        mov(A3("YU", 0, 16, 8 * gm, 8 * gm + 8), A3("YT", 16 * gm, 16 * gm + 16, 0, 8))
        store(T.yo[gm:8:2, :], A3("YU", 0, 16, 8 * gm, 8 * gm + 8), 0.3)
    k0 = len(calls)
    for a, b in ((0, 640), (640, 1536), (1536, 2432), (2432, 3328), (3328, W)):
        h = (a + b) // 2
        mov(A("FD", a, h), IND(A("X"), A("FU", a // 16, h // 16)))
        mov(A("FD", h, b), IND(A("X"), A("FU", h // 16, b // 16)))
        store(T.y[:, a:b], A("FD", a, b), 0.25 + (b - a) * 0.0006)
    chain(k0, "s")

    if not ORDER:
        ORDER.extend(schedule(calls, lanes))
    cnt = {"v": 0, "s": 0, "t": 0, "g": 0}
    seen = {k: {} for k in eng}
    acc = {}

    def wait(q, sem, val):
        if seen[q].get(sem, 0) < val:
            eng[q].wait_ge(T.sem[sem], val)
            seen[q][sem] = val

    for t in range(3):
        for name, n, sem, src in (("AL", 72, "a", rank - 1 - t), ("EL", 32, "e", rank + 1 + t), ("LL", 240, "l", rank + 1 + t)):
            acc.setdefault(name, []).append([bits(range(n * t, n * t + n), True), True, sem + str(t),
                                             len(engines(T.cores[src % n_ranks], core)), "r"])
    for i, qn in ORDER:
        calls[i]["q"] = qn
    for i, _ in ORDER:
        c = calls[i]
        qn, items, need = c["q"], touched(c), {}
        if c["dma"]:
            sem, val = c["sem"], c["val"]
        else:
            cnt[qn] += c["n"]
            sem, val = "q" + qn, cnt[qn]
        for name, m, w, psum in items:
            for e in acc.get(name, []):
                if e[0] & m and (w or e[1] or (psum and e[4] != qn)) and not (qn == "t" and e[4] == "t"):
                    need[e[2]] = max(need.get(e[2], 0), e[3])
        for s in need:
            wait(qn, s, need[s])
        for name, m, w, psum in items:
            lst = acc.setdefault(name, [])
            lst[:] = [e for e in lst if not ((w or (e[4] == qn and not e[1] and not c["dma"])) and e[0] & ~m == 0)]
            lst.append([m, w, sem, val, qn])
        if isinstance(c["fn"], list):
            for k, step in enumerate(c["fn"]):
                if k >= 2:
                    wait(qn, sem, val - c["n"] + k - 1)
                step().then_inc(T.sem[sem], 1)
            continue
        done = c["fn"]()
        if not c["dma"]:
            for ins in (done if c["n"] > 1 else [done]):
                ins.then_inc(T.sem["q" + qn], 1)
    g.sync.wait_ge(T.sem.out0, nout[0])
    g.wait_ge(T.sem.loc, sent[0])
    for k in ("v", "s", "t", "g"):
        wait("g", "q" + k, cnt[k])
